import numpy as np, ml_dtypes
CORES = [1,5,17,21,33,37,49,53]
N = 8
import mx_ref
BF = ml_dtypes.bfloat16
def gcols(t, e):
    v = np.concatenate([t.reshape(8, 16, -1, 4), np.zeros((8, 16, 1, 4), BF)], axis=2)
    return np.ascontiguousarray(np.stack([v[g][:, e[g]] for g in range(8)])).reshape(128, -1)
def tile(rs):
    return np.stack(rs, axis=2).reshape(128, -1).astype(BF)
def pick(q, e):
    c = np.concatenate([q[0].reshape(128, -1, 4), np.zeros((128, 1, 4), np.uint8)], axis=1); s = np.concatenate([q[1], np.ones((16, 1), np.uint8)], axis=1)
    return (np.ascontiguousarray(c[:, e].reshape(128, -1)), np.ascontiguousarray(s[:, e]))
def join(*qs):
    return (np.concatenate([q[0] for q in qs], axis=1), np.concatenate([q[1] for q in qs], axis=1))
def put(q, e, v):
    c, s = q[0].reshape(128, -1, 4).copy(), q[1].copy(); c[:, e] = v[0].reshape(128, -1, 4); s[:, e] = v[1]
    return (c.reshape(128, -1), s)
def pk(c, s):
    return (np.ascontiguousarray(c), mx_ref.live(s))
def emit(q):
    return q[0], q[1]
def packed(v, rng):
    q = [mx_ref.quantize(np.ascontiguousarray(v[r])) for r in range(N)]
    return np.stack([a for a, b in q]), np.stack([mx_ref.plane(b, rng) for a, b in q])
def values_of_codes():
    e, c = np.zeros((128, 128, 4), np.float32), np.zeros((128, 2, 4), np.uint8)
    e[np.arange(128), np.arange(128), 0] = 1
    c[:127, :, 0] = np.arange(256).reshape(2, 128).T[:127]
    return mx_ref.matmul(mx_ref.quantize(e.reshape(128, 512).astype(BF)), (c.reshape(128, 8), np.full((16, 2), 127, np.uint8))).T.reshape(-1).astype(np.float64)
CODE_VALUE, SCALE_VALUE = values_of_codes(), 2.0 ** (np.arange(256) - 127.0)
def decode(q):
    return (CODE_VALUE[q[0]].reshape(16, 8, -1, 4) * SCALE_VALUE[q[1]][:, None, :, None] + 0.0).reshape(128, -1).astype(np.float32)
def f(rng, *shape):
    return mx_ref.flush((rng.standard_normal(shape, dtype=np.float32) * np.exp2(rng.integers(-2, 3, shape[:-1] + (1,)))).astype(BF))
def wide(rng, *shape, cols=0):
    v = rng.standard_normal(shape, dtype=np.float32) * np.exp2(rng.integers(-12, 13, shape)).astype(np.float32)
    if cols: v *= np.repeat(np.exp2(rng.integers(-cols, cols + 1, shape[:-2] + (1, shape[-1] // 4))) * (rng.random(shape[:-2] + (1, shape[-1] // 4)) > 0.0625), 4, axis=-1).astype(np.float32)
    return mx_ref.flush(v.astype(BF))
C, M, R = 256, 32, 3
def numbers_of(rng):
    return {"x": np.array(f(rng, N, 128, 4 * C)), "u": np.array(f(rng, N, 128, 512)), "v": np.array(f(rng, N, 128, 512))}
def weights(rng, still=0):
    w = np.array(f(rng, N, 128, 2048)).reshape(N, 8, 16, 4, 8, 16, 4)
    w[:, :, :still] = 0
    w[:, :, :, :, :, :still] = 0
    c, p = packed(np.ascontiguousarray(w).reshape(N, 128, 2048), rng)
    return {"wc": c, "ws": p}
def plant(rng, d, word, sym, size, full=False):
    x, u = d["x"].reshape(N, 8, 16, C, 4), d["u"].reshape(N, 8, 16, 128, 4)
    low = rng.integers(-1, 1, (N, 8, 3))
    size = np.reshape(size, (N, 1, 1, 1))
    x[:, :, :8] = 0
    for k in range(3): u[:, :, :, k::16] = 0
    for g in range(8):
        h = (g + 1) % 8
        s = np.take_along_axis(sym[:, g], word & ~(1 << h), axis=1)
        for k, yes in enumerate((word >> g, s >> 1, s)):
            i, j, m = ((0, 6, 4), (6, 7, 4), (7, 8, 4))[k] if full else (k, k + 1, 1)
            a = np.where(yes & 1, 1, low[:, g, k, None])[:, None, :, None] * size
            x[:, h, i:j, :, :m] = a.astype(np.float32).astype(BF)
            u[:, h, i:j, 16 * g + k, :m] = size[:, :, :, 0].astype(np.float32).astype(BF)
def setup_inputs(rng):
    return {**numbers_of(rng), **weights(rng)}
def setup_inputs_caps(rng):
    d = numbers_of(rng)
    w = np.concatenate([np.repeat(np.arange(8), [M, M + 1, M, M - 1, 2 * M, 1, 0, 0]), np.full(C - 6 * M - 1, 8)])
    word = np.stack([(255 - (1 << np.append(rng.permutation(8), 8)) % 256)[rng.permutation(w)] for r in range(N)])
    sym = rng.integers(0, 4, (N, 8, 256))
    for g in range(8):
        h = (g + 1) % 8
        sym[:, g, 255 - (1 << h)] = rng.integers(4)
        sym[:, g, 255 - (1 << h) - (1 << g)] = sym[0, g, 255 - (1 << h)]
    plant(rng, d, word, sym, np.ones(N))
    return {**d, **weights(rng, 8)}
def setup_inputs_near(rng):
    d = numbers_of(rng)
    o = rng.permutation(N) % 2
    word = rng.integers(0, 256, (N, C))
    word[:, 0] = 255
    j = rng.integers(1, C, N)
    word[np.arange(N), j] = 255
    sym = rng.integers(0, 4, (N, 8, 256))
    sym[rng.integers(N)] = rng.integers(0, 4, (8, 1))
    plant(rng, d, word, sym, np.where(o == 0, 2.0 ** -30, 1.0))
    x = d["x"].reshape(N, 8, 16, C, 4)
    for r in range(N):
        for h in rng.permutation(8)[:4]: x[r, h, :3, j[r]] = (x[r, h, :3, j[r]].astype(np.float32) * np.float32(2.0 ** 50 if o[r] == 0 else 2.0 ** 20)).astype(BF)
    return {**d, **weights(rng, 8)}
def setup_inputs_huge(rng):
    d = numbers_of(rng)
    sym = rng.integers(0, 4, (N, 8, 256))
    g, none = int(rng.integers(8)), int(rng.integers(N))
    word = np.zeros((N, C), np.int64)
    for r in range(N):
        word[r] = rng.integers(256)
        if r == none: continue
        o = (g + 2 + rng.permutation(6)) % 8
        k = rng.integers(0, 16, C)
        k[:8] = 2 * np.arange(8) + 1
        k[8:8 + 4 * M] = 2 * (np.arange(4 * M) // M) + 8 * rng.integers(0, 2, 4 * M)
        k = rng.permutation(k)
        for i, e in enumerate((g, int(o[0]), int(o[1]), int(rng.choice(np.append(o[2:], (g + 1) % 8))))):
            word[r] = word[r] & ~(1 << e) | ((k >> i) & 1) << e
        n = np.arange(256)
        sym[r, g] = (2 * ((n >> int(o[1])) & 1) + ((n >> int(o[0])) & 1)) ^ int(rng.integers(4))
    d["x"] = (d["x"].astype(np.float32) * np.float32(2.0 ** 20)).astype(BF)
    plant(rng, d, word, sym, np.full(N, 2.0 ** 30), True)
    return {**d, **weights(rng, 8)}
def setup_inputs_late(rng):
    d = numbers_of(rng)
    x, u = d["x"].reshape(N, 8, 16, C, 4), d["u"].reshape(N, 128, 128, 4)
    k = (N, 8, 8, C, 4)
    a = np.exp2(-rng.integers(8, 15, k).astype(np.float64)) * (1.0 + (2 * rng.integers(0, 64, k) + 1) * 2.0 ** -7) * rng.choice([-1.0, 1.0], k)
    a[:, :, 0, :, 0] = 1.96875 * rng.choice([-1.0, 1.0], (N, 8, C))
    a[:, :, 1:4, :, 0] = 2.0 ** -13
    a[:, :, 4:7, :, 0] = 7 * 2.0 ** -16
    x[:, :, 8:] = a.astype(np.float32).astype(BF)
    x[:, :, :3, :, 0] = -0.0625
    for r in range(N):
        g = rng.permutation(C) % 16
        j = np.flatnonzero(g < 8)
        x[r, g[j], :3, j, 0] = 0
    s = (rng.permutation(N) % 2 * 2.0 - 1.0).astype(np.float32).astype(BF)
    for i in range(3):
        u[:, :, i::16] = 0
        for h in range(i, 128, 16):
            u[:, h, h, 0] = s
            u[:, h + 9, h, 0] = -s
            u[:, h + 12, h, 0] = s
    return {**d, **weights(rng)}
def setup_inputs_spread(rng):
    d = setup_inputs(rng)
    d["x"] = wide(rng, N, 128, 4 * C, cols=6)
    return d
def check_inputs(d):
    b = []
    for k in ("x", "u", "v"):
        a = np.abs(d[k].astype(np.float32))
        if not (np.isfinite(a).all() and ((a == 0) | (a >= 2.0 ** -30) & (a <= 2.0 ** 30)).all()): b.append("a value of " + k)
    none, least, most = [emit(mx_ref.quantize(np.full((128, 16), k, np.float32).astype(BF)))[1][0, 0] for k in (0.0, 2.0 ** -30, 2.0 ** 30)]
    for r in range(N):
        if ((d["wc"][r] == 0x7F) | (d["wc"][r] == 0xFF)).any(): b.append("wc: a code that is no number")
        s = mx_ref.live(d["ws"][r])
        if ((s != none) & ((s < least) | (s > most))).any(): b.append("ws: a scale out of range")
    return b
def mine(s):
    bit = s[::16] > 0
    word = np.packbits(bit, axis=0, bitorder="little")[0].astype(np.int64)
    sym = 2 * (s[1::16] > 0) + (s[2::16] > 0)
    first = np.full(256, -1)
    k, i = np.unique(word, return_index=True)
    first[k] = i
    a, b, take = np.full((8, 4 * M), -1), np.full((8, 4 * M), -1), np.zeros((8, C), np.int64)
    for g in range(8):
        mate = first[word ^ (1 << g)]
        for c in range(4):
            j = np.flatnonzero(~bit[g] & (mate >= 0) & (sym[g] == c))[:M]
            a[g, M * c:M * c + len(j)] = j
            b[g, M * c:M * c + len(j)] = mate[j]
            i = np.flatnonzero(sym[g] == c)
            take[g, i] = M * c + np.arange(len(i)) % M
    return a, b, take
def reference(x, u, v, wc, ws):
    qu = [mx_ref.quantize(u[r]) for r in range(N)]
    lay = [pk(wc[r], ws[r]) for r in range(N)]
    now = [x[r] for r in range(N)]
    for t in range(R):
        own, sent, takes = [], [], []
        for r in range(N):
            q = mx_ref.quantize(now[r])
            own.append(decode(q).astype(BF))
            a, b, take = mine(mx_ref.matmul(qu[r], q))
            e = (gcols(own[r], b).astype(np.float32) - gcols(own[r], a).astype(np.float32)).astype(BF)
            sent.append(mx_ref.quantize(e))
            takes.append(take)
        for r in range(N):
            came = decode(sent[(r - 1 - t) % N]).astype(BF)
            z = (own[r].astype(np.float32) + gcols(came, takes[r]).astype(np.float32)).astype(BF)
            q = mx_ref.quantize(z)
            now[r] = tile([np.maximum(mx_ref.matmul(pick(lay[r], np.arange(128 * b, 128 * b + 128)), q), np.float32(0.0)) * np.float32(0.015625) + z[:, b::4].astype(np.float32) for b in range(4)])
    y = np.zeros((N, 128, C), np.float32)
    oc, osc = np.zeros((N, 128, 4 * C), np.uint8), np.zeros((N, 16, C), np.uint8)
    for r in range(N):
        q = mx_ref.quantize(now[r])
        y[r] = mx_ref.matmul(mx_ref.quantize(v[r]), q)
        oc[r], osc[r] = emit(q)
    return {"y": y, "oc": oc, "osc": osc}

@@ -1,0 +1,458 @@
+from concourse.mybir import dt, AluOpType, AxisListType, ActivationFunctionType
+
+N, C, M, R = 8, 256, 32, 3
+X4, U8, BF, F32, I32, U16 = "float8_e4m3fn_x4", "uint8", "bfloat16", "float32", "int32", "uint16"
+FP = C + 16
+OWN = 2048.0
+HOLD = 4096.0
+SWW = 2416
+
+SCRATCH = {
+    "xt": ("sbuf", [128, 1024], BF), "ut": ("sbuf", [128, 512], BF), "vt": ("sbuf", [128, 512], BF),
+    "xn": ("sbuf", [128, 1024], BF), "zt": ("sbuf", [128, 1024], BF), "et": ("sbuf", [128, 512], BF),
+    "qx": ("sbuf", [128, 256], X4), "sx": ("sbuf", [128, 256], U8),
+    "qz": ("sbuf", [128, 256], X4), "sz": ("sbuf", [128, 256], U8),
+    "qu": ("sbuf", [128, 128], X4), "su": ("sbuf", [128, 128], U8),
+    "qup": ("sbuf", [128, 128], X4), "sup": ("sbuf", [128, 128], U8),
+    "qv": ("sbuf", [128, 128], X4), "sv": ("sbuf", [128, 128], U8),
+    "qw": ("sbuf", [128, 512], X4), "sw": ("sbuf", [128, 512], U8),
+    "ones": ("sbuf", [128, 512], BF), "tt": ("sbuf", [128, 1536], BF),
+    "qt": ("sbuf", [128, 384], X4), "st": ("sbuf", [128, 384], U8),
+    "la": ("sbuf", [128, 516], BF), "lb": ("sbuf", [128, 516], BF),
+    "qd": ("sbuf", [128, 512], X4), "sd": ("sbuf", [128, 512], U8),
+    "pint": ("sbuf", [128, 16], I32), "rint": ("sbuf", [128, 25], I32), "rf": ("sbuf", [128, 25], F32),
+    "col": ("sbuf", [128, 16], F32), "sm8": ("sbuf", [128, 16], F32), "lf": ("sbuf", [128, 32], F32),
+    "mi": ("sbuf", [128, 32], I32), "mf": ("sbuf", [128, 16], F32),
+    "off": ("sbuf", [128, 64], U16), "iot": ("sbuf", [128, 256], BF),
+    "cwa": ("sbuf", [128, 32], BF), "cw16": ("sbuf", [128, 16], BF), "cw": ("sbuf", [128, 256], BF),
+    "mask": ("sbuf", [128, 256], BF), "hd": ("sbuf", [128, 32], BF), "keep": ("sbuf", [128, 64], BF),
+    "gri": ("sbuf", [128, 128], BF),
+    "cc": ("sbuf", [128, 64], F32), "kk": ("sbuf", [128, 64], F32), "kt": ("sbuf", [128, 16], F32),
+    "bits": ("sbuf", [128, 64], BF), "hv": ("sbuf", [128, 80], BF),
+    "ot": ("sbuf", [128, 1088], BF), "qo": ("sbuf", [128, 272], X4), "so": ("sbuf", [128, 272], U8),
+    "yt": ("sbuf", [128, 512], BF), "qy": ("sbuf", [128, 128], X4), "sy": ("sbuf", [128, 128], U8),
+    "nt": ("sbuf", [128, 1024], BF), "qn": ("sbuf", [128, 256], X4), "sn": ("sbuf", [128, 256], U8),
+    "ct": ("sbuf", [128, 520], BF), "qc": ("sbuf", [128, 128], X4), "sc": ("sbuf", [128, 128], U8),
+    "tv": ("sbuf", [128, 384], BF), "ft": ("sbuf", [128, 384], BF),
+    "tvr": ("sbuf", [128, 256], BF), "mate": ("sbuf", [128, FP], BF), "gw": ("sbuf", [128, 256], BF),
+    "sym": ("sbuf", [128, 128], BF), "thr": ("sbuf", [128, 64], BF), "inv": ("sbuf", [128, 16], F32),
+    "x1": ("sbuf", [128, 112], F32), "x2": ("sbuf", [128, 112], F32), "xi": ("sbuf", [128, 32], I32),
+    "t16": ("sbuf", [128, 16], U16), "p16": ("sbuf", [128, 16], U16), "k16": ("sbuf", [128, 16], U16),
+    "a16": ("sbuf", [128, 8], U16), "b16": ("sbuf", [128, 8], U16),
+    "swin": ("sbuf", [128, SWW], BF), "wa": ("sbuf", [128, 128], BF), "wb": ("sbuf", [128, 128], BF),
+    "brow": ("sbuf", [128, 128], BF),
+    "fp": ("sbuf", [128, 4 * FP], BF), "ap": ("sbuf", [128, 512], BF), "gp": ("sbuf", [128, 512], BF),
+    "zg": ("sbuf", [128, 384], BF), "rl": ("sbuf", [128, 1024], F32), "yo": ("sbuf", [128, 256], F32),
+    "ps": ("psum", [128, 4096], F32),
+}
+for _t in range(R):
+    SCRATCH["qe%d" % _t] = ("sbuf", [128, 128], X4)
+    SCRATCH["se%d" % _t] = ("sbuf", [128, 128], U8)
+    SCRATCH["ql%d" % _t] = ("sbuf", [128, 128], X4)
+    SCRATCH["sl%d" % _t] = ("sbuf", [128, 128], U8)
+
+SEMAPHORES = ["cV", "cA", "cP", "cG", "sent"] + ["arr%d" % _t for _t in range(R)] + ["d%d" % _i for _i in range(24)]
+
+
+def rank_program(g, core, T, topo):
+    rank = T.rank_of(core)
+    if rank is None:
+        return
+    A, AF, AX = AluOpType, ActivationFunctionType, AxisListType.X
+    eng = {"V": g.vector, "A": g.scalar, "P": g.tensor, "G": g, "S": g.sync}
+    clock = {q: {} for q in eng}
+    count = {}
+    seen = {}
+    wrote, reads = {}, {}
+    ndma = [0]
+
+    def order(q, r, w, ext):
+        need = {}
+        for k in r:
+            for e in ([wrote[k]] if k in wrote else []) + ([x for x in reads.get(k, []) if x[2] != q] if k[0] == "B" else []):
+                need[e[0]] = max(need.get(e[0], 0), e[1])
+        for k in w:
+            for e in ([wrote[k]] if k in wrote else []) + reads.get(k, []):
+                need[e[0]] = max(need.get(e[0], 0), e[1])
+        for s, n in ext:
+            need[s] = n
+        todo = sorted(need.items())
+        for s, n in todo:
+            if any(seen.get(o, {}).get(s, 0) >= n for o in todo if o[0] != s):
+                continue
+            if clock[q].get(s, 0) < n:
+                eng[q].wait_ge(T.sem[s], n)
+                clock[q][s] = n
+                for s2, n2 in seen.get((s, n), {}).items():
+                    clock[q][s2] = max(clock[q].get(s2, 0), n2)
+
+    def done(q, s, n, r, w):
+        count[s] = n
+        seen[(s, n)] = dict(clock[q])
+        for k in r:
+            reads.setdefault(k, []).append((s, n, q))
+        for k in w:
+            wrote[k] = (s, n, q)
+            reads[k] = []
+
+    def op(q, fn, r=(), w=(), ext=()):
+        order(q, r, w, ext)
+        s = "c" + q
+        fn().then_inc(T.sem[s], 1)
+        done(q, s, count.get(s, 0) + 1, r, w)
+
+    def dma(q, out, in_, r=(), w=()):
+        order(q, r, w, ())
+        s = "d%d" % ndma[0]
+        ndma[0] += 1
+        eng[q].dma_start(out, in_).then_inc(T.sem[s], 16)
+        done(q, s, 16, r, w)
+
+    V, S_ = g.vector, g.scalar
+
+    def ts(out, in0, s1, o0, r, w, s2=None, o1=None):
+        if o1 is None:
+            op("V", lambda: V.tensor_scalar(out, in0, s1, None, o0), r, w)
+        else:
+            op("V", lambda: V.tensor_scalar(out, in0, s1, s2, o0, o1), r, w)
+
+    def tt(out, a, b, o, r, w):
+        op("V", lambda: V.tensor_tensor(out, a, b, o), r, w)
+
+    def cp(out, in_, r, w):
+        op("V", lambda: V.tensor_copy(out, in_), r, w)
+
+    def ms(out, c, w):
+        op("V", lambda: V.memset(out, c), (), w)
+
+    def scan(out, d0, d1, o0, o1, r, w):
+        op("V", lambda: V.tensor_tensor_scan(out, d0, d1, 0.0, o0, o1), r, w)
+
+    def qz(q, s, t, r, w):
+        op("V", lambda: V.quantize_mx(q, s, t), r, w)
+
+    def act(out, in_, r, w, f=None, scale=None, bias=None):
+        if f is None:
+            op("A", lambda: S_.activation(out, in_, AF.Copy), r, w)
+        elif bias is None:
+            op("A", lambda: S_.activation(out, in_, f, scale=scale), r, w)
+        else:
+            op("A", lambda: S_.activation(out, in_, f, bias=bias, scale=scale), r, w)
+
+    def iota(out, pat, base, cm, w, small=True):
+        if small:
+            op("G", lambda: g.iota(out, pat, base, cm, allow_small_or_imprecise_dtypes=True), (), w)
+        else:
+            op("G", lambda: g.iota(out, pat, base, cm), (), w)
+
+    def sel(out, in_, pat, cmp, fill, cm, r, w, base=0):
+        op("G", lambda: g.affine_select(out, in_, pat, cmp, fill, base, cm), r, w)
+
+    def bank(b, lo, hi):
+        return T.ps[:, 512 * b + lo:512 * b + hi]
+
+    def mmc(b, lname, la, rname, ra, rb, r, ext=()):
+        lq, ls = T["q" + lname][:, la:la + 128], T["s" + lname][:, la:la + 128]
+        rq, rs = T["q" + rname][:, ra:rb], T["s" + rname][:, ra:rb]
+        op("P", lambda: g.tensor.matmul_mx(bank(b, 0, rb - ra), lq, ls, rq, rs, True, True), r, ["B%d" % b], ext)
+
+    col = lambda i: T.col[:, i:i + 1]
+    rf = lambda i: T.rf[:, i:i + 1]
+
+    dma("A", T.ut[:], T.u[:], (), ["ut"])
+    dma("S", T.xt[:, 0:512], T.x[:, 0:512], (), ["X0"])
+    dma("S", T.xt[:, 512:1024], T.x[:, 512:1024], (), ["X1"])
+
+    zsrc = ["otz", "otw"]
+    iota(T.pint[:], [[0, 16]], 0, 1, ["pint"], False)
+    iota(T.iot[:], [[1, 256]], 0, 0, ["iot"])
+    ms(T.ot[:, 1:1088:2], 0.0, zsrc)
+    ms(T.ones[:], 1.0, ["ones"])
+    act(T.la[:], T.ot[:, 1:1033:2], zsrc, ["la"])
+    act(T.lb[:], T.ot[:, 1:1033:2], zsrc, ["lb"])
+    ts(T.rint[:, 0:16], T.pint[:], 15, A.bitwise_and, ["pint"], ["ri0"])
+    ts(T.rint[:, 16:17], T.pint[:, 0:1], 4, A.arith_shift_right, ["pint"], ["ri1"])
+    ts(T.rint[:, 17:18], T.pint[:, 0:1], 1, A.bitwise_and, ["pint"], ["ri2"])
+    ts(T.rint[:, 18:19], T.pint[:, 0:1], 7, A.bitwise_and, ["pint"], ["ri3"])
+    ts(T.rint[:, 19:20], T.pint[:, 0:1], 8, A.bitwise_and, ["pint"], ["ri4"])
+    ts(T.rint[:, 24:25], T.pint[:, 0:1], 1, A.arith_shift_right, ["pint"], ["ri6"], 7, A.bitwise_and)
+    cp(T.rint[:, 20:24], T.pint[:, 0:4], ["pint"], ["ri5"])
+    ms(T.lf[:, 2:8], 0.0, ["lf2"])
+    cp(T.rf[:], T.rint[:], ["ri0", "ri1", "ri2", "ri3", "ri4", "ri5", "ri6"], ["rf"])
+    ms(T.hd[:], 2.0, ["hd"])
+    ts(T.lf[:, 0:1], rf(18), -16.0, A.mult, ["rf"], ["lf0"], 112.0, A.add)
+    ts(col(0), rf(17), -7.0, A.mult, ["rf"], ["c0"], 1.0, A.add)
+    ts(col(1), rf(0), 1.0, A.add, ["rf"], ["c1"])
+    ts(T.lf[:, 1:2], rf(0), 8.0, A.mult, ["rf", "c0"], ["lf1"], col(0), A.add)
+    cp(T.off[:, 26:42], T.rf[:, 0:16], ["rf"], ["o_r"])
+    ts(T.cwa[:, 0:16], T.iot[:, 0:16], col(1), A.is_equal, ["iot", "c1"], ["cwa"], HOLD, A.mult)
+    ts(T.cwa[:, 16:32], T.iot[:, 0:16], rf(0), A.not_equal, ["iot", "rf"], ["cwb"])
+    cp(T.off[:, 0:8], T.lf[:, 0:8], ["lf0", "lf1", "lf2"], ["o_u"])
+    tt(T.cw16[:], T.cwa[:, 0:16], T.cwa[:, 16:32], A.max, ["cwa", "cwb"], ["cw16"])
+    iota(T.gri[:], [[1, 8], [0, 16]], 0, 0, ["gri"])
+    sel(T.tt[:, 512:1024:2], T.ones[:, 0:256], [[1, 128], [-1000, 2]], A.is_ge, 0.0, -1, ["ones"], ["t2a"])
+    act(T.cw[:], T.cw16[:].indirect(T.off[:, 26:42]), ["cw16", "o_r"], ["cw"])
+    act(T.tt[:, 0:512:2], T.ones[:, 0:256], ["ones"], ["t1a"])
+    ts(T.tt[:, 515:1024:4], T.gri[:], rf(16), A.is_equal, ["gri", "rf"], ["t2c"], 4.0, A.mult)
+    sel(T.tt[:, 513:1024:4], T.tt[:, 515:1024:4], [[1, 128]], A.is_gt, 0.0, -1, ["t2c"], ["t2b"])
+    sel(T.tt[:, 513:1024:4], T.tt[:, 513:1024:4], [[1, 128]], A.not_equal, OWN, -1, ["t2b"], ["t2b"])
+    sel(T.tt[:, 1024:1536], T.ones[:], [[1, 128], [-1000, 4]], A.is_ge, 0.0, -1, ["ones"], ["t3"], 2000)
+    iota(T.cc[:], [[1, 4], [0, 16]], 0, 0, ["cc"])
+    iota(T.kk[:, 16:64], [[1, 3], [0, 16]], 1, 0, ["kk1"])
+    iota(T.kt[:], [[16, 16]], int(OWN) + 1024, 1, ["kt"])
+    iota(T.nt[:, 1:1024:2], [[0, 512]], 0, 0, ["ntz"])
+    ts(T.sm8[:, 0:8], T.iot[:, 0:8], rf(16), A.is_lt, ["iot", "rf"], ["s8a"], 1.0, A.add)
+    ts(T.sm8[:, 8:16], T.iot[:, 0:8], rf(16), A.is_ge, ["iot", "rf"], ["s8b"], 0.5, A.max)
+    ts(T.mf[:], T.iot[:, 0:16], 16.0, A.mult, ["iot", "rf"], ["mf"], rf(0), A.add)
+    op("V", lambda: V.tensor_reduce(col(3), T.sm8[:, 8:16], AX, A.mult), ["s8b"], ["c3"])
+    op("V", lambda: V.tensor_reduce(col(2), T.sm8[:, 0:8], AX, A.mult), ["s8a"], ["c2"])
+    ts(T.mi[:, 0:16], T.mf[:], col(3), A.mult, ["mf", "c3"], ["mi0"], -0.496, A.add)
+    ts(T.la[:, 2:514:4], T.iot[:, 0:128], rf(20), A.is_equal, ["iot", "rf"], ["la"])
+    ts(T.mi[:, 16:32], T.mi[:, 0:16], 1, A.bitwise_and, ["mi0"], ["mi1"])
+    ts(T.lb[:, 3:515:4], T.iot[:, 0:128], rf(20), A.is_equal, ["iot", "rf"], ["lb"])
+    cp(T.off[:, 42:58], T.mi[:, 16:32], ["mi1"], ["o_m"])
+    act(T.mask[:], T.iot[:, 0:16].indirect(T.off[:, 42:58]), ["iot", "o_m"], ["mask"])
+    ms(T.hd[:, 0:13:12], 0.0, ["hd"])
+    ts(col(8), rf(17), 12.0, A.mult, ["rf"], ["c8"], 19.0, A.add)
+    ts(col(9), rf(24), rf(16), A.is_equal, ["rf"], ["c9"])
+    ts(col(4), rf(19), 4.0, A.mult, ["rf"], ["c4"], 33.0, A.add)
+    ts(col(10), rf(18), rf(16), A.is_equal, ["rf"], ["c10"])
+    ms(T.hd[:, 16:32:2], 0.0, ["hd"])
+    ts(T.lf[:, 8:9], col(8), col(9), A.mult, ["c8", "c9"], ["lf8"])
+    ts(T.lf[:, 9:10], col(8), 32.0, A.add, ["c8", "c9"], ["lf9"], col(9), A.mult)
+    ts(T.mf[:, 0:8], T.iot[:, 0:8], 2.0, A.mult, ["iot", "c4"], ["mf"], col(4), A.add)
+    cp(T.lf[:, 18:22], T.rf[:, 20:24], ["rf"], ["lf18"])
+    ts(T.lf[:, 22:26], T.rf[:, 0:4], 16.0, A.mult, ["rf"], ["lf22"], 15.0, A.add)
+    ts(T.lf[:, 10:18], T.mf[:, 0:8], col(10), A.mult, ["mf", "c10"], ["lf10"])
+    ts(T.tt[:, 1:512:4], T.cw[:, 0:128], 0.0, A.is_equal, ["cw"], ["t1b"], 16.0, A.mult)
+    ts(T.tt[:, 3:512:4], T.cw[:, 0:128], 0.0, A.is_equal, ["cw"], ["t1c"])
+    cp(T.off[:, 8:26], T.lf[:, 8:26], ["lf8", "lf9", "lf10", "lf18", "lf22"], ["o_l"])
+    qz(T.qt[:, 0:128], T.st[:, 0:128], T.tt[:, 0:512], ["t1a", "t1b", "t1c"], ["qt1"])
+    ms(T.hv[:, 0:16], 0.0, ["hvz"])
+    qz(T.qu[:], T.su[:], T.ut[:], ["ut"], ["qu"])
+    ms(T.ot[:, 0:64:2], 0.0, ["otw0"])
+    op("V", lambda: V.tensor_copy(T.qup[:].bitcast(dt.uint32), T.qu[:].bitcast(dt.uint32).indirect(T.off[:, 0:8])),
+       ["qu", "o_u"], ["qup"])
+    act(T.sup[:], T.su[:].indirect(T.off[:, 0:8]), ["qu", "o_u"], ["sup"])
+    act(T.yt[:], T.ot[:, 65:1088:2], ["otz"], ["ytz", "yt"])
+
+    def unpackers(bs):
+        for b in bs:
+            src = T.la if b % 2 == 0 else T.lb
+            o = 2 - 2 * (b // 2)
+            qz(T.qd[:, 128 * b:128 * b + 128], T.sd[:, 128 * b:128 * b + 128], src[:, o:o + 512],
+               ["la" if b % 2 == 0 else "lb"], ["qd%d" % b])
+
+    def quant_x(src, h):
+        qz(T.qx[:, 128 * h:128 * h + 128], T.sx[:, 128 * h:128 * h + 128], src[:, 512 * h:512 * h + 512],
+           ["X%d" % h], ["qx%d" % h])
+
+    def scores(h):
+        mmc(h, "x", 128 * h, "up", 0, 128, ["qx%d" % h, "qup", "sup"])
+
+    def signs(h):
+        ts(T.bits[:, 32 * h:32 * h + 32], bank(h, 0, 32), 0.0, A.is_gt, ["B%d" % h], ["bits%d" % h])
+
+    def horner(h):
+        scan(T.hv[:, 32 * h + 16:32 * h + 48], T.hd[:], T.bits[:, 32 * h:32 * h + 32], A.mult, A.add,
+             ["hd", "bits%d" % h], ["hv%d" % h])
+
+    def onehot(h):
+        ts(T.ot[:, 64 + 2 * h:1088:4], T.iot[:], T.hv[:, 32 * h + 23:32 * h + 24], A.is_equal,
+           ["iot", "hv%d" % h], ["ot%d" % h])
+
+    def unpack_own(ks):
+        for k in ks:
+            mmc(2 + k, "d", 128 * k, "x", 0, 256, ["qd%d" % k, "qx0", "qx1"])
+
+    def copy_own(ks):
+        for k in ks:
+            act(T.fp[:, FP * k:FP * k + 256], bank(2 + k, 0, 256), ["B%d" % (2 + k)], ["fp%d" % k])
+
+    quant_x(T.xt, 0)
+    scores(0)
+    quant_x(T.xt, 1)
+    dma("S", T.qw[:].bitcast(dt.uint8), T.wc[:], ["X1"], ["qw"])
+    dma("S", T.sw[:], T.ws[:], (), ["sw"])
+    dma("S", T.vt[:], T.v[:], (), ["vt"])
+    unpackers([0])
+    signs(0)
+    unpackers([1])
+    horner(0)
+
+    hv = ["hv0", "hv1", "hvz"]
+    for t in range(R):
+        scores(1)
+        if t > 0:
+            unpack_own(range(4))
+        onehot(0)
+        signs(1)
+        if t == 0:
+            ms(T.tv[:, 256:384], 0.0, ["tvz"])
+        horner(1)
+        if t == 0:
+            ms(T.fp[:, 256:4 * FP:FP], 0.0, ["fpz"])
+        act(T.yt[:, 3:512:4], T.hv[:].indirect(T.off[:, 10:18]), hv + ["o_l"], ["yt"])
+        onehot(1)
+        cp(T.ot[:, 1:64:2], T.hv[:].indirect(T.off[:, 8:10]), hv + ["o_l"], ["otw"])
+        if t == 0:
+            unpackers([2])
+        qz(T.qo[:], T.so[:], T.ot[:], ["ot0", "ot1", "otw", "otw0", "otz"], ["qo"])
+        qz(T.qy[:], T.sy[:], T.yt[:], ["yt", "ytz"], ["qy"])
+        if t == 0:
+            unpackers([3])
+        mmc(0, "t", 0, "o", 0, 272, ["qt1", "qo"])
+        mmc(1, "t", 0, "y", 0, 128, ["qt1", "qy"])
+        if t == 0:
+            unpack_own(range(4))
+        copy_own([0, 1, 2] if t > 0 else [0])
+        ts(T.t16[:], bank(0, 0, 16), col(2), A.add, ["B0", "c2"], ["t16"])
+        tt(T.tv[:, 0:256], bank(0, 16, 272), T.mask[:], A.min, ["B0", "mask"], ["tv"])
+        if t == 0:
+            qz(T.qt[:, 128:384], T.st[:, 128:384], T.tt[:, 512:1536], ["t2a", "t2b", "t2c", "t3"], ["qt2"])
+        mmc(6, "t", 128, "o", 16, 272, ["qt2", "qo"])
+        mmc(7, "t", 256, "o", 16, 272, ["qt2", "qo"])
+        act(T.tvr[:], T.tv[:].indirect(T.t16[:]), ["tv", "tvz", "t16"], ["tvr"])
+        act(T.nt[:, 0:1024:4], bank(6, 0, 256), ["B6"], ["nt0"], AF.Relu, -1.0, 1.0)
+        act(T.nt[:, 2:1024:4], bank(7, 0, 256), ["B7"], ["nt1"], AF.Relu, -1.0, 1.0)
+        copy_own([3] if t > 0 else [1, 2, 3])
+        if t == 0:
+            ms(T.ct[:, 0:512:2], 0.0, ["ctz0"])
+            ms(T.ct[:, 3:4], 0.0, ["ctz1"])
+            ms(T.keep[:], 1.0, ["keep"])
+            ts(col(5), rf(0), 15.0, A.is_lt, ["rf"], ["c5"], 2.0 * HOLD - 2.0, A.mult)
+            ms(T.keep[:, 15:64:16], 0.0, ["keep"])
+        cp(T.sym[:], bank(1, 0, 128), ["B1"], ["sym"])
+        if t == 0:
+            ts(col(6), col(5), 2.0, A.add, ["c5"], ["c6"])
+        tt(T.ct[:, 257:513:4], T.sym[:].indirect(T.off[:, 18:22]), T.cc[:], A.is_equal, ["sym", "o_l", "cc"], ["ct2"])
+        if t == 0:
+            ts(col(7), rf(0), 15.0, A.is_equal, ["rf"], ["c7"], 1.0 / HOLD, A.max)
+        ts(T.thr[:], T.ct[:, 257:513:4], 0.5, A.subtract, ["ct2", "c6"], ["thr"], col(6), A.mult)
+        scan(T.gw[:], T.cw[:], T.tvr[:], A.mult, A.max, ["cw", "tvr"], ["gw"])
+        scan(T.ct[:, 263:519:4], T.ct[:, 257:513:4], T.keep[:], A.add, A.mult, ["ct2", "keep"], ["ct3"])
+        tt(T.ct[:, 1:257:4], T.gw[:].indirect(T.off[:, 22:26]), T.thr[:], A.is_equal, ["gw", "o_l", "thr"], ["ct0"])
+        ts(T.inv[:], T.gw[:, 15:256:16], 2.0, A.mult, ["gw", "c6"], ["inv"], col(6), A.is_lt)
+        scan(T.ct[:, 7:263:4], T.ct[:, 1:257:4], T.keep[:], A.add, A.mult, ["ct0", "keep"], ["ct1"])
+        tt(T.kk[:, 0:16], T.inv[:], T.kt[:], A.mult, ["inv", "kt"], ["kk0"])
+        qz(T.qc[:], T.sc[:], T.ct[:, 0:512], ["ct0", "ct1", "ct2", "ct3", "ctz0", "ctz1"], ["qc"])
+        mmc(1, "t", 128, "c", 0, 128, ["qt2", "qc"])
+        qz(T.qn[:], T.sn[:], T.nt[:], ["nt0", "nt1", "ntz"], ["qn"])
+        mmc(0, "t", 0, "n", 0, 256, ["qt1", "qn"])
+        tt(T.x1[:, 0:64], bank(1, 0, 64), T.kk[:], A.add, ["B1", "kk0", "kk1"], ["x1a"])
+        if t == 0:
+            ms(T.ft[:, 256:384], 256.0, ["ftz"])
+        tt(T.x1[:, 64:96], T.x1[:, 0:32], T.x1[:, 32:64], A.max, ["x1a"], ["x1b"])
+        if t == 0:
+            ms(T.mate[:, 256:FP], 256.0, ["matez"])
+        tt(T.x1[:, 96:112], T.x1[:, 64:80], T.x1[:, 80:96], A.max, ["x1b"], ["x1c"])
+        if t == 0:
+            ms(T.swin[:, 0:128], 256.0, ["swin"])
+        ts(T.p16[:], T.x1[:, 96:112], OWN, A.subtract, ["x1c"], ["p16"])
+        act(T.ft[:, 0:256], bank(0, 0, 256), ["B0"], ["ft"])
+        act(T.mate[:, 0:256], T.ft[:].indirect(T.t16[:]), ["ft", "ftz", "t16"], ["mate"])
+        cp(T.swin[:].indirect(T.p16[:]), T.iot[:], ["iot", "p16"], ["swin"])
+        scan(T.wa[:], T.cw[:, 0:128], T.swin[:, 0:128], A.mult, A.max, ["cw", "swin"], ["wa"])
+        ts(T.a16[:], T.wa[:, 15:128:16], col(7), A.mult, ["wa", "c7"], ["a16"])
+        for k in range(4):
+            act(T.ap[:, 128 * k:128 * k + 128], T.fp[:, FP * k:FP * k + C + 1].indirect(T.a16[:]),
+                ["fp%d" % k, "fpz", "a16"], ["ap%d" % k])
+        cp(T.brow[:], T.mate[:, 0:C + 1].indirect(T.a16[:]), ["mate", "matez", "a16"], ["brow"])
+        scan(T.wb[:], T.cw[:, 0:128], T.brow[:], A.mult, A.max, ["cw", "brow"], ["wb"])
+        ts(T.b16[:], T.wb[:, 15:128:16], col(7), A.mult, ["wb", "c7"], ["b16"])
+        for k in range(4):
+            tt(T.et[:, k:512:4], T.fp[:, FP * k:FP * k + C + 1].indirect(T.b16[:]), T.ap[:, 128 * k:128 * k + 128],
+               A.subtract, ["fp%d" % k, "fpz", "b16", "ap%d" % k], ["et%d" % k])
+        qz(T["qe%d" % t][:], T["se%d" % t][:], T.et[:], ["et0", "et1", "et2", "et3"], ["qe%d" % t])
+        dst = T.cores[(rank + 1 + t) % N]
+        src = T.cores[(rank - 1 - t) % N]
+        rid, pid = topo.addr(dst)[0], topo.addr(dst)[1]
+        order("G", ["qe%d" % t], (), ())
+        g.remote_dma(T["ql%d" % t][:].bitcast(dt.uint8), T["qe%d" % t][:].bitcast(dt.uint8),
+                     T.sem["arr%d" % t], T.sem.sent, pid, rid, topo.mask(core, dst))
+        g.remote_dma(T["sl%d" % t][:], T["se%d" % t][:], T.sem["arr%d" % t], T.sem.sent, pid, rid, topo.mask(core, dst))
+        count["sent"] = count.get("sent", 0) + 2 * len(topo.engines(core, dst))
+        arrived = [("arr%d" % t, 2 * len(topo.engines(src, core)))]
+        tt(T.x2[:, 0:64], bank(1, 64, 128), T.cc[:], A.add, ["B1", "cc"], ["x2a"])
+        if t < R - 1:
+            ms(T.swin[:, 0:128], 256.0, ["swin"])
+        tt(T.x2[:, 64:96], T.x2[:, 0:32], T.x2[:, 32:64], A.max, ["x2a"], ["x2b"])
+        tt(T.x2[:, 96:112], T.x2[:, 64:80], T.x2[:, 80:96], A.max, ["x2b"], ["x2c"])
+        cp(T.xi[:, 0:16], T.x2[:, 96:112], ["x2c"], ["xi0"])
+        ts(T.xi[:, 16:32], T.xi[:, 0:16], 4 * M - 1, A.bitwise_and, ["xi0"], ["xi1"])
+        cp(T.k16[:], T.xi[:, 16:32], ["xi1"], ["k16"])
+        if t == 0:
+            qz(T.qv[:], T.sv[:], T.vt[:], ["vt"], ["qv"])
+        gb = [0, 1, 6, 7]
+        for k in range(4):
+            mmc(gb[k], "d", 128 * k, "l%d" % t, 0, 128, ["qd%d" % k], arrived if k == 0 else ())
+        cp(T.gp[:, 0:128], bank(gb[0], 0, 128), ["B%d" % gb[0]], ["gp0"])
+        for k in range(1, 4):
+            act(T.gp[:, 128 * k:128 * k + 128], bank(gb[k], 0, 128), ["B%d" % gb[k]], ["gp%d" % k])
+        rb = [[2, 0, 1, 6], [7, 3, 4, 5]]
+        for k in (2, 3, 1):
+            act(T.zg[:, 128 * k - 128:128 * k], T.gp[:, 128 * k:128 * k + 128].indirect(T.k16[:, 8:16]),
+                ["gp%d" % k, "k16"], ["zg%d" % k])
+        for h in range(2):
+            for k in (0, 1, 2, 3) if h == 0 else (0, 2, 3, 1):
+                zo = T.zt[:, 512 * h + k:512 * h + 512:4]
+                if h == 0 or k == 0:
+                    tt(zo, T.gp[:, 128 * k:128 * k + 128].indirect(T.k16[:, 8 * h:8 * h + 8]),
+                       T.fp[:, FP * k + 128 * h:FP * k + 128 * h + 128], A.add,
+                       ["gp%d" % k, "k16", "fp%d" % k], ["z%d%d" % (h, k)])
+                else:
+                    tt(zo, bank(2 + k, 128, 256), T.zg[:, 128 * k - 128:128 * k], A.add,
+                       ["B%d" % (2 + k), "zg%d" % k], ["z%d%d" % (h, k)])
+            qz(T.qz[:, 128 * h:128 * h + 128], T.sz[:, 128 * h:128 * h + 128], T.zt[:, 512 * h:512 * h + 512],
+               ["z%d%d" % (h, k) for k in range(4)], ["qz%d" % h])
+            for k in range(4):
+                mmc(rb[h][k], "w", 128 * k, "z", 128 * h, 128 * h + 128, ["qw", "sw", "qz%d" % h])
+                o = 512 * h + 128 * k
+                act(T.rl[:, o:o + 128], bank(rb[h][k], 0, 128), ["B%d" % rb[h][k]], ["rl%d%d" % (h, k)], AF.Relu, 0.015625)
+        last = t == R - 1
+
+        def add(h, k):
+            o = 512 * h + 128 * k
+            tt(T.xn[:, 512 * h + k:512 * h + 512:4], T.rl[:, o:o + 128], T.zt[:, 512 * h + k:512 * h + 512:4], A.add,
+               ["rl%d%d" % (h, k), "z%d%d" % (h, k)], ["xn%d%d" % (h, k)])
+
+        def newx(h):
+            qz(T.qx[:, 128 * h:128 * h + 128], T.sx[:, 128 * h:128 * h + 128], T.xn[:, 512 * h:512 * h + 512],
+               ["xn%d%d" % (h, k) for k in range(4)], ["qx%d" % h])
+
+        def store(h, qa, qb):
+            lo, hi = 128 * h, 128 * h + 128
+            dma(qa, T.oc[:, 4 * lo:4 * hi], T.qx[:, lo:hi].bitcast(dt.uint8), ["qx%d" % h])
+            for k in range(4):
+                dma(qb if k < 2 else qa, T.osc[4 * k:4 * k + 4, lo:hi], T.sx[32 * k:32 * k + 4, lo:hi], ["qx%d" % h])
+
+        for k in range(4):
+            add(0, k)
+        if last:
+            add(1, 0)
+            newx(0)
+            mmc(2, "v", 0, "x", 0, 128, ["qv", "qx0"])
+            store(0, "S", "S")
+            act(T.yo[:, 0:128], bank(2, 0, 128), ["B2"], ["yo0"])
+            dma("A", T.y[:, 0:128], T.yo[:, 0:128], ["yo0"])
+            for k in range(1, 4):
+                add(1, k)
+            newx(1)
+            mmc(0, "v", 0, "x", 128, 256, ["qv", "qx1"])
+            store(1, "A", "S")
+            cp(T.yo[:, 128:256], bank(0, 0, 128), ["B0"], ["yo1"])
+            dma("S", T.y[:, 128:256], T.yo[:, 128:256], ["yo1"])
+        else:
+            add(1, 0)
+            newx(0)
+            scores(0)
+            add(1, 1)
+            add(1, 2)
+            signs(0)
+            add(1, 3)
+            horner(0)
+            newx(1)
+
+    for s, n in sorted(count.items()):
+        if not any(clock[q].get(s, 0) >= n for q in clock):
+            g.wait_ge(T.sem[s], n)

@@ -7,49 +7,20 @@ OWN = 2048.0
 HOLD = 4096.0
 SWW = 2416
 
-SCRATCH = {
-    "xt": ("sbuf", [128, 1024], BF), "ut": ("sbuf", [128, 512], BF), "vt": ("sbuf", [128, 512], BF),
-    "xn": ("sbuf", [128, 1024], BF), "zt": ("sbuf", [128, 1024], BF), "et": ("sbuf", [128, 512], BF),
-    "qx": ("sbuf", [128, 256], X4), "sx": ("sbuf", [128, 256], U8),
-    "qz": ("sbuf", [128, 256], X4), "sz": ("sbuf", [128, 256], U8),
-    "qu": ("sbuf", [128, 128], X4), "su": ("sbuf", [128, 128], U8),
-    "qup": ("sbuf", [128, 128], X4), "sup": ("sbuf", [128, 128], U8),
-    "qv": ("sbuf", [128, 128], X4), "sv": ("sbuf", [128, 128], U8),
-    "qw": ("sbuf", [128, 512], X4), "sw": ("sbuf", [128, 512], U8),
-    "ones": ("sbuf", [128, 512], BF), "tt": ("sbuf", [128, 1536], BF),
-    "qt": ("sbuf", [128, 384], X4), "st": ("sbuf", [128, 384], U8),
-    "la": ("sbuf", [128, 516], BF), "lb": ("sbuf", [128, 516], BF),
-    "qd": ("sbuf", [128, 512], X4), "sd": ("sbuf", [128, 512], U8),
-    "pint": ("sbuf", [128, 16], I32), "rint": ("sbuf", [128, 25], I32), "rf": ("sbuf", [128, 25], F32),
-    "col": ("sbuf", [128, 16], F32), "sm8": ("sbuf", [128, 16], F32), "lf": ("sbuf", [128, 32], F32),
-    "mi": ("sbuf", [128, 32], I32), "mf": ("sbuf", [128, 16], F32),
-    "off": ("sbuf", [128, 64], U16), "iot": ("sbuf", [128, 256], BF),
-    "cwa": ("sbuf", [128, 32], BF), "cw16": ("sbuf", [128, 16], BF), "cw": ("sbuf", [128, 256], BF),
-    "mask": ("sbuf", [128, 256], BF), "hd": ("sbuf", [128, 32], BF), "keep": ("sbuf", [128, 64], BF),
-    "gri": ("sbuf", [128, 128], BF),
-    "cc": ("sbuf", [128, 64], F32), "kk": ("sbuf", [128, 64], F32), "kt": ("sbuf", [128, 16], F32),
-    "bits": ("sbuf", [128, 64], BF), "hv": ("sbuf", [128, 80], BF),
-    "ot": ("sbuf", [128, 1088], BF), "qo": ("sbuf", [128, 272], X4), "so": ("sbuf", [128, 272], U8),
-    "yt": ("sbuf", [128, 512], BF), "qy": ("sbuf", [128, 128], X4), "sy": ("sbuf", [128, 128], U8),
-    "nt": ("sbuf", [128, 1024], BF), "qn": ("sbuf", [128, 256], X4), "sn": ("sbuf", [128, 256], U8),
-    "ct": ("sbuf", [128, 520], BF), "qc": ("sbuf", [128, 128], X4), "sc": ("sbuf", [128, 128], U8),
-    "tv": ("sbuf", [128, 384], BF), "ft": ("sbuf", [128, 384], BF),
-    "tvr": ("sbuf", [128, 256], BF), "mate": ("sbuf", [128, FP], BF), "gw": ("sbuf", [128, 256], BF),
-    "sym": ("sbuf", [128, 128], BF), "thr": ("sbuf", [128, 64], BF), "inv": ("sbuf", [128, 16], F32),
-    "x1": ("sbuf", [128, 112], F32), "x2": ("sbuf", [128, 112], F32), "xi": ("sbuf", [128, 32], I32),
-    "t16": ("sbuf", [128, 16], U16), "p16": ("sbuf", [128, 16], U16), "k16": ("sbuf", [128, 16], U16),
-    "a16": ("sbuf", [128, 8], U16), "b16": ("sbuf", [128, 8], U16),
-    "swin": ("sbuf", [128, SWW], BF), "wa": ("sbuf", [128, 128], BF), "wb": ("sbuf", [128, 128], BF),
-    "brow": ("sbuf", [128, 128], BF),
-    "fp": ("sbuf", [128, 4 * FP], BF), "ap": ("sbuf", [128, 512], BF), "gp": ("sbuf", [128, 512], BF),
-    "zg": ("sbuf", [128, 384], BF), "rl": ("sbuf", [128, 1024], F32), "yo": ("sbuf", [128, 256], F32),
-    "ps": ("psum", [128, 4096], F32),
-}
-for _t in range(R):
-    SCRATCH["qe%d" % _t] = ("sbuf", [128, 128], X4)
-    SCRATCH["se%d" % _t] = ("sbuf", [128, 128], U8)
-    SCRATCH["ql%d" % _t] = ("sbuf", [128, 128], X4)
-    SCRATCH["sl%d" % _t] = ("sbuf", [128, 128], U8)
+SCRATCH = {"ps": ("psum", [128, 4096], F32)}
+for _d, _l in (
+    (BF, "xt:1024 ut:512 vt:512 xn:1024 zt:1024 et:512 ones:512 zz:516 tt:1536 la:516 lb:516 iot:256 cwa:32 cw16:16 "
+         "cw:256 mask:256 hd:32 keep:64 gri:128 bits:64 hv:80 ot:1088 yt:512 nt:1024 ct:520 tv:384 ft:384 tvr:256 "
+         "mate:%d gw:256 sym:128 thr:64 swin:%d wa:128 wb:128 brow:128 fp:%d ap:512 gp:512 zg:512" % (FP, SWW, 4 * FP)),
+    (F32, "rf:25 col:16 sm8:16 lf:32 mf:24 cc:64 kk:64 kt:16 inv:16 x1:112 x2:112 rl:1024 yo:256"),
+    (I32, "pint:16 rint:25 mi:32 xi:32"),
+    (U16, "off:64 t16:16 p16:16 k16:16 a16:8 b16:8"),
+):
+    for _e in _l.split():
+        SCRATCH[_e.split(":")[0]] = ("sbuf", [128, int(_e.split(":")[1])], _d)
+for _e in "x:256 z:256 u:128 up:128 v:128 w:512 t:384 d:512 o:272 y:128 n:256 c:128 e0:128 e1:128 e2:128 l0:128 l1:128 l2:128".split():
+    SCRATCH["q" + _e.split(":")[0]] = ("sbuf", [128, int(_e.split(":")[1])], X4)
+    SCRATCH["s" + _e.split(":")[0]] = ("sbuf", [128, int(_e.split(":")[1])], U8)
 
 SEMAPHORES = ["cV", "cA", "cP", "cG", "sent"] + ["arr%d" % _t for _t in range(R)] + ["d%d" % _i for _i in range(24)]
 
@@ -139,6 +110,9 @@ def rank_program(g, core, T, topo):
         else:
             op("A", lambda: S_.activation(out, in_, f, bias=bias, scale=scale), r, w)
 
+    def lin(out, in_, scale, bias, r, w):
+        act(out, in_, r, w, AF.Identity, scale, bias)
+
     def iota(out, pat, base, cm, w, small=True):
         if small:
             op("G", lambda: g.iota(out, pat, base, cm, allow_small_or_imprecise_dtypes=True), (), w)
@@ -156,85 +130,11 @@ def rank_program(g, core, T, topo):
         rq, rs = T["q" + rname][:, ra:rb], T["s" + rname][:, ra:rb]
         op("P", lambda: g.tensor.matmul_mx(bank(b, 0, rb - ra), lq, ls, rq, rs, True, True), r, ["B%d" % b], ext)
 
-    col = lambda i: T.col[:, i:i + 1]
-    rf = lambda i: T.rf[:, i:i + 1]
-
-    dma("A", T.ut[:], T.u[:], (), ["ut"])
-    dma("S", T.xt[:, 0:512], T.x[:, 0:512], (), ["X0"])
-    dma("S", T.xt[:, 512:1024], T.x[:, 512:1024], (), ["X1"])
-
-    zsrc = ["otz", "otw"]
-    iota(T.pint[:], [[0, 16]], 0, 1, ["pint"], False)
-    iota(T.iot[:], [[1, 256]], 0, 0, ["iot"])
-    ms(T.ot[:, 1:1088:2], 0.0, zsrc)
-    ms(T.ones[:], 1.0, ["ones"])
-    act(T.la[:], T.ot[:, 1:1033:2], zsrc, ["la"])
-    act(T.lb[:], T.ot[:, 1:1033:2], zsrc, ["lb"])
-    ts(T.rint[:, 0:16], T.pint[:], 15, A.bitwise_and, ["pint"], ["ri0"])
-    ts(T.rint[:, 16:17], T.pint[:, 0:1], 4, A.arith_shift_right, ["pint"], ["ri1"])
-    ts(T.rint[:, 17:18], T.pint[:, 0:1], 1, A.bitwise_and, ["pint"], ["ri2"])
-    ts(T.rint[:, 18:19], T.pint[:, 0:1], 7, A.bitwise_and, ["pint"], ["ri3"])
-    ts(T.rint[:, 19:20], T.pint[:, 0:1], 8, A.bitwise_and, ["pint"], ["ri4"])
-    ts(T.rint[:, 24:25], T.pint[:, 0:1], 1, A.arith_shift_right, ["pint"], ["ri6"], 7, A.bitwise_and)
-    cp(T.rint[:, 20:24], T.pint[:, 0:4], ["pint"], ["ri5"])
-    ms(T.lf[:, 2:8], 0.0, ["lf2"])
-    cp(T.rf[:], T.rint[:], ["ri0", "ri1", "ri2", "ri3", "ri4", "ri5", "ri6"], ["rf"])
-    ms(T.hd[:], 2.0, ["hd"])
-    ts(T.lf[:, 0:1], rf(18), -16.0, A.mult, ["rf"], ["lf0"], 112.0, A.add)
-    ts(col(0), rf(17), -7.0, A.mult, ["rf"], ["c0"], 1.0, A.add)
-    ts(col(1), rf(0), 1.0, A.add, ["rf"], ["c1"])
-    ts(T.lf[:, 1:2], rf(0), 8.0, A.mult, ["rf", "c0"], ["lf1"], col(0), A.add)
-    cp(T.off[:, 26:42], T.rf[:, 0:16], ["rf"], ["o_r"])
-    ts(T.cwa[:, 0:16], T.iot[:, 0:16], col(1), A.is_equal, ["iot", "c1"], ["cwa"], HOLD, A.mult)
-    ts(T.cwa[:, 16:32], T.iot[:, 0:16], rf(0), A.not_equal, ["iot", "rf"], ["cwb"])
-    cp(T.off[:, 0:8], T.lf[:, 0:8], ["lf0", "lf1", "lf2"], ["o_u"])
-    tt(T.cw16[:], T.cwa[:, 0:16], T.cwa[:, 16:32], A.max, ["cwa", "cwb"], ["cw16"])
-    iota(T.gri[:], [[1, 8], [0, 16]], 0, 0, ["gri"])
-    sel(T.tt[:, 512:1024:2], T.ones[:, 0:256], [[1, 128], [-1000, 2]], A.is_ge, 0.0, -1, ["ones"], ["t2a"])
-    act(T.cw[:], T.cw16[:].indirect(T.off[:, 26:42]), ["cw16", "o_r"], ["cw"])
-    act(T.tt[:, 0:512:2], T.ones[:, 0:256], ["ones"], ["t1a"])
-    ts(T.tt[:, 515:1024:4], T.gri[:], rf(16), A.is_equal, ["gri", "rf"], ["t2c"], 4.0, A.mult)
-    sel(T.tt[:, 513:1024:4], T.tt[:, 515:1024:4], [[1, 128]], A.is_gt, 0.0, -1, ["t2c"], ["t2b"])
-    sel(T.tt[:, 513:1024:4], T.tt[:, 513:1024:4], [[1, 128]], A.not_equal, OWN, -1, ["t2b"], ["t2b"])
-    sel(T.tt[:, 1024:1536], T.ones[:], [[1, 128], [-1000, 4]], A.is_ge, 0.0, -1, ["ones"], ["t3"], 2000)
-    iota(T.cc[:], [[1, 4], [0, 16]], 0, 0, ["cc"])
-    iota(T.kk[:, 16:64], [[1, 3], [0, 16]], 1, 0, ["kk1"])
-    iota(T.kt[:], [[16, 16]], int(OWN) + 1024, 1, ["kt"])
-    iota(T.nt[:, 1:1024:2], [[0, 512]], 0, 0, ["ntz"])
-    ts(T.sm8[:, 0:8], T.iot[:, 0:8], rf(16), A.is_lt, ["iot", "rf"], ["s8a"], 1.0, A.add)
-    ts(T.sm8[:, 8:16], T.iot[:, 0:8], rf(16), A.is_ge, ["iot", "rf"], ["s8b"], 0.5, A.max)
-    ts(T.mf[:], T.iot[:, 0:16], 16.0, A.mult, ["iot", "rf"], ["mf"], rf(0), A.add)
-    op("V", lambda: V.tensor_reduce(col(3), T.sm8[:, 8:16], AX, A.mult), ["s8b"], ["c3"])
-    op("V", lambda: V.tensor_reduce(col(2), T.sm8[:, 0:8], AX, A.mult), ["s8a"], ["c2"])
-    ts(T.mi[:, 0:16], T.mf[:], col(3), A.mult, ["mf", "c3"], ["mi0"], -0.496, A.add)
-    ts(T.la[:, 2:514:4], T.iot[:, 0:128], rf(20), A.is_equal, ["iot", "rf"], ["la"])
-    ts(T.mi[:, 16:32], T.mi[:, 0:16], 1, A.bitwise_and, ["mi0"], ["mi1"])
-    ts(T.lb[:, 3:515:4], T.iot[:, 0:128], rf(20), A.is_equal, ["iot", "rf"], ["lb"])
-    cp(T.off[:, 42:58], T.mi[:, 16:32], ["mi1"], ["o_m"])
-    act(T.mask[:], T.iot[:, 0:16].indirect(T.off[:, 42:58]), ["iot", "o_m"], ["mask"])
-    ms(T.hd[:, 0:13:12], 0.0, ["hd"])
-    ts(col(8), rf(17), 12.0, A.mult, ["rf"], ["c8"], 19.0, A.add)
-    ts(col(9), rf(24), rf(16), A.is_equal, ["rf"], ["c9"])
-    ts(col(4), rf(19), 4.0, A.mult, ["rf"], ["c4"], 33.0, A.add)
-    ts(col(10), rf(18), rf(16), A.is_equal, ["rf"], ["c10"])
-    ms(T.hd[:, 16:32:2], 0.0, ["hd"])
-    ts(T.lf[:, 8:9], col(8), col(9), A.mult, ["c8", "c9"], ["lf8"])
-    ts(T.lf[:, 9:10], col(8), 32.0, A.add, ["c8", "c9"], ["lf9"], col(9), A.mult)
-    ts(T.mf[:, 0:8], T.iot[:, 0:8], 2.0, A.mult, ["iot", "c4"], ["mf"], col(4), A.add)
-    cp(T.lf[:, 18:22], T.rf[:, 20:24], ["rf"], ["lf18"])
-    ts(T.lf[:, 22:26], T.rf[:, 0:4], 16.0, A.mult, ["rf"], ["lf22"], 15.0, A.add)
-    ts(T.lf[:, 10:18], T.mf[:, 0:8], col(10), A.mult, ["mf", "c10"], ["lf10"])
-    ts(T.tt[:, 1:512:4], T.cw[:, 0:128], 0.0, A.is_equal, ["cw"], ["t1b"], 16.0, A.mult)
-    ts(T.tt[:, 3:512:4], T.cw[:, 0:128], 0.0, A.is_equal, ["cw"], ["t1c"])
-    cp(T.off[:, 8:26], T.lf[:, 8:26], ["lf8", "lf9", "lf10", "lf18", "lf22"], ["o_l"])
-    qz(T.qt[:, 0:128], T.st[:, 0:128], T.tt[:, 0:512], ["t1a", "t1b", "t1c"], ["qt1"])
-    ms(T.hv[:, 0:16], 0.0, ["hvz"])
-    qz(T.qu[:], T.su[:], T.ut[:], ["ut"], ["qu"])
-    ms(T.ot[:, 0:64:2], 0.0, ["otw0"])
-    op("V", lambda: V.tensor_copy(T.qup[:].bitcast(dt.uint32), T.qu[:].bitcast(dt.uint32).indirect(T.off[:, 0:8])),
-       ["qu", "o_u"], ["qup"])
-    act(T.sup[:], T.su[:].indirect(T.off[:, 0:8]), ["qu", "o_u"], ["sup"])
-    act(T.yt[:], T.ot[:, 65:1088:2], ["otz"], ["ytz", "yt"])
+    def engines(c):
+        i, m = T.rank_of(c), -1
+        for t in range(R):
+            m &= topo.mask(c, T.cores[(i + 1 + t) % N])
+        return m
 
     def unpackers(bs):
         for b in bs:
@@ -242,6 +142,90 @@ def rank_program(g, core, T, topo):
             o = 2 - 2 * (b // 2)
             qz(T.qd[:, 128 * b:128 * b + 128], T.sd[:, 128 * b:128 * b + 128], src[:, o:o + 512],
                ["la" if b % 2 == 0 else "lb"], ["qd%d" % b])
+
+    col = lambda i: T.col[:, i:i + 1]
+    rf = lambda i: T.rf[:, i:i + 1]
+
+    dma("A", T.ut[:], T.u[:], (), ["ut"])
+    dma("S", T.xt[:], T.x[:], (), ["X0", "X1"])
+
+    iota(T.pint[:], [[0, 16]], 0, 1, ["pint"], False)
+    iota(T.iot[:], [[1, 256]], 0, 0, ["iot"])
+    ms(T.zz[:], 0.0, ["zz"])
+    dma("S", T.yt[:], T.zz[:, 0:512], ["zz"], ["ytz", "yt"])
+    dma("S", T.nt[:, 0:512], T.zz[:, 0:512], ["zz", "ut"], ["ntz"])
+    dma("S", T.nt[:, 512:1024], T.zz[:, 0:512], ["zz"], ["nty"])
+    act(T.la[:], T.zz[:], ["zz"], ["la"])
+    act(T.lb[:], T.zz[:], ["zz"], ["lb"])
+    act(T.lf[:, 2:8], T.zz[:, 0:6], ["zz"], ["lf2"])
+    ts(T.rint[:, 0:16], T.pint[:], 15, A.bitwise_and, ["pint"], ["ri0"])
+    ts(T.rint[:, 16:17], T.pint[:, 0:1], 4, A.arith_shift_right, ["pint"], ["ri1"])
+    ts(T.rint[:, 17:18], T.pint[:, 0:1], 1, A.bitwise_and, ["pint"], ["ri2"])
+    ts(T.rint[:, 18:19], T.pint[:, 0:1], 7, A.bitwise_and, ["pint"], ["ri3"])
+    ts(T.rint[:, 19:20], T.pint[:, 0:1], 8, A.bitwise_and, ["pint"], ["ri4"])
+    ts(T.rint[:, 24:25], T.pint[:, 0:1], 1, A.arith_shift_right, ["pint"], ["ri6"], 7, A.bitwise_and)
+    cp(T.rint[:, 20:24], T.pint[:, 0:4], ["pint"], ["ri5"])
+    ms(T.ones[:], 1.0, ["ones"])
+    cp(T.rf[:], T.rint[:], ["ri0", "ri1", "ri2", "ri3", "ri4", "ri5", "ri6"], ["rf"])
+    lin(T.mf[:, 0:16], T.iot[:, 0:16], 16.0, rf(0), ["iot", "rf"], ["mf"])
+    lin(col(8), rf(17), 12.0, 19.0, ["rf"], ["c8"])
+    ms(T.ot[:, 1:1088:2], 0.0, ["otz", "otw"])
+    ts(col(1), rf(0), 1.0, A.add, ["rf"], ["c1"])
+    ts(T.cwa[:, 16:32], T.iot[:, 0:16], rf(0), A.not_equal, ["iot", "rf"], ["cwb"])
+    ts(T.cwa[:, 0:16], T.iot[:, 0:16], col(1), A.is_equal, ["iot", "c1"], ["cwa"], HOLD, A.mult)
+    cp(T.off[:, 26:42], T.rf[:, 0:16], ["rf"], ["o_r"])
+    tt(T.cw16[:], T.cwa[:, 0:16], T.cwa[:, 16:32], A.max, ["cwa", "cwb"], ["cw16"])
+    iota(T.gri[:], [[1, 8], [0, 16]], 0, 0, ["gri"])
+    iota(T.hd[:, 0:16], [[0, 16]], 2, 0, ["hd"])
+    iota(T.hd[:, 16:32], [[0, 8], [2, 2]], 0, 0, ["hd2"])
+    sel(T.tt[:, 512:1024:2], T.ones[:, 0:256], [[1, 128], [-1000, 2]], A.is_ge, 0.0, -1, ["ones"], ["t2a"])
+    act(T.cw[:], T.cw16[:].indirect(T.off[:, 26:42]), ["cw16", "o_r"], ["cw"])
+    act(T.tt[:, 0:512:2], T.ones[:, 0:256], ["ones"], ["t1a"])
+    lin(col(4), rf(19), 4.0, 33.0, ["rf"], ["c4"])
+    ts(T.tt[:, 515:1024:4], T.gri[:], rf(16), A.is_equal, ["gri", "rf"], ["t2c"], 4.0, A.mult)
+    sel(T.tt[:, 513:1024:4], T.tt[:, 515:1024:4], [[1, 128]], A.is_gt, 0.0, -1, ["t2c"], ["t2b"])
+    sel(T.tt[:, 513:1024:4], T.tt[:, 513:1024:4], [[1, 128]], A.not_equal, OWN, -1, ["t2b"], ["t2b"])
+    sel(T.tt[:, 1024:1536], T.ones[:], [[1, 128], [-1000, 4]], A.is_ge, 0.0, -1, ["ones"], ["t3"], 2000)
+    iota(T.cc[:], [[1, 4], [0, 16]], 0, 0, ["cc"])
+    iota(T.tv[:, 256:384], [[0, 128]], 0, 0, ["tvz"])
+    iota(T.keep[:], [[0, 64]], 1, 0, ["keep"])
+    iota(T.ct[:, 0:512:2], [[0, 256]], 0, 0, ["ctz0"])
+    iota(T.kt[:], [[16, 16]], int(OWN) + 1024, 1, ["kt"])
+    iota(T.kk[:, 16:64], [[1, 3], [0, 16]], 1, 0, ["kk1"])
+    iota(T.swin[:, 0:128], [[0, 128]], C, 0, ["swin"])
+    iota(T.ft[:, 256:384], [[0, 128]], C, 0, ["ftz"])
+    iota(T.fp[:, 256:4 * FP:FP], [[0, 4]], 0, 0, ["fpz"])
+    iota(T.mate[:, 256:FP], [[0, FP - C]], C, 0, ["matez"])
+    ts(col(0), rf(17), -7.0, A.mult, ["rf"], ["c0"], 1.0, A.add)
+    ts(T.lf[:, 0:1], rf(18), -16.0, A.mult, ["rf"], ["lf0"], 112.0, A.add)
+    ts(T.lf[:, 1:2], rf(0), 8.0, A.mult, ["rf", "c0"], ["lf1"], col(0), A.add)
+    ts(col(9), rf(24), rf(16), A.is_equal, ["rf"], ["c9"])
+    cp(T.off[:, 0:8], T.lf[:, 0:8], ["lf0", "lf1", "lf2"], ["o_u"])
+    ts(col(10), rf(18), rf(16), A.is_equal, ["rf"], ["c10"])
+    lin(T.mf[:, 16:24], T.iot[:, 0:8], 2.0, col(4), ["iot", "c4"], ["mg"])
+    ts(T.sm8[:, 8:16], T.iot[:, 0:8], rf(16), A.is_ge, ["iot", "rf"], ["s8b"], 0.5, A.max)
+    ts(T.sm8[:, 0:8], T.iot[:, 0:8], rf(16), A.is_lt, ["iot", "rf"], ["s8a"], 1.0, A.add)
+    op("V", lambda: V.tensor_reduce(col(3), T.sm8[:, 8:16], AX, A.mult), ["s8b"], ["c3"])
+    op("V", lambda: V.tensor_reduce(col(2), T.sm8[:, 0:8], AX, A.mult), ["s8a"], ["c2"])
+    ts(T.mi[:, 0:16], T.mf[:, 0:16], col(3), A.mult, ["mf", "c3"], ["mi0"], -0.496, A.add)
+    ts(T.lf[:, 8:9], col(8), col(9), A.mult, ["c8", "c9"], ["lf8"])
+    ts(T.mi[:, 16:32], T.mi[:, 0:16], 1, A.bitwise_and, ["mi0"], ["mi1"])
+    ts(T.lf[:, 9:10], col(8), 32.0, A.add, ["c8", "c9"], ["lf9"], col(9), A.mult)
+    cp(T.off[:, 42:58], T.mi[:, 16:32], ["mi1"], ["o_m"])
+    ts(T.tt[:, 1:512:4], T.cw[:, 0:128], 0.0, A.is_equal, ["cw"], ["t1b"], 16.0, A.mult)
+    ts(T.tt[:, 3:512:4], T.cw[:, 0:128], 0.0, A.is_equal, ["cw"], ["t1c"])
+    qz(T.qu[:], T.su[:], T.ut[:], ["ut"], ["qu"])
+    act(T.sup[:], T.su[:].indirect(T.off[:, 0:8]), ["qu", "o_u"], ["sup"])
+    ts(T.la[:, 2:514:4], T.iot[:, 0:128], rf(20), A.is_equal, ["iot", "rf"], ["la"])
+    op("V", lambda: V.tensor_copy(T.qup[:].bitcast(dt.uint32), T.qu[:].bitcast(dt.uint32).indirect(T.off[:, 0:8])),
+       ["qu", "o_u"], ["qup"])
+    ts(T.lb[:, 3:515:4], T.iot[:, 0:128], rf(20), A.is_equal, ["iot", "rf"], ["lb"])
+    unpackers([0, 1])
+    act(T.hd[:, 0:13:12], T.zz[:, 0:2], ["zz"], ["hd"])
+    act(T.mask[:], T.iot[:, 0:16].indirect(T.off[:, 42:58]), ["iot", "o_m"], ["mask"])
+    lin(T.lf[:, 10:18], T.mf[:, 16:24], col(10), None, ["mg", "c10"], ["lf10"])
+    act(T.hv[:, 0:16], T.zz[:, 0:16], ["zz"], ["hvz"])
+    act(T.ot[:, 0:64:2], T.zz[:, 0:32], ["zz"], ["otw0"])
 
     def quant_x(src, h):
         qz(T.qx[:, 128 * h:128 * h + 128], T.sx[:, 128 * h:128 * h + 128], src[:, 512 * h:512 * h + 512],
@@ -253,9 +237,10 @@ def rank_program(g, core, T, topo):
     def signs(h):
         ts(T.bits[:, 32 * h:32 * h + 32], bank(h, 0, 32), 0.0, A.is_gt, ["B%d" % h], ["bits%d" % h])
 
-    def horner(h):
-        scan(T.hv[:, 32 * h + 16:32 * h + 48], T.hd[:], T.bits[:, 32 * h:32 * h + 32], A.mult, A.add,
-             ["hd", "bits%d" % h], ["hv%d" % h])
+    def horner(lo, hi):
+        for h in range(lo, hi):
+            scan(T.hv[:, 32 * h + 16:32 * h + 48], T.hd[:], T.bits[:, 32 * h:32 * h + 32], A.mult, A.add,
+                 ["hd", "hd2", "bits%d" % h], ["hv%d" % h])
 
     def onehot(h):
         ts(T.ot[:, 64 + 2 * h:1088:4], T.iot[:], T.hv[:, 32 * h + 23:32 * h + 24], A.is_equal,
@@ -269,88 +254,89 @@ def rank_program(g, core, T, topo):
         for k in ks:
             act(T.fp[:, FP * k:FP * k + 256], bank(2 + k, 0, 256), ["B%d" % (2 + k)], ["fp%d" % k])
 
+    def pair_flags():
+        tt(T.ct[:, 1:257:4], T.gw[:].indirect(T.off[:, 22:26]), T.thr[:], A.is_equal, ["gw", "o_k", "thr"], ["ct0"])
+
     quant_x(T.xt, 0)
     scores(0)
     quant_x(T.xt, 1)
-    dma("S", T.qw[:].bitcast(dt.uint8), T.wc[:], ["X1"], ["qw"])
+    dma("S", T.qw[:].bitcast(dt.uint8), T.wc[:], ["X1", "nty"], ["qw"])
     dma("S", T.sw[:], T.ws[:], (), ["sw"])
     dma("S", T.vt[:], T.v[:], (), ["vt"])
-    unpackers([0])
+    qz(T.qt[:, 0:128], T.st[:, 0:128], T.tt[:, 0:512], ["t1a", "t1b", "t1c"], ["qt1"])
     signs(0)
-    unpackers([1])
-    horner(0)
 
     hv = ["hv0", "hv1", "hvz"]
     for t in range(R):
         scores(1)
+        unpack_own([0, 1])
         if t > 0:
-            unpack_own(range(4))
-        onehot(0)
-        signs(1)
-        if t == 0:
-            ms(T.tv[:, 256:384], 0.0, ["tvz"])
-        horner(1)
-        if t == 0:
-            ms(T.fp[:, 256:4 * FP:FP], 0.0, ["fpz"])
+            horner(0, 1)
+            onehot(0)
+            signs(1)
+            horner(1, 2)
+        else:
+            cp(T.lf[:, 18:22], T.rf[:, 20:24], ["rf"], ["lf18"])
+            signs(1)
+            horner(0, 2)
+            cp(T.off[:, 8:18], T.lf[:, 8:18], ["lf8", "lf9", "lf10"], ["o_l"])
+            onehot(0)
+        act(T.ot[:, 1:64:2], T.hv[:].indirect(T.off[:, 8:10]), hv + ["o_l"], ["otw"])
         act(T.yt[:, 3:512:4], T.hv[:].indirect(T.off[:, 10:18]), hv + ["o_l"], ["yt"])
         onehot(1)
-        cp(T.ot[:, 1:64:2], T.hv[:].indirect(T.off[:, 8:10]), hv + ["o_l"], ["otw"])
         if t == 0:
-            unpackers([2])
+            ts(T.lf[:, 22:26], T.rf[:, 0:4], 16.0, A.mult, ["rf"], ["lf22"], 15.0, A.add)
         qz(T.qo[:], T.so[:], T.ot[:], ["ot0", "ot1", "otw", "otw0", "otz"], ["qo"])
         qz(T.qy[:], T.sy[:], T.yt[:], ["yt", "ytz"], ["qy"])
         if t == 0:
-            unpackers([3])
+            qz(T.qt[:, 128:384], T.st[:, 128:384], T.tt[:, 512:1536], ["t2a", "t2b", "t2c", "t3"], ["qt2"])
         mmc(0, "t", 0, "o", 0, 272, ["qt1", "qo"])
         mmc(1, "t", 0, "y", 0, 128, ["qt1", "qy"])
-        if t == 0:
-            unpack_own(range(4))
-        copy_own([0, 1, 2] if t > 0 else [0])
+        copy_own([0])
         ts(T.t16[:], bank(0, 0, 16), col(2), A.add, ["B0", "c2"], ["t16"])
         tt(T.tv[:, 0:256], bank(0, 16, 272), T.mask[:], A.min, ["B0", "mask"], ["tv"])
-        if t == 0:
-            qz(T.qt[:, 128:384], T.st[:, 128:384], T.tt[:, 512:1536], ["t2a", "t2b", "t2c", "t3"], ["qt2"])
         mmc(6, "t", 128, "o", 16, 272, ["qt2", "qo"])
         mmc(7, "t", 256, "o", 16, 272, ["qt2", "qo"])
-        act(T.tvr[:], T.tv[:].indirect(T.t16[:]), ["tv", "tvz", "t16"], ["tvr"])
-        act(T.nt[:, 0:1024:4], bank(6, 0, 256), ["B6"], ["nt0"], AF.Relu, -1.0, 1.0)
-        act(T.nt[:, 2:1024:4], bank(7, 0, 256), ["B7"], ["nt1"], AF.Relu, -1.0, 1.0)
-        copy_own([3] if t > 0 else [1, 2, 3])
         if t == 0:
-            ms(T.ct[:, 0:512:2], 0.0, ["ctz0"])
-            ms(T.ct[:, 3:4], 0.0, ["ctz1"])
-            ms(T.keep[:], 1.0, ["keep"])
+            cp(T.off[:, 18:26], T.lf[:, 18:26], ["lf18", "lf22"], ["o_k"])
+            unpackers([2, 3])
+        unpack_own([2, 3])
+        act(T.sym[:], bank(1, 0, 128), ["B1"], ["sym"])
+        cut = 16 if t == 0 else 10
+        act(T.tvr[:, 0:16 * cut], T.tv[:].indirect(T.t16[:, 0:cut]), ["tv", "tvz", "t16"], ["tvr"])
+        act(T.nt[:, 0:1024:4], bank(6, 0, 256), ["B6", "ntz", "nty"], ["nt0"], AF.Relu, -1.0, 1.0)
+        act(T.nt[:, 2:1024:4], bank(7, 0, 256), ["B7", "ntz", "nty"], ["nt1"], AF.Relu, -1.0, 1.0)
+        if t == 0:
             ts(col(5), rf(0), 15.0, A.is_lt, ["rf"], ["c5"], 2.0 * HOLD - 2.0, A.mult)
-            ms(T.keep[:, 15:64:16], 0.0, ["keep"])
-        cp(T.sym[:], bank(1, 0, 128), ["B1"], ["sym"])
+        tt(T.ct[:, 257:513:4], T.sym[:].indirect(T.off[:, 18:22]), T.cc[:], A.is_equal, ["sym", "o_k", "cc"], ["ct2"])
         if t == 0:
             ts(col(6), col(5), 2.0, A.add, ["c5"], ["c6"])
-        tt(T.ct[:, 257:513:4], T.sym[:].indirect(T.off[:, 18:22]), T.cc[:], A.is_equal, ["sym", "o_l", "cc"], ["ct2"])
-        if t == 0:
-            ts(col(7), rf(0), 15.0, A.is_equal, ["rf"], ["c7"], 1.0 / HOLD, A.max)
+            ms(T.keep[:, 15:64:16], 0.0, ["keep"])
+        else:
+            cp(T.tvr[:, 16 * cut:256], T.tv[:].indirect(T.t16[:, cut:16]), ["tv", "tvz", "t16"], ["tvs"])
+        copy_own([1, 2])
         ts(T.thr[:], T.ct[:, 257:513:4], 0.5, A.subtract, ["ct2", "c6"], ["thr"], col(6), A.mult)
-        scan(T.gw[:], T.cw[:], T.tvr[:], A.mult, A.max, ["cw", "tvr"], ["gw"])
+        scan(T.gw[:], T.cw[:], T.tvr[:], A.mult, A.max, ["cw", "tvr", "tvs"], ["gw"])
         scan(T.ct[:, 263:519:4], T.ct[:, 257:513:4], T.keep[:], A.add, A.mult, ["ct2", "keep"], ["ct3"])
-        tt(T.ct[:, 1:257:4], T.gw[:].indirect(T.off[:, 22:26]), T.thr[:], A.is_equal, ["gw", "o_l", "thr"], ["ct0"])
+        pair_flags()
         ts(T.inv[:], T.gw[:, 15:256:16], 2.0, A.mult, ["gw", "c6"], ["inv"], col(6), A.is_lt)
         scan(T.ct[:, 7:263:4], T.ct[:, 1:257:4], T.keep[:], A.add, A.mult, ["ct0", "keep"], ["ct1"])
+        if t == 0:
+            ms(T.ct[:, 3:4], 0.0, ["ctz1"])
         tt(T.kk[:, 0:16], T.inv[:], T.kt[:], A.mult, ["inv", "kt"], ["kk0"])
         qz(T.qc[:], T.sc[:], T.ct[:, 0:512], ["ct0", "ct1", "ct2", "ct3", "ctz0", "ctz1"], ["qc"])
         mmc(1, "t", 128, "c", 0, 128, ["qt2", "qc"])
-        qz(T.qn[:], T.sn[:], T.nt[:], ["nt0", "nt1", "ntz"], ["qn"])
+        qz(T.qn[:], T.sn[:], T.nt[:], ["nt0", "nt1"], ["qn"])
         mmc(0, "t", 0, "n", 0, 256, ["qt1", "qn"])
         tt(T.x1[:, 0:64], bank(1, 0, 64), T.kk[:], A.add, ["B1", "kk0", "kk1"], ["x1a"])
         if t == 0:
-            ms(T.ft[:, 256:384], 256.0, ["ftz"])
+            ts(col(7), rf(0), 15.0, A.is_equal, ["rf"], ["c7"], 1.0 / HOLD, A.max)
         tt(T.x1[:, 64:96], T.x1[:, 0:32], T.x1[:, 32:64], A.max, ["x1a"], ["x1b"])
-        if t == 0:
-            ms(T.mate[:, 256:FP], 256.0, ["matez"])
         tt(T.x1[:, 96:112], T.x1[:, 64:80], T.x1[:, 80:96], A.max, ["x1b"], ["x1c"])
-        if t == 0:
-            ms(T.swin[:, 0:128], 256.0, ["swin"])
         ts(T.p16[:], T.x1[:, 96:112], OWN, A.subtract, ["x1c"], ["p16"])
         act(T.ft[:, 0:256], bank(0, 0, 256), ["B0"], ["ft"])
         act(T.mate[:, 0:256], T.ft[:].indirect(T.t16[:]), ["ft", "ftz", "t16"], ["mate"])
+        copy_own([3])
         cp(T.swin[:].indirect(T.p16[:]), T.iot[:], ["iot", "p16"], ["swin"])
         scan(T.wa[:], T.cw[:, 0:128], T.swin[:, 0:128], A.mult, A.max, ["cw", "swin"], ["wa"])
         ts(T.a16[:], T.wa[:, 15:128:16], col(7), A.mult, ["wa", "c7"], ["a16"])
@@ -369,10 +355,10 @@ def rank_program(g, core, T, topo):
         rid, pid = topo.addr(dst)[0], topo.addr(dst)[1]
         order("G", ["qe%d" % t], (), ())
         g.remote_dma(T["ql%d" % t][:].bitcast(dt.uint8), T["qe%d" % t][:].bitcast(dt.uint8),
-                     T.sem["arr%d" % t], T.sem.sent, pid, rid, topo.mask(core, dst))
-        g.remote_dma(T["sl%d" % t][:], T["se%d" % t][:], T.sem["arr%d" % t], T.sem.sent, pid, rid, topo.mask(core, dst))
-        count["sent"] = count.get("sent", 0) + 2 * len(topo.engines(core, dst))
-        arrived = [("arr%d" % t, 2 * len(topo.engines(src, core)))]
+                     T.sem["arr%d" % t], T.sem.sent, pid, rid, engines(core))
+        g.remote_dma(T["sl%d" % t][:], T["se%d" % t][:], T.sem["arr%d" % t], T.sem.sent, pid, rid, engines(core))
+        count["sent"] = count.get("sent", 0) + 2 * bin(engines(core)).count("1")
+        arrived = [("arr%d" % t, 2 * bin(engines(src)).count("1"))]
         tt(T.x2[:, 0:64], bank(1, 64, 128), T.cc[:], A.add, ["B1", "cc"], ["x2a"])
         if t < R - 1:
             ms(T.swin[:, 0:128], 256.0, ["swin"])
@@ -383,74 +369,78 @@ def rank_program(g, core, T, topo):
         cp(T.k16[:], T.xi[:, 16:32], ["xi1"], ["k16"])
         if t == 0:
             qz(T.qv[:], T.sv[:], T.vt[:], ["vt"], ["qv"])
+        order("V", ["k16", "fp0", "fp1", "fp2", "fp3", "B2", "B3", "B4", "B5"], (), ())
+        order("A", ["k16"], (), ())
+        order("P", ["qw", "sw"], ["B0", "B1", "B6", "B7"], ())
         gb = [0, 1, 6, 7]
-        for k in range(4):
+        for k in (0, 2, 1, 3):
             mmc(gb[k], "d", 128 * k, "l%d" % t, 0, 128, ["qd%d" % k], arrived if k == 0 else ())
-        cp(T.gp[:, 0:128], bank(gb[0], 0, 128), ["B%d" % gb[0]], ["gp0"])
-        for k in range(1, 4):
+        for k in (0, 1):
+            cp(T.gp[:, 128 * k:128 * k + 128], bank(gb[k], 0, 128), ["B%d" % gb[k]], ["gp%d" % k])
+        for k in (2, 3):
             act(T.gp[:, 128 * k:128 * k + 128], bank(gb[k], 0, 128), ["B%d" % gb[k]], ["gp%d" % k])
-        rb = [[2, 0, 1, 6], [7, 3, 4, 5]]
-        for k in (2, 3, 1):
-            act(T.zg[:, 128 * k - 128:128 * k], T.gp[:, 128 * k:128 * k + 128].indirect(T.k16[:, 8:16]),
+        rb = [gb, [2, 3, 4, 5]]
+        for k in range(4):
+            act(T.zg[:, 128 * k:128 * k + 128], T.gp[:, 128 * k:128 * k + 128].indirect(T.k16[:, 8:16]),
                 ["gp%d" % k, "k16"], ["zg%d" % k])
-        for h in range(2):
-            for k in (0, 1, 2, 3) if h == 0 else (0, 2, 3, 1):
-                zo = T.zt[:, 512 * h + k:512 * h + 512:4]
-                if h == 0 or k == 0:
-                    tt(zo, T.gp[:, 128 * k:128 * k + 128].indirect(T.k16[:, 8 * h:8 * h + 8]),
-                       T.fp[:, FP * k + 128 * h:FP * k + 128 * h + 128], A.add,
-                       ["gp%d" % k, "k16", "fp%d" % k], ["z%d%d" % (h, k)])
-                else:
-                    tt(zo, bank(2 + k, 128, 256), T.zg[:, 128 * k - 128:128 * k], A.add,
-                       ["B%d" % (2 + k), "zg%d" % k], ["z%d%d" % (h, k)])
+
+        def zsum(h, k):
+            zo = T.zt[:, 512 * h + k:512 * h + 512:4]
+            if h == 0:
+                tt(zo, T.gp[:, 128 * k:128 * k + 128].indirect(T.k16[:, 0:8]), T.fp[:, FP * k:FP * k + 128], A.add,
+                   ["gp%d" % k, "k16", "fp%d" % k] + (["gp3"] if k == 2 else []), ["z%d%d" % (h, k)])
+            else:
+                tt(zo, bank(2 + k, 128, 256), T.zg[:, 128 * k:128 * k + 128], A.add,
+                   ["B%d" % (2 + k), "zg%d" % k] + (["zg2"] if k == 0 else []), ["z%d%d" % (h, k)])
+
+        def layer(h):
             qz(T.qz[:, 128 * h:128 * h + 128], T.sz[:, 128 * h:128 * h + 128], T.zt[:, 512 * h:512 * h + 512],
                ["z%d%d" % (h, k) for k in range(4)], ["qz%d" % h])
-            for k in range(4):
+            for k in (0, 2, 1, 3):
                 mmc(rb[h][k], "w", 128 * k, "z", 128 * h, 128 * h + 128, ["qw", "sw", "qz%d" % h])
-                o = 512 * h + 128 * k
-                act(T.rl[:, o:o + 128], bank(rb[h][k], 0, 128), ["B%d" % rb[h][k]], ["rl%d%d" % (h, k)], AF.Relu, 0.015625)
-        last = t == R - 1
+                act(T.rl[:, 512 * h + k:512 * h + 512:4], bank(rb[h][k], 0, 128), ["B%d" % rb[h][k]],
+                    ["rl%d%d" % (h, k)], AF.Relu, 0.015625)
 
         def add(h, k):
-            o = 512 * h + 128 * k
-            tt(T.xn[:, 512 * h + k:512 * h + 512:4], T.rl[:, o:o + 128], T.zt[:, 512 * h + k:512 * h + 512:4], A.add,
-               ["rl%d%d" % (h, k), "z%d%d" % (h, k)], ["xn%d%d" % (h, k)])
+            v = slice(512 * h + k, 512 * h + 512, 2)
+            tt(T.xn[:, v], T.rl[:, v], T.zt[:, v], A.add,
+               ["rl%d%d" % (h, k), "rl%d%d" % (h, k + 2), "z%d%d" % (h, k), "z%d%d" % (h, k + 2)], ["xn%d%d" % (h, k)])
 
         def newx(h):
             qz(T.qx[:, 128 * h:128 * h + 128], T.sx[:, 128 * h:128 * h + 128], T.xn[:, 512 * h:512 * h + 512],
-               ["xn%d%d" % (h, k) for k in range(4)], ["qx%d" % h])
+               ["xn%d0" % h, "xn%d1" % h], ["qx%d" % h])
 
-        def store(h, qa, qb):
+        def store(h, qc, qs):
             lo, hi = 128 * h, 128 * h + 128
-            dma(qa, T.oc[:, 4 * lo:4 * hi], T.qx[:, lo:hi].bitcast(dt.uint8), ["qx%d" % h])
-            for k in range(4):
-                dma(qb if k < 2 else qa, T.osc[4 * k:4 * k + 4, lo:hi], T.sx[32 * k:32 * k + 4, lo:hi], ["qx%d" % h])
+            dma(qc, T.oc[:, 4 * lo:4 * hi], T.qx[:, lo:hi].bitcast(dt.uint8), ["qx%d" % h])
+            for k in range(len(qs)):
+                dma(qs[k], T.osc[4 * k:4 * k + 4, :], T.sx[32 * k:32 * k + 4, :], ["qx0", "qx1"])
 
         for k in range(4):
-            add(0, k)
-        if last:
-            add(1, 0)
-            newx(0)
-            mmc(2, "v", 0, "x", 0, 128, ["qv", "qx0"])
-            store(0, "S", "S")
-            act(T.yo[:, 0:128], bank(2, 0, 128), ["B2"], ["yo0"])
+            zsum(0, k)
+        layer(0)
+        for k in range(4):
+            zsum(1, k)
+        layer(1)
+        add(0, 0)
+        add(0, 1)
+        add(1, 0)
+        newx(0)
+        if t == R - 1:
+            mmc(0, "v", 0, "x", 0, 128, ["qv", "qx0"])
+            store(0, "S", "")
+            act(T.yo[:, 0:128], bank(0, 0, 128), ["B0"], ["yo0"])
             dma("A", T.y[:, 0:128], T.yo[:, 0:128], ["yo0"])
-            for k in range(1, 4):
-                add(1, k)
+            add(1, 1)
             newx(1)
-            mmc(0, "v", 0, "x", 128, 256, ["qv", "qx1"])
-            store(1, "A", "S")
-            cp(T.yo[:, 128:256], bank(0, 0, 128), ["B0"], ["yo1"])
+            mmc(1, "v", 0, "x", 128, 256, ["qv", "qx1"])
+            store(1, "A", "SAAA")
+            cp(T.yo[:, 128:256], bank(1, 0, 128), ["B1"], ["yo1"])
             dma("S", T.y[:, 128:256], T.yo[:, 128:256], ["yo1"])
         else:
-            add(1, 0)
-            newx(0)
             scores(0)
             add(1, 1)
-            add(1, 2)
             signs(0)
-            add(1, 3)
-            horner(0)
             newx(1)
 
     for s, n in sorted(count.items()):

@@ -2,23 +2,24 @@ from concourse.mybir import dt, AluOpType, AxisListType, ActivationFunctionType
 
 N, C, M, R = 8, 256, 32, 3
 X4, U8, BF, F32, I32, U16 = "float8_e4m3fn_x4", "uint8", "bfloat16", "float32", "int32", "uint16"
-FP = C + 16
 OWN = 2048.0
-HOLD = 4096.0
-SWW = 2416
+HOLD = 256.0
+DUMP = 4 * C + 4
+SWW = 1408
+NEAR = 1.5 * 2.0 ** 31
 
 SCRATCH = {"ps": ("psum", [128, 4096], F32)}
 for _d, _l in (
-    (BF, "xt:1024 ut:512 vt:512 xn:1024 zt:1024 et:512 ones:512 zz:516 tt:1536 la:516 lb:516 iot:256 cwa:32 cw16:16 "
-         "cw:256 mask:256 hd:32 keep:64 gri:128 bits:64 hv:80 ot:1088 yt:512 nt:1024 ct:520 tv:384 ft:384 tvr:256 "
-         "mate:%d gw:256 sym:128 thr:64 swin:%d wa:128 wb:128 brow:128 fp:%d ap:512 gp:512 zg:512" % (FP, SWW, 4 * FP)),
-    (F32, "rf:25 col:16 sm8:16 lf:32 mf:24 cc:64 kk:64 kt:16 inv:16 x1:112 x2:112 rl:1024 yo:256"),
-    (I32, "pint:16 rint:25 mi:32 xi:32"),
-    (U16, "off:64 t16:16 p16:16 k16:16 a16:8 b16:8"),
+    (BF, "xt:1024 ut:512 vt:512 xn:1024 zt:1024 et:512 tt:1536 la:516 iot:256 dd:96 cw:256 cw8:256 hd:48 gri:128 keep:32 "
+         "sg:48 hv:208 ot:1024 ct:664 cc:80 tf:640 tvr:256 mate:272 gw:256 sym:128 thr:80 "
+         "swin:%d wa:128 wa8:128 wb8:128 brow:128 fa:528 fb:528 ap:512 ga:256 gb:256 zg:512 m128:1024 tkb:256 wk:256" % SWW),
+    (F32, "rf:52 col:16 sm8:8 lf:32 kd:80 x1:80 x2:80 rl:1024 yo:256"),
+    (I32, "rint:52 ji:6"),
+    (U16, "off:64 t16:16 p16:16 k16:16 a16:8 a8:16 b8:16 k8:32"),
 ):
     for _e in _l.split():
         SCRATCH[_e.split(":")[0]] = ("sbuf", [128, int(_e.split(":")[1])], _d)
-for _e in "x:256 z:256 u:128 up:128 v:128 w:512 t:384 d:512 o:272 y:128 n:256 c:128 e0:128 e1:128 e2:128 l0:128 l1:128 l2:128".split():
+for _e in "x:256 z:256 u:128 up:128 v:128 w:512 t:384 d:512 o:256 y:160 n:256 c:160 e0:128 e1:128 e2:128 l0:128 l1:128 l2:128".split():
     SCRATCH["q" + _e.split(":")[0]] = ("sbuf", [128, int(_e.split(":")[1])], X4)
     SCRATCH["s" + _e.split(":")[0]] = ("sbuf", [128, int(_e.split(":")[1])], U8)
 
@@ -102,7 +103,7 @@ def rank_program(g, core, T, topo):
     def qz(q, s, t, r, w):
         op("V", lambda: V.quantize_mx(q, s, t), r, w)
 
-    def act(out, in_, r, w, f=None, scale=None, bias=None):
+    def act(out, in_, r, w, f=None, scale=1.0, bias=None):
         if f is None:
             op("A", lambda: S_.activation(out, in_, AF.Copy), r, w)
         elif bias is None:
@@ -125,10 +126,19 @@ def rank_program(g, core, T, topo):
     def bank(b, lo, hi):
         return T.ps[:, 512 * b + lo:512 * b + hi]
 
-    def mmc(b, lname, la, rname, ra, rb, r, ext=()):
+    def mmc(b, lname, la, rname, ra, rb, r, ext=(), shift=0):
         lq, ls = T["q" + lname][:, la:la + 128], T["s" + lname][:, la:la + 128]
-        rq, rs = T["q" + rname][:, ra:rb], T["s" + rname][:, ra:rb]
-        op("P", lambda: g.tensor.matmul_mx(bank(b, 0, rb - ra), lq, ls, rq, rs, True, True), r, ["B%d" % b], ext)
+
+        def mm(o, start, stop):
+            return g.tensor.matmul_mx(bank(b, 0, rb - ra), lq, ls, T["q" + rname][:, ra + o:rb + o],
+                                      T["s" + rname][:, ra + o:rb + o], start, stop)
+
+        def call():
+            if shift:
+                mm(shift, True, False).then_inc(T.sem.cP, 1)
+                count["cP"] += 1
+            return mm(0, not shift, True)
+        op("P", call, r, ["B%d" % b], ext)
 
     def engines(c):
         i, m = T.rank_of(c), -1
@@ -138,94 +148,61 @@ def rank_program(g, core, T, topo):
 
     def unpackers(bs):
         for b in bs:
-            src = T.la if b % 2 == 0 else T.lb
-            o = 2 - 2 * (b // 2)
-            qz(T.qd[:, 128 * b:128 * b + 128], T.sd[:, 128 * b:128 * b + 128], src[:, o:o + 512],
-               ["la" if b % 2 == 0 else "lb"], ["qd%d" % b])
+            qz(T.qd[:, 128 * b:128 * b + 128], T.sd[:, 128 * b:128 * b + 128], T.la[:, 3 - b:515 - b], ["la"], ["qd%d" % b])
 
     col = lambda i: T.col[:, i:i + 1]
-    rf = lambda i: T.rf[:, i:i + 1]
+    R16, G16, R8, K64, R2 = [T.rf[:, i:i + 1] for i in (0, 16, 17, 18, 19)]
+    ones = T.tt[:, 513:1024:2]
+    ft, tv = T.tf[:, 0:384], T.tf[:, 256:640]
+    lu, lr, ly, ls_, lg = [T.off[:, a:b] for a, b in ((0, 8), (4, 20), (20, 30), (30, 35), (36, 41))]
 
+    dma("S", T.xt[:, 0:512], T.x[:, 0:512], (), ["X0"])
     dma("A", T.ut[:], T.u[:], (), ["ut"])
-    dma("S", T.xt[:], T.x[:], (), ["X0", "X1"])
+    dma("S", T.xt[:, 512:1024], T.x[:, 512:1024], (), ["X1"])
 
-    iota(T.pint[:], [[0, 16]], 0, 1, ["pint"], False)
+    iota(T.rint[:, 0:16], [[0, 16]], 0, 16, ["ri0"], False)
+    for i, m in ((16, 1), (17, 32), (18, 64), (19, 128)):
+        iota(T.rint[:, i:i + 1], [[0, 1]], 0, m, ["ri%d" % i], False)
+    iota(T.rint[:, 20:36], [[16, 16]], 2048, -16, ["ri20"], False)
+    iota(T.rint[:, 36:52], [[0, 2], [32, 8]], 2064, -16, ["ri36"], False)
+    iota(T.lf[:, 0:2], [[256, 2]], 12, 0, ["lf0"])
     iota(T.iot[:], [[1, 256]], 0, 0, ["iot"])
-    ms(T.zz[:], 0.0, ["zz"])
-    dma("S", T.yt[:], T.zz[:, 0:512], ["zz"], ["ytz", "yt"])
-    dma("S", T.nt[:, 0:512], T.zz[:, 0:512], ["zz", "ut"], ["ntz"])
-    dma("S", T.nt[:, 512:1024], T.zz[:, 0:512], ["zz"], ["nty"])
-    act(T.la[:], T.zz[:], ["zz"], ["la"])
-    act(T.lb[:], T.zz[:], ["zz"], ["lb"])
-    act(T.lf[:, 2:8], T.zz[:, 0:6], ["zz"], ["lf2"])
-    ts(T.rint[:, 0:16], T.pint[:], 15, A.bitwise_and, ["pint"], ["ri0"])
-    ts(T.rint[:, 16:17], T.pint[:, 0:1], 4, A.arith_shift_right, ["pint"], ["ri1"])
-    ts(T.rint[:, 17:18], T.pint[:, 0:1], 1, A.bitwise_and, ["pint"], ["ri2"])
-    ts(T.rint[:, 18:19], T.pint[:, 0:1], 7, A.bitwise_and, ["pint"], ["ri3"])
-    ts(T.rint[:, 19:20], T.pint[:, 0:1], 8, A.bitwise_and, ["pint"], ["ri4"])
-    ts(T.rint[:, 24:25], T.pint[:, 0:1], 1, A.arith_shift_right, ["pint"], ["ri6"], 7, A.bitwise_and)
-    cp(T.rint[:, 20:24], T.pint[:, 0:4], ["pint"], ["ri5"])
-    ms(T.ones[:], 1.0, ["ones"])
-    cp(T.rf[:], T.rint[:], ["ri0", "ri1", "ri2", "ri3", "ri4", "ri5", "ri6"], ["rf"])
-    lin(T.mf[:, 0:16], T.iot[:, 0:16], 16.0, rf(0), ["iot", "rf"], ["mf"])
-    lin(col(8), rf(17), 12.0, 19.0, ["rf"], ["c8"])
-    ms(T.ot[:, 1:1088:2], 0.0, ["otz", "otw"])
-    ts(col(1), rf(0), 1.0, A.add, ["rf"], ["c1"])
-    ts(T.cwa[:, 16:32], T.iot[:, 0:16], rf(0), A.not_equal, ["iot", "rf"], ["cwb"])
-    ts(T.cwa[:, 0:16], T.iot[:, 0:16], col(1), A.is_equal, ["iot", "c1"], ["cwa"], HOLD, A.mult)
-    cp(T.off[:, 26:42], T.rf[:, 0:16], ["rf"], ["o_r"])
-    tt(T.cw16[:], T.cwa[:, 0:16], T.cwa[:, 16:32], A.max, ["cwa", "cwb"], ["cw16"])
-    iota(T.gri[:], [[1, 8], [0, 16]], 0, 0, ["gri"])
-    iota(T.hd[:, 0:16], [[0, 16]], 2, 0, ["hd"])
-    iota(T.hd[:, 16:32], [[0, 8], [2, 2]], 0, 0, ["hd2"])
-    sel(T.tt[:, 512:1024:2], T.ones[:, 0:256], [[1, 128], [-1000, 2]], A.is_ge, 0.0, -1, ["ones"], ["t2a"])
-    act(T.cw[:], T.cw16[:].indirect(T.off[:, 26:42]), ["cw16", "o_r"], ["cw"])
-    act(T.tt[:, 0:512:2], T.ones[:, 0:256], ["ones"], ["t1a"])
-    lin(col(4), rf(19), 4.0, 33.0, ["rf"], ["c4"])
-    ts(T.tt[:, 515:1024:4], T.gri[:], rf(16), A.is_equal, ["gri", "rf"], ["t2c"], 4.0, A.mult)
-    sel(T.tt[:, 513:1024:4], T.tt[:, 515:1024:4], [[1, 128]], A.is_gt, 0.0, -1, ["t2c"], ["t2b"])
-    sel(T.tt[:, 513:1024:4], T.tt[:, 513:1024:4], [[1, 128]], A.not_equal, OWN, -1, ["t2b"], ["t2b"])
-    sel(T.tt[:, 1024:1536], T.ones[:], [[1, 128], [-1000, 4]], A.is_ge, 0.0, -1, ["ones"], ["t3"], 2000)
-    iota(T.cc[:], [[1, 4], [0, 16]], 0, 0, ["cc"])
-    iota(T.tv[:, 256:384], [[0, 128]], 0, 0, ["tvz"])
-    iota(T.keep[:], [[0, 64]], 1, 0, ["keep"])
-    iota(T.ct[:, 0:512:2], [[0, 256]], 0, 0, ["ctz0"])
-    iota(T.kt[:], [[16, 16]], int(OWN) + 1024, 1, ["kt"])
-    iota(T.kk[:, 16:64], [[1, 3], [0, 16]], 1, 0, ["kk1"])
-    iota(T.swin[:, 0:128], [[0, 128]], C, 0, ["swin"])
-    iota(T.ft[:, 256:384], [[0, 128]], C, 0, ["ftz"])
-    iota(T.fp[:, 256:4 * FP:FP], [[0, 4]], 0, 0, ["fpz"])
-    iota(T.mate[:, 256:FP], [[0, FP - C]], C, 0, ["matez"])
-    ts(col(0), rf(17), -7.0, A.mult, ["rf"], ["c0"], 1.0, A.add)
-    ts(T.lf[:, 0:1], rf(18), -16.0, A.mult, ["rf"], ["lf0"], 112.0, A.add)
-    ts(T.lf[:, 1:2], rf(0), 8.0, A.mult, ["rf", "c0"], ["lf1"], col(0), A.add)
-    ts(col(9), rf(24), rf(16), A.is_equal, ["rf"], ["c9"])
-    cp(T.off[:, 0:8], T.lf[:, 0:8], ["lf0", "lf1", "lf2"], ["o_u"])
-    ts(col(10), rf(18), rf(16), A.is_equal, ["rf"], ["c10"])
-    lin(T.mf[:, 16:24], T.iot[:, 0:8], 2.0, col(4), ["iot", "c4"], ["mg"])
-    ts(T.sm8[:, 8:16], T.iot[:, 0:8], rf(16), A.is_ge, ["iot", "rf"], ["s8b"], 0.5, A.max)
-    ts(T.sm8[:, 0:8], T.iot[:, 0:8], rf(16), A.is_lt, ["iot", "rf"], ["s8a"], 1.0, A.add)
-    op("V", lambda: V.tensor_reduce(col(3), T.sm8[:, 8:16], AX, A.mult), ["s8b"], ["c3"])
-    op("V", lambda: V.tensor_reduce(col(2), T.sm8[:, 0:8], AX, A.mult), ["s8a"], ["c2"])
-    ts(T.mi[:, 0:16], T.mf[:, 0:16], col(3), A.mult, ["mf", "c3"], ["mi0"], -0.496, A.add)
-    ts(T.lf[:, 8:9], col(8), col(9), A.mult, ["c8", "c9"], ["lf8"])
-    ts(T.mi[:, 16:32], T.mi[:, 0:16], 1, A.bitwise_and, ["mi0"], ["mi1"])
-    ts(T.lf[:, 9:10], col(8), 32.0, A.add, ["c8", "c9"], ["lf9"], col(9), A.mult)
-    cp(T.off[:, 42:58], T.mi[:, 16:32], ["mi1"], ["o_m"])
-    ts(T.tt[:, 1:512:4], T.cw[:, 0:128], 0.0, A.is_equal, ["cw"], ["t1b"], 16.0, A.mult)
-    ts(T.tt[:, 3:512:4], T.cw[:, 0:128], 0.0, A.is_equal, ["cw"], ["t1c"])
+    ms(T.tt[:, 0:1024], 1.0, ["ones", "t1b", "t1c", "t3"])
+    ms(T.ot[:, 1:1024:2], 0.0, ["otz"])
+    ms(T.ct[:], 0.0, ["ct", "cu", "ctz"])
+    lin(T.la[:], T.tt[:, 0:516], 0.0, None, ["ones", "t1b", "t1c", "t3"], ["la"])
+    lin(T.tt[:, 3:512:4], T.tt[:, 512:640], 0.0, None, ["ones", "t3"], ["t1c"])
+    ts(T.rint[:, 0:36], T.rint[:, 0:36], 240, A.bitwise_and, ["ri0", "ri16", "ri17", "ri18", "ri19"], ["ri20"])
+    ts(T.rint[:, 36:52], T.rint[:, 36:52], 1, A.arith_shift_right, [], ["ri36"], 112, A.bitwise_and)
+    cp(T.rf[:], T.rint[:], ["ri20", "ri36"], ["rf"])
+    iota(T.hv[:, 0:112], [[0, 112]], 0, 0, ["bits0", "bits1", "hvz"])
+    iota(col(12), [[0, 1]], 0, 1, ["c12"])
+    iota(T.hd[:], [[0, 48]], 2, 0, ["hd", "hd1"])
+    iota(T.gri[:], [[16, 8], [0, 16]], 0, 0, ["gri"])
+    iota(T.hd[:, 1:32:4], [[0, 8]], 0, 0, ["hd"])
+    iota(T.hd[:, 36:41:4], [[0, 2]], 0, 0, ["hd1"])
+    sel(T.tt[:, 1024:1536:2], ones, [[1, 128], [-1000, 2]], A.is_ge, 0.0, -1, ["ones"], ["t2a"])
+    sel(T.tt[:, 514:1024:4], T.tt[:, 513:1024:4], [[1, 128]], A.is_ge, 0.0, -1, ["ones"], ["t3"])
+    ts(col(0), K64, -0.3125, A.mult, ["rf"], ["c0"], R16, A.add)
+    ts(lr, T.rf[:, 0:16], 0.0625, A.mult, ["rf"], ["lr"])
+    ts(T.off[:, 2:4], T.rf[:, 17:19], -0.5, A.mult, ["rf"], ["lu2"], 112.0, A.add)
+    ts(T.off[:, 0:2], T.lf[:, 0:2], col(0), A.add, ["lf0", "c0"], ["lu0"], 0.25, A.mult)
+    act(T.dd[:, 0:32], T.rf[:, 20:52], ["rf"], ["dd0"], AF.Relu, -0.375 * HOLD, 6.0 * HOLD)
+    act(T.dd[:, 32:64], T.rf[:, 20:52], ["rf"], ["dd1"], AF.Relu, -HOLD / 16, 2.0 * HOLD)
+    lin(col(3), R16, 0.375, 19.0, ["rf"], ["c3"])
+    lin(col(11), R16, 0.0125, -0.4, ["rf"], ["c11"])
+    lin(col(4), R8, -0.1875, col(3), ["rf", "c3"], ["c4"])
+    ts(col(10), R8, 0.5, A.mult, ["rf"], ["c10"], G16, A.is_equal)
     qz(T.qu[:], T.su[:], T.ut[:], ["ut"], ["qu"])
-    act(T.sup[:], T.su[:].indirect(T.off[:, 0:8]), ["qu", "o_u"], ["sup"])
-    ts(T.la[:, 2:514:4], T.iot[:, 0:128], rf(20), A.is_equal, ["iot", "rf"], ["la"])
-    op("V", lambda: V.tensor_copy(T.qup[:].bitcast(dt.uint32), T.qu[:].bitcast(dt.uint32).indirect(T.off[:, 0:8])),
-       ["qu", "o_u"], ["qup"])
-    ts(T.lb[:, 3:515:4], T.iot[:, 0:128], rf(20), A.is_equal, ["iot", "rf"], ["lb"])
-    unpackers([0, 1])
-    act(T.hd[:, 0:13:12], T.zz[:, 0:2], ["zz"], ["hd"])
-    act(T.mask[:], T.iot[:, 0:16].indirect(T.off[:, 42:58]), ["iot", "o_m"], ["mask"])
-    lin(T.lf[:, 10:18], T.mf[:, 16:24], col(10), None, ["mg", "c10"], ["lf10"])
-    act(T.hv[:, 0:16], T.zz[:, 0:16], ["zz"], ["hvz"])
-    act(T.ot[:, 0:64:2], T.zz[:, 0:32], ["zz"], ["otw0"])
+    tt(T.dd[:, 64:96], T.dd[:, 0:32], T.dd[:, 32:64], A.subtract, ["dd0", "dd1"], ["dd2"])
+    act(T.sup[:], T.su[:].indirect(lu), ["qu", "lu0", "lu2", "lr"], ["sup"])
+    op("V", lambda: V.tensor_copy(T.qup[:].bitcast(dt.uint32), T.qu[:].bitcast(dt.uint32).indirect(lu)),
+       ["qu", "lu0", "lu2", "lr"], ["qup"])
+    act(T.cw[:], T.dd[:, 64:80].indirect(lr), ["dd2", "lr"], ["cw"])
+    lin(T.lf[:, 10:18], T.iot[:, 0:8], 4.0, col(4), ["iot", "c4"], ["lf10"])
+    lin(T.lf[:, 18:20], T.iot[:, 9:12:2], 4.0, col(4), ["iot", "c4"], ["lf18"])
+    act(T.tt[:, 1:512:4], T.cw[:, 0:128], ["cw"], ["t1b"], AF.Relu, 0.25 / HOLD)
+    lin(T.lf[:, 20:26], T.iot[:, 0:6], 3.2, col(11), ["iot", "c11"], ["lf20"])
 
     def quant_x(src, h):
         qz(T.qx[:, 128 * h:128 * h + 128], T.sx[:, 128 * h:128 * h + 128], src[:, 512 * h:512 * h + 512],
@@ -235,121 +212,137 @@ def rank_program(g, core, T, topo):
         mmc(h, "x", 128 * h, "up", 0, 128, ["qx%d" % h, "qup", "sup"])
 
     def signs(h):
-        ts(T.bits[:, 32 * h:32 * h + 32], bank(h, 0, 32), 0.0, A.is_gt, ["B%d" % h], ["bits%d" % h])
+        ts(T.hv[:, 48 * h:48 * h + 44], bank(h, 0, 44), 0.0, A.is_gt, ["B%d" % h], ["bits%d" % h])
 
-    def horner(lo, hi):
-        for h in range(lo, hi):
-            scan(T.hv[:, 32 * h + 16:32 * h + 48], T.hd[:], T.bits[:, 32 * h:32 * h + 32], A.mult, A.add,
-                 ["hd", "hd2", "bits%d" % h], ["hv%d" % h])
+    def horner(h):
+        scan(T.hv[:, 48 * h + 112:48 * h + 160], T.hd[:], T.hv[:, 48 * h:48 * h + 48], A.mult, A.add,
+             ["hd", "hd1", "bits%d" % h], ["hv%d" % h])
 
     def onehot(h):
-        ts(T.ot[:, 64 + 2 * h:1088:4], T.iot[:], T.hv[:, 32 * h + 23:32 * h + 24], A.is_equal,
-           ["iot", "hv%d" % h], ["ot%d" % h])
+        ts(T.ot[:, 2 * h:1024:4], T.iot[:], T.hv[:, 48 * h + 159:48 * h + 160], A.subtract,
+           ["iot", "hv%d" % h], ["ot%d" % h], T.hv[:, 48 * h + 151:48 * h + 152], A.is_equal)
 
     def unpack_own(ks):
         for k in ks:
             mmc(2 + k, "d", 128 * k, "x", 0, 256, ["qd%d" % k, "qx0", "qx1"])
 
+    def plane(a, b, k, n):
+        return (a, b)[k % 2][:, k // 2:2 * n:2]
+
     def copy_own(ks):
         for k in ks:
-            act(T.fp[:, FP * k:FP * k + 256], bank(2 + k, 0, 256), ["B%d" % (2 + k)], ["fp%d" % k])
-
-    def pair_flags():
-        tt(T.ct[:, 1:257:4], T.gw[:].indirect(T.off[:, 22:26]), T.thr[:], A.is_equal, ["gw", "o_k", "thr"], ["ct0"])
+            act(plane(T.fa, T.fb, k, C), bank(2 + k, 0, 256), ["B%d" % (2 + k)], ["fp%d" % k])
 
     quant_x(T.xt, 0)
     scores(0)
     quant_x(T.xt, 1)
-    dma("S", T.qw[:].bitcast(dt.uint8), T.wc[:], ["X1", "nty"], ["qw"])
+    dma("S", T.qw[:].bitcast(dt.uint8), T.wc[:], ["X1"], ["qw"])
     dma("S", T.sw[:], T.ws[:], (), ["sw"])
     dma("S", T.vt[:], T.v[:], (), ["vt"])
-    qz(T.qt[:, 0:128], T.st[:, 0:128], T.tt[:, 0:512], ["t1a", "t1b", "t1c"], ["qt1"])
+    ts(T.tt[:, 1027:1536:4], T.gri[:], G16, A.is_equal, ["gri", "rf"], ["t2c"], 4.0, A.mult)
+    ts(T.la[:, 3:515:4], T.iot[:, 0:128], col(12), A.is_equal, ["iot", "c12"], ["la"])
     signs(0)
+    unpackers([0])
+    sel(T.tt[:, 1025:1536:4], T.tt[:, 1027:1536:4], [[1, 128]], A.is_gt, 0.0, -1, ["t2c"], ["t2b"])
+    iota(T.tf[:, 512:640], [[0, 128]], 0, 0, ["tvz"])
+    sel(T.tt[:, 1025:1536:4], T.tt[:, 1025:1536:4], [[1, 128]], A.not_equal, -OWN, -1, ["t2b"], ["t2b"])
+    iota(T.cc[:], [[0, 16], [256, 5]], -192, 0, ["cc"])
+    sel(T.keep[:], T.tt[:, 513:577:2], [[1, 32]], A.not_equal, 0.0, 0, ["ones"], ["keep"], -15)
+    iota(T.cc[:, 0:80:5], [[0, 16]], 8192, 0, ["cc"])
+    iota(T.kd[:], [[0, 80]], -1, 0, ["kd", "kd1"])
+    iota(T.swin[:, 0:128], [[0, 128]], C, 0, ["swin"])
+    iota(T.kd[:, 0:80:5], [[16, 16]], DUMP - int(OWN), 1, ["kd"])
+    iota(T.kd[:, 4:80:5], [[0, 16]], int(OWN) + 3, 0, ["kd1"])
+    iota(T.m128[:, 0:256], [[0, 2], [1, 128]], 0, 0, ["m0"])
+    iota(T.mate[:, 256:272], [[0, 16]], C, 0, ["matez"])
+    iota(T.fa[:, 512:528], [[0, 16]], 0, 0, ["faz"])
+    iota(T.fb[:, 512:528], [[0, 16]], 0, 0, ["fbz"])
+    for k in (1, 2, 3):
+        dma("S", T.m128[:, 256 * k:256 * k + 256], T.m128[:, 0:256], ["m0"], ["m%d" % k])
 
     hv = ["hv0", "hv1", "hvz"]
     for t in range(R):
+        first = t == 0
         scores(1)
-        unpack_own([0, 1])
-        if t > 0:
-            horner(0, 1)
-            onehot(0)
-            signs(1)
-            horner(1, 2)
-        else:
-            cp(T.lf[:, 18:22], T.rf[:, 20:24], ["rf"], ["lf18"])
-            signs(1)
-            horner(0, 2)
-            cp(T.off[:, 8:18], T.lf[:, 8:18], ["lf8", "lf9", "lf10"], ["o_l"])
-            onehot(0)
-        act(T.ot[:, 1:64:2], T.hv[:].indirect(T.off[:, 8:10]), hv + ["o_l"], ["otw"])
-        act(T.yt[:, 3:512:4], T.hv[:].indirect(T.off[:, 10:18]), hv + ["o_l"], ["yt"])
+        if not first:
+            unpack_own([0, 2])
+        horner(0)
+        signs(1)
+        onehot(0)
+        horner(1)
+        if first:
+            unpackers([2])
+            unpack_own([0, 2])
+            ts(ly, T.lf[:, 10:20], col(10), A.mult, ["lf10", "lf18", "c10"], ["ly"])
+        act(T.ct[:, 1:640:4], T.hv[:, 96:208].indirect(ly), hv + ["ly"], ["ct", "cu"])
         onehot(1)
-        if t == 0:
-            ts(T.lf[:, 22:26], T.rf[:, 0:4], 16.0, A.mult, ["rf"], ["lf22"], 15.0, A.add)
-        qz(T.qo[:], T.so[:], T.ot[:], ["ot0", "ot1", "otw", "otw0", "otz"], ["qo"])
-        qz(T.qy[:], T.sy[:], T.yt[:], ["yt", "ytz"], ["qy"])
-        if t == 0:
-            qz(T.qt[:, 128:384], T.st[:, 128:384], T.tt[:, 512:1536], ["t2a", "t2b", "t2c", "t3"], ["qt2"])
-        mmc(0, "t", 0, "o", 0, 272, ["qt1", "qo"])
-        mmc(1, "t", 0, "y", 0, 128, ["qt1", "qy"])
+        if first:
+            qz(T.qt[:, 0:128], T.st[:, 0:128], T.tt[:, 0:512], ["t1b", "t1c"], ["qt1"])
+        qz(T.qo[:], T.so[:], T.ot[:], ["ot0", "ot1", "otz"], ["qo"])
+        if first:
+            ts(T.sm8[:], T.iot[:, 0:128:16], G16, A.is_lt, ["iot", "rf"], ["s8"], 1.0, A.add)
+            unpackers([1])
+        qz(T.qy[:], T.sy[:], T.ct[:, 0:640], ["ct", "cu", "ct0", "ct1", "ct2", "ct3"], ["qy"])
+        mmc(0, "t", 0, "o", 0, 256, ["qt1", "qo"])
+        mmc(1, "t", 0, "y", 16, 144, ["qt1", "qy"], (), 16)
+        mmc(5, "t", 0, "y", 0, 128, ["qt1", "qy"])
+        if first:
+            op("V", lambda: V.tensor_reduce(col(2), T.sm8[:], AX, A.mult), ["s8"], ["c2"])
+            cp(T.ji[:], T.lf[:, 20:26], ["lf20"], ["ji"])
+            ts(T.col[:, 5:7], T.rf[:, 35:44:8], 0.0, A.is_gt, ["rf"], ["c5"], HOLD, A.mult)
+            unpackers([3])
         copy_own([0])
-        ts(T.t16[:], bank(0, 0, 16), col(2), A.add, ["B0", "c2"], ["t16"])
-        tt(T.tv[:, 0:256], bank(0, 16, 272), T.mask[:], A.min, ["B0", "mask"], ["tv"])
-        mmc(6, "t", 128, "o", 16, 272, ["qt2", "qo"])
-        mmc(7, "t", 256, "o", 16, 272, ["qt2", "qo"])
-        if t == 0:
-            cp(T.off[:, 18:26], T.lf[:, 18:26], ["lf18", "lf22"], ["o_k"])
-            unpackers([2, 3])
-        unpack_own([2, 3])
-        act(T.sym[:], bank(1, 0, 128), ["B1"], ["sym"])
-        cut = 16 if t == 0 else 10
-        act(T.tvr[:, 0:16 * cut], T.tv[:].indirect(T.t16[:, 0:cut]), ["tv", "tvz", "t16"], ["tvr"])
-        act(T.nt[:, 0:1024:4], bank(6, 0, 256), ["B6", "ntz", "nty"], ["nt0"], AF.Relu, -1.0, 1.0)
-        act(T.nt[:, 2:1024:4], bank(7, 0, 256), ["B7", "ntz", "nty"], ["nt1"], AF.Relu, -1.0, 1.0)
-        if t == 0:
-            ts(col(5), rf(0), 15.0, A.is_lt, ["rf"], ["c5"], 2.0 * HOLD - 2.0, A.mult)
-        tt(T.ct[:, 257:513:4], T.sym[:].indirect(T.off[:, 18:22]), T.cc[:], A.is_equal, ["sym", "o_k", "cc"], ["ct2"])
-        if t == 0:
-            ts(col(6), col(5), 2.0, A.add, ["c5"], ["c6"])
-            ms(T.keep[:, 15:64:16], 0.0, ["keep"])
-        else:
-            cp(T.tvr[:, 16 * cut:256], T.tv[:].indirect(T.t16[:, cut:16]), ["tv", "tvz", "t16"], ["tvs"])
-        copy_own([1, 2])
-        ts(T.thr[:], T.ct[:, 257:513:4], 0.5, A.subtract, ["ct2", "c6"], ["thr"], col(6), A.mult)
-        scan(T.gw[:], T.cw[:], T.tvr[:], A.mult, A.max, ["cw", "tvr", "tvs"], ["gw"])
-        scan(T.ct[:, 263:519:4], T.ct[:, 257:513:4], T.keep[:], A.add, A.mult, ["ct2", "keep"], ["ct3"])
-        pair_flags()
-        ts(T.inv[:], T.gw[:, 15:256:16], 2.0, A.mult, ["gw", "c6"], ["inv"], col(6), A.is_lt)
-        scan(T.ct[:, 7:263:4], T.ct[:, 1:257:4], T.keep[:], A.add, A.mult, ["ct0", "keep"], ["ct1"])
-        if t == 0:
-            ms(T.ct[:, 3:4], 0.0, ["ctz1"])
-        tt(T.kk[:, 0:16], T.inv[:], T.kt[:], A.mult, ["inv", "kt"], ["kk0"])
-        qz(T.qc[:], T.sc[:], T.ct[:, 0:512], ["ct0", "ct1", "ct2", "ct3", "ctz0", "ctz1"], ["qc"])
-        mmc(1, "t", 128, "c", 0, 128, ["qt2", "qc"])
-        qz(T.qn[:], T.sn[:], T.nt[:], ["nt0", "nt1"], ["qn"])
+        act(T.tf[:, 256:512], bank(0, 0, 256), ["B0"], ["tv"], AF.Sign)
+        if first:
+            act(T.cw8[:], T.dd[:, 80:96].indirect(lr), ["dd2", "lr"], ["cw8"])
+        ts(T.t16[:], bank(1, 112, 128), col(2), A.add, ["B1", "c2"], ["t16"])
+        if first:
+            ts(ls_, T.ji[:, 0:5], G16, A.add, ["ji", "rf"], ["ls"])
+        ts(T.sym[:], bank(5, 0, 128), 128.0, A.mult, ["B5"], ["sym"])
+        if first:
+            qz(T.qt[:, 128:384], T.st[:, 128:384], T.tt[:, 512:1536], ["t2a", "t2b", "t2c", "t3"], ["qt2"])
+            ts(lg, T.ji[:, 0:5], 16.0, A.mult, ["ji"], ["lg"], 15.0, A.add)
+        mmc(6, "t", 256, "o", 0, 256, ["qt2", "qo"])
+        mmc(7, "t", 128, "o", 0, 256, ["qt2", "qo"])
+        unpack_own([1, 3])
+        cut = 10
+        lin(T.tvr[:, 0:16 * cut], tv.indirect(T.t16[:, 0:cut]), -64.0, col(5), ["tv", "tvz", "t16", "c5"], ["tvr"])
+        if first:
+            lin(col(7), R2, 1.0 / 256, col(6), ["rf", "c5"], ["c7"])
+        act(T.ot[:, 0:1024:4], bank(6, 0, 256), ["B6"], ["ot0"], AF.Relu, -1.0, 1.0)
+        act(T.ot[:, 2:1024:4], bank(7, 0, 256), ["B7"], ["ot1"], AF.Relu, -1.0, 1.0)
+        ts(T.tvr[:, 16 * cut:256], tv.indirect(T.t16[:, cut:16]), -64.0, A.mult, ["tv", "tvz", "t16", "c5"], ["tvs"],
+           col(5), A.add)
+        tt(T.thr[:], T.sym[:].indirect(ls_), T.cc[:], A.subtract, ["sym", "ls", "cc"], ["thr"])
+        scan(T.gw[:], T.cw[:], T.tvr[:], A.add, A.min, ["cw", "tvr", "tvs"], ["gw"])
+        ts(T.ct[:, 321:640:4], T.thr[:], NEAR, A.add, ["thr", "ctz"], ["cu"], NEAR, A.is_equal)
+        tt(T.ct[:, 1:320:4], T.gw[:].indirect(lg), T.thr[:], A.is_equal, ["gw", "lg", "thr", "ctz"], ["ct"])
+        for s in range(4):
+            scan(T.ct[:, 27 + 4 * s:660:20], T.ct[:, 5 + 4 * s:640:20], T.keep[:], A.add, A.mult, ["keep", "ct", "cu"], ["ct%d" % s])
+        qz(T.qc[:], T.sc[:], T.ct[:, 0:640], ["ct", "cu", "ct0", "ct1", "ct2", "ct3"], ["qc"])
+        mmc(1, "t", 256, "c", 0, 160, ["qt2", "qc"])
+        qz(T.qn[:], T.sn[:], T.ot[:], ["ot0", "ot1"], ["qn"])
         mmc(0, "t", 0, "n", 0, 256, ["qt1", "qn"])
-        tt(T.x1[:, 0:64], bank(1, 0, 64), T.kk[:], A.add, ["B1", "kk0", "kk1"], ["x1a"])
-        if t == 0:
-            ts(col(7), rf(0), 15.0, A.is_equal, ["rf"], ["c7"], 1.0 / HOLD, A.max)
-        tt(T.x1[:, 64:96], T.x1[:, 0:32], T.x1[:, 32:64], A.max, ["x1a"], ["x1b"])
-        tt(T.x1[:, 96:112], T.x1[:, 64:80], T.x1[:, 80:96], A.max, ["x1b"], ["x1c"])
-        ts(T.p16[:], T.x1[:, 96:112], OWN, A.subtract, ["x1c"], ["p16"])
-        act(T.ft[:, 0:256], bank(0, 0, 256), ["B0"], ["ft"])
-        act(T.mate[:, 0:256], T.ft[:].indirect(T.t16[:]), ["ft", "ftz", "t16"], ["mate"])
-        copy_own([3])
+        copy_own([2, 1, 3])
+        scan(T.x1[:], bank(1, 0, 80), T.kd[:], A.min, A.add, ["B1", "kd", "kd1"], ["x1"])
+        cp(T.p16[:], T.x1[:, 4:80:5], ["x1"], ["p16"])
+        act(T.tf[:, 0:256], bank(0, 0, 256), ["B0"], ["ft"])
+        act(T.mate[:, 0:256], ft.indirect(T.t16[:]), ["ft", "tv", "t16"], ["mate"])
         cp(T.swin[:].indirect(T.p16[:]), T.iot[:], ["iot", "p16"], ["swin"])
-        scan(T.wa[:], T.cw[:, 0:128], T.swin[:, 0:128], A.mult, A.max, ["cw", "swin"], ["wa"])
-        ts(T.a16[:], T.wa[:, 15:128:16], col(7), A.mult, ["wa", "c7"], ["a16"])
-        for k in range(4):
-            act(T.ap[:, 128 * k:128 * k + 128], T.fp[:, FP * k:FP * k + C + 1].indirect(T.a16[:]),
-                ["fp%d" % k, "fpz", "a16"], ["ap%d" % k])
-        cp(T.brow[:], T.mate[:, 0:C + 1].indirect(T.a16[:]), ["mate", "matez", "a16"], ["brow"])
-        scan(T.wb[:], T.cw[:, 0:128], T.brow[:], A.mult, A.max, ["cw", "brow"], ["wb"])
-        ts(T.b16[:], T.wb[:, 15:128:16], col(7), A.mult, ["wb", "c7"], ["b16"])
-        for k in range(4):
-            tt(T.et[:, k:512:4], T.fp[:, FP * k:FP * k + C + 1].indirect(T.b16[:]), T.ap[:, 128 * k:128 * k + 128],
-               A.subtract, ["fp%d" % k, "fpz", "b16", "ap%d" % k], ["et%d" % k])
-        qz(T["qe%d" % t][:], T["se%d" % t][:], T.et[:], ["et0", "et1", "et2", "et3"], ["qe%d" % t])
+        scan(T.wa8[:], T.cw8[:, 0:128], T.swin[:, 0:128], A.add, A.min, ["cw8", "swin"], ["wa8"])
+        scan(T.wa[:], T.cw[:, 0:128], T.swin[:, 0:128], A.add, A.min, ["cw", "swin"], ["wa"])
+        ts(T.a8[:], T.wa8[:, 7:128:8], col(7), A.add, ["wa8", "c7"], ["a8"], 2.0, A.mult)
+        ts(T.a16[:], T.wa[:, 15:128:16], col(5), A.add, ["wa", "c5"], ["a16"])
+        fab = ((T.fa, ["fp0", "fp2", "faz"]), (T.fb, ["fp1", "fp3", "fbz"]))
+        for k in range(2):
+            act(T.ap[:, 256 * k:256 * k + 256], fab[k][0][:].indirect(T.a8[:]), fab[k][1] + ["a8"], ["ap%d" % k])
+        cp(T.brow[:], T.mate[:].indirect(T.a16[:]), ["mate", "matez", "a16"], ["brow"])
+        scan(T.wb8[:], T.cw8[:, 0:128], T.brow[:], A.add, A.min, ["cw8", "brow"], ["wb8"])
+        ts(T.b8[:], T.wb8[:, 7:128:8], col(7), A.add, ["wb8", "c7"], ["b8"], 2.0, A.mult)
+        for k in range(2):
+            tt(T.et[:, k:512:2], fab[k][0][:].indirect(T.b8[:]), T.ap[:, 256 * k:256 * k + 256], A.subtract,
+               fab[k][1] + ["b8", "ap%d" % k], ["et%d" % k])
+        qz(T["qe%d" % t][:], T["se%d" % t][:], T.et[:], ["et0", "et1"], ["qe%d" % t])
         dst = T.cores[(rank + 1 + t) % N]
         src = T.cores[(rank - 1 - t) % N]
         rid, pid = topo.addr(dst)[0], topo.addr(dst)[1]
@@ -359,39 +352,29 @@ def rank_program(g, core, T, topo):
         g.remote_dma(T["sl%d" % t][:], T["se%d" % t][:], T.sem["arr%d" % t], T.sem.sent, pid, rid, engines(core))
         count["sent"] = count.get("sent", 0) + 2 * bin(engines(core)).count("1")
         arrived = [("arr%d" % t, 2 * bin(engines(src)).count("1"))]
-        tt(T.x2[:, 0:64], bank(1, 64, 128), T.cc[:], A.add, ["B1", "cc"], ["x2a"])
+        scan(T.x2[:], bank(1, 80, 160), T.kd[:], A.min, A.add, ["B1", "kd"], ["x2"])
         if t < R - 1:
             ms(T.swin[:, 0:128], 256.0, ["swin"])
-        tt(T.x2[:, 64:96], T.x2[:, 0:32], T.x2[:, 32:64], A.max, ["x2a"], ["x2b"])
-        tt(T.x2[:, 96:112], T.x2[:, 64:80], T.x2[:, 80:96], A.max, ["x2b"], ["x2c"])
-        cp(T.xi[:, 0:16], T.x2[:, 96:112], ["x2c"], ["xi0"])
-        ts(T.xi[:, 16:32], T.xi[:, 0:16], 4 * M - 1, A.bitwise_and, ["xi0"], ["xi1"])
-        cp(T.k16[:], T.xi[:, 16:32], ["xi1"], ["k16"])
-        if t == 0:
+        cp(T.k16[:], T.x2[:, 4:80:5], ["x2"], ["k16"])
+        cp(T.tkb[:], T.m128[:].indirect(T.k16[:]), ["m0", "m1", "m2", "m3", "k16"], ["tk"])
+        if first:
             qz(T.qv[:], T.sv[:], T.vt[:], ["vt"], ["qv"])
-        order("V", ["k16", "fp0", "fp1", "fp2", "fp3", "B2", "B3", "B4", "B5"], (), ())
-        order("A", ["k16"], (), ())
+        scan(T.wk[:], T.cw8[:], T.tkb[:], A.add, A.min, ["cw8", "tk"], ["wk"])
+        ts(T.k8[:], T.wk[:, 7:256:8], col(7), A.add, ["wk", "c7"], ["k8"], 2.0, A.mult)
+        order("V", ["k8", "fp0", "fp1", "fp2", "fp3", "B2", "B3", "B4", "B5"], (), ())
+        order("A", ["k8"], (), ())
         order("P", ["qw", "sw"], ["B0", "B1", "B6", "B7"], ())
         gb = [0, 1, 6, 7]
         for k in (0, 2, 1, 3):
             mmc(gb[k], "d", 128 * k, "l%d" % t, 0, 128, ["qd%d" % k], arrived if k == 0 else ())
-        for k in (0, 1):
-            cp(T.gp[:, 128 * k:128 * k + 128], bank(gb[k], 0, 128), ["B%d" % gb[k]], ["gp%d" % k])
-        for k in (2, 3):
-            act(T.gp[:, 128 * k:128 * k + 128], bank(gb[k], 0, 128), ["B%d" % gb[k]], ["gp%d" % k])
+        for k in (0, 2):
+            cp(plane(T.ga, T.gb, k, 128), bank(gb[k], 0, 128), ["B%d" % gb[k]], ["gp%d" % k])
+        for k in (1, 3):
+            act(plane(T.ga, T.gb, k, 128), bank(gb[k], 0, 128), ["B%d" % gb[k]], ["gp%d" % k])
         rb = [gb, [2, 3, 4, 5]]
-        for k in range(4):
-            act(T.zg[:, 128 * k:128 * k + 128], T.gp[:, 128 * k:128 * k + 128].indirect(T.k16[:, 8:16]),
-                ["gp%d" % k, "k16"], ["zg%d" % k])
-
-        def zsum(h, k):
-            zo = T.zt[:, 512 * h + k:512 * h + 512:4]
-            if h == 0:
-                tt(zo, T.gp[:, 128 * k:128 * k + 128].indirect(T.k16[:, 0:8]), T.fp[:, FP * k:FP * k + 128], A.add,
-                   ["gp%d" % k, "k16", "fp%d" % k] + (["gp3"] if k == 2 else []), ["z%d%d" % (h, k)])
-            else:
-                tt(zo, bank(2 + k, 128, 256), T.zg[:, 128 * k:128 * k + 128], A.add,
-                   ["B%d" % (2 + k), "zg%d" % k] + (["zg2"] if k == 0 else []), ["z%d%d" % (h, k)])
+        gab = (T.ga, T.gb)
+        for k in range(2):
+            act(T.zg[:, 256 * k:256 * k + 256], gab[k][:].indirect(T.k8[:, 16:32]), ["gp%d" % k, "gp%d" % (k + 2), "k8"], ["zg%d" % k])
 
         def layer(h):
             qz(T.qz[:, 128 * h:128 * h + 128], T.sz[:, 128 * h:128 * h + 128], T.zt[:, 512 * h:512 * h + 512],
@@ -416,11 +399,13 @@ def rank_program(g, core, T, topo):
             for k in range(len(qs)):
                 dma(qs[k], T.osc[4 * k:4 * k + 4, :], T.sx[32 * k:32 * k + 4, :], ["qx0", "qx1"])
 
-        for k in range(4):
-            zsum(0, k)
+        for k in range(2):
+            tt(T.zt[:, k:512:2], gab[k][:].indirect(T.k8[:, 0:16]), fab[k][0][:, 0:256], A.add,
+               ["gp%d" % k, "gp%d" % (k + 2), "k8"] + fab[k][1], ["z0%d" % k, "z0%d" % (k + 2)])
         layer(0)
-        for k in range(4):
-            zsum(1, k)
+        for k in (0, 2, 1, 3):
+            tt(T.zt[:, 512 + k:1024:4], bank(2 + k, 128, 256), T.zg[:, 256 * (k % 2) + k // 2:256 * (k % 2) + 256:2], A.add,
+               ["B%d" % (2 + k), "zg%d" % (k % 2)], ["z1%d" % k])
         layer(1)
         add(0, 0)
         add(0, 1)
@@ -439,8 +424,9 @@ def rank_program(g, core, T, topo):
             dma("S", T.y[:, 128:256], T.yo[:, 128:256], ["yo1"])
         else:
             scores(0)
+            act(T.sg[:, 0:44], bank(0, 0, 44), ["B0"], ["sg"], AF.Sign)
+            act(T.hv[:, 0:44], T.sg[:, 0:44], ["sg"], ["bits0"], AF.Relu)
             add(1, 1)
-            signs(0)
             newx(1)
 
     for s, n in sorted(count.items()):

@@ -1,25 +1,26 @@
 from concourse.mybir import dt, AluOpType, AxisListType, ActivationFunctionType
 
 N, C, M, R = 8, 256, 32, 3
-X4, U8, BF, F32, I32, U16 = "float8_e4m3fn_x4", "uint8", "bfloat16", "float32", "int32", "uint16"
+X4, U8, BF, F16, F32, I32, U16 = "float8_e4m3fn_x4", "uint8", "bfloat16", "float16", "float32", "int32", "uint16"
 OWN = 2048.0
 HOLD = 256.0
-DUMP = 4 * C + 4
-SWW = 1408
-NEAR = 1.5 * 2.0 ** 31
+STEP = 2.0 * C
+NEAR = 1.5 * 2.0 ** 23
+SCANS = 7
 
 SCRATCH = {"ps": ("psum", [128, 4096], F32)}
 for _d, _l in (
-    (BF, "xt:1024 ut:512 vt:512 xn:1024 zt:1024 et:512 tt:1536 la:516 iot:256 dd:96 cw:256 cw8:256 hd:48 gri:128 keep:32 "
-         "sg:48 hv:208 ot:1024 ct:664 cc:80 tf:640 tvr:256 mate:272 gw:256 sym:128 thr:80 "
-         "swin:%d wa:128 wa8:128 wb8:128 brow:128 fa:528 fb:528 ap:512 ga:256 gb:256 zg:512 m128:1024 tkb:256 wk:256" % SWW),
-    (F32, "rf:52 col:16 sm8:8 lf:32 kd:80 x1:80 x2:80 rl:1024 yo:256"),
-    (I32, "rint:52 ji:6"),
-    (U16, "off:64 t16:16 p16:16 k16:16 a16:8 a8:16 b8:16 k8:32"),
+    (BF, "xt:1024 ut:512 vt:512 xn:1024 zt:1024 et:512 tt:1536 la:528 iot:256 dd:96 cw:128 cw8:256 half:8 gri:128 "
+         "sg:128 bits:16 hv:16 ot:1024 ct:528 tf:640 mask:256 fl:256 cnt:256 junk:256 mate:272 "
+         "brow:128 wb8:128 fa:528 fb:528 ap:512 ga:256 gb:256 zg:512 m128:1024 tkb:256 wk:256"),
+    (F16, "ramp:%d th:%d" % (C * SCANS, C * SCANS)),
+    (F32, "rf:44 col:16 sm8:8 gw:256 rr:16 fr:16 back:8 ya:8 kd:64 x2:64 rl:1024 yo:256"),
+    (I32, "rint:44"),
+    (U16, "lr:8 t16:16 k16:16 a16:8 a0:8 a1:8 b8:16 k8:32"),
 ):
     for _e in _l.split():
         SCRATCH[_e.split(":")[0]] = ("sbuf", [128, int(_e.split(":")[1])], _d)
-for _e in "x:256 z:256 u:128 up:128 v:128 w:512 t:384 d:512 o:256 y:160 n:256 c:160 e0:128 e1:128 e2:128 l0:128 l1:128 l2:128".split():
+for _e in "x:256 z:256 u:128 v:128 w:512 t:384 d:512 o:256 b:256 n:256 c:128 e0:128 e1:128 e2:128 l0:128 l1:128 l2:128".split():
     SCRATCH["q" + _e.split(":")[0]] = ("sbuf", [128, int(_e.split(":")[1])], X4)
     SCRATCH["s" + _e.split(":")[0]] = ("sbuf", [128, int(_e.split(":")[1])], U8)
 
@@ -97,8 +98,8 @@ def rank_program(g, core, T, topo):
     def ms(out, c, w):
         op("V", lambda: V.memset(out, c), (), w)
 
-    def scan(out, d0, d1, o0, o1, r, w):
-        op("V", lambda: V.tensor_tensor_scan(out, d0, d1, 0.0, o0, o1), r, w)
+    def scan(out, d0, d1, o0, o1, r, w, init=0.0):
+        op("V", lambda: V.tensor_tensor_scan(out, d0, d1, init, o0, o1), r, w)
 
     def qz(q, s, t, r, w):
         op("V", lambda: V.quantize_mx(q, s, t), r, w)
@@ -123,22 +124,12 @@ def rank_program(g, core, T, topo):
     def sel(out, in_, pat, cmp, fill, cm, r, w, base=0):
         op("G", lambda: g.affine_select(out, in_, pat, cmp, fill, base, cm), r, w)
 
-    def bank(b, lo, hi):
-        return T.ps[:, 512 * b + lo:512 * b + hi]
+    def bank(b, lo, hi, step=1):
+        return T.ps[:, 512 * b + lo:512 * b + hi:step]
 
-    def mmc(b, lname, la, rname, ra, rb, r, ext=(), shift=0):
-        lq, ls = T["q" + lname][:, la:la + 128], T["s" + lname][:, la:la + 128]
-
-        def mm(o, start, stop):
-            return g.tensor.matmul_mx(bank(b, 0, rb - ra), lq, ls, T["q" + rname][:, ra + o:rb + o],
-                                      T["s" + rname][:, ra + o:rb + o], start, stop)
-
-        def call():
-            if shift:
-                mm(shift, True, False).then_inc(T.sem.cP, 1)
-                count["cP"] += 1
-            return mm(0, not shift, True)
-        op("P", call, r, ["B%d" % b], ext)
+    def mmc(b, lname, la, rname, ra, rb, r, ext=()):
+        op("P", lambda: g.tensor.matmul_mx(bank(b, 0, rb - ra), T["q" + lname][:, la:la + 128], T["s" + lname][:, la:la + 128],
+                                           T["q" + rname][:, ra:rb], T["s" + rname][:, ra:rb], True, True), r, ["B%d" % b], ext)
 
     def engines(c):
         i, m = T.rank_of(c), -1
@@ -146,202 +137,243 @@ def rank_program(g, core, T, topo):
             m &= topo.mask(c, T.cores[(i + 1 + t) % N])
         return m
 
+    def quant(name, src, lo, hi, r, w):
+        qz(T["q" + name][:, lo:hi], T["s" + name][:, lo:hi], src[:, 4 * lo:4 * hi], r, w)
+
     def unpackers(bs):
         for b in bs:
             qz(T.qd[:, 128 * b:128 * b + 128], T.sd[:, 128 * b:128 * b + 128], T.la[:, 3 - b:515 - b], ["la"], ["qd%d" % b])
 
+    def ramps(cs):
+        for c in cs:
+            lin(T.ramp[:, C * c:C * c + C], T.iot[:], 2.0, -STEP * (c + 1), ["iot"], ["ramp%d" % c])
+
     col = lambda i: T.col[:, i:i + 1]
-    R16, G16, R8, K64, R2 = [T.rf[:, i:i + 1] for i in (0, 16, 17, 18, 19)]
-    ones = T.tt[:, 513:1024:2]
+    K16, R2, G16, P16, R16 = [T.rf[:, i:i + 1] for i in range(5)]
+    ones = T.tt[:, 0:1024:4]
     ft, tv = T.tf[:, 0:384], T.tf[:, 256:640]
-    lu, lr, ly, ls_, lg = [T.off[:, a:b] for a, b in ((0, 8), (4, 20), (20, 30), (30, 35), (36, 41))]
+    POW, H16, H8, PAR, E0, W3, ACOL, BCOL, WCOL, CNT0, TCOL = range(11)
+    cts = ["cf%d" % s for s in range(4)] + ["cr%d" % s for s in range(4)]
 
     dma("S", T.xt[:, 0:512], T.x[:, 0:512], (), ["X0"])
     dma("A", T.ut[:], T.u[:], (), ["ut"])
     dma("S", T.xt[:, 512:1024], T.x[:, 512:1024], (), ["X1"])
 
-    iota(T.rint[:, 0:16], [[0, 16]], 0, 16, ["ri0"], False)
-    for i, m in ((16, 1), (17, 32), (18, 64), (19, 128)):
-        iota(T.rint[:, i:i + 1], [[0, 1]], 0, m, ["ri%d" % i], False)
-    iota(T.rint[:, 20:36], [[16, 16]], 2048, -16, ["ri20"], False)
-    iota(T.rint[:, 36:52], [[0, 2], [32, 8]], 2064, -16, ["ri36"], False)
-    iota(T.lf[:, 0:2], [[256, 2]], 12, 0, ["lf0"])
-    iota(T.iot[:], [[1, 256]], 0, 0, ["iot"])
-    ms(T.tt[:, 0:1024], 1.0, ["ones", "t1b", "t1c", "t3"])
-    ms(T.ot[:, 1:1024:2], 0.0, ["otz"])
-    ms(T.ct[:], 0.0, ["ct", "cu", "ctz"])
-    lin(T.la[:], T.tt[:, 0:516], 0.0, None, ["ones", "t1b", "t1c", "t3"], ["la"])
-    lin(T.tt[:, 3:512:4], T.tt[:, 512:640], 0.0, None, ["ones", "t3"], ["t1c"])
-    ts(T.rint[:, 0:36], T.rint[:, 0:36], 240, A.bitwise_and, ["ri0", "ri16", "ri17", "ri18", "ri19"], ["ri20"])
-    ts(T.rint[:, 36:52], T.rint[:, 36:52], 1, A.arith_shift_right, [], ["ri36"], 112, A.bitwise_and)
-    cp(T.rf[:], T.rint[:], ["ri20", "ri36"], ["rf"])
-    iota(T.hv[:, 0:112], [[0, 112]], 0, 0, ["bits0", "bits1", "hvz"])
-    iota(col(12), [[0, 1]], 0, 1, ["c12"])
-    iota(T.hd[:], [[0, 48]], 2, 0, ["hd", "hd1"])
+    iota(T.rint[:, 0:12], [[0, 12]], 0, 16, ["ri0", "ri1", "ri2", "ri4"], False)
+    iota(T.rint[:, 12:28], [[16, 16]], 2048, -16, ["ri12"], False)
+    iota(T.rint[:, 28:44], [[0, 2], [32, 8]], 2064, -16, ["ri28"], False)
     iota(T.gri[:], [[16, 8], [0, 16]], 0, 0, ["gri"])
-    iota(T.hd[:, 1:32:4], [[0, 8]], 0, 0, ["hd"])
-    iota(T.hd[:, 36:41:4], [[0, 2]], 0, 0, ["hd1"])
-    sel(T.tt[:, 1024:1536:2], ones, [[1, 128], [-1000, 2]], A.is_ge, 0.0, -1, ["ones"], ["t2a"])
-    sel(T.tt[:, 514:1024:4], T.tt[:, 513:1024:4], [[1, 128]], A.is_ge, 0.0, -1, ["ones"], ["t3"])
-    ts(col(0), K64, -0.3125, A.mult, ["rf"], ["c0"], R16, A.add)
-    ts(lr, T.rf[:, 0:16], 0.0625, A.mult, ["rf"], ["lr"])
-    ts(T.off[:, 2:4], T.rf[:, 17:19], -0.5, A.mult, ["rf"], ["lu2"], 112.0, A.add)
-    ts(T.off[:, 0:2], T.lf[:, 0:2], col(0), A.add, ["lf0", "c0"], ["lu0"], 0.25, A.mult)
-    act(T.dd[:, 0:32], T.rf[:, 20:52], ["rf"], ["dd0"], AF.Relu, -0.375 * HOLD, 6.0 * HOLD)
-    act(T.dd[:, 32:64], T.rf[:, 20:52], ["rf"], ["dd1"], AF.Relu, -HOLD / 16, 2.0 * HOLD)
-    lin(col(3), R16, 0.375, 19.0, ["rf"], ["c3"])
-    lin(col(11), R16, 0.0125, -0.4, ["rf"], ["c11"])
-    lin(col(4), R8, -0.1875, col(3), ["rf", "c3"], ["c4"])
-    ts(col(10), R8, 0.5, A.mult, ["rf"], ["c10"], G16, A.is_equal)
-    qz(T.qu[:], T.su[:], T.ut[:], ["ut"], ["qu"])
-    tt(T.dd[:, 64:96], T.dd[:, 0:32], T.dd[:, 32:64], A.subtract, ["dd0", "dd1"], ["dd2"])
-    act(T.sup[:], T.su[:].indirect(lu), ["qu", "lu0", "lu2", "lr"], ["sup"])
-    op("V", lambda: V.tensor_copy(T.qup[:].bitcast(dt.uint32), T.qu[:].bitcast(dt.uint32).indirect(lu)),
-       ["qu", "lu0", "lu2", "lr"], ["qup"])
-    act(T.cw[:], T.dd[:, 64:80].indirect(lr), ["dd2", "lr"], ["cw"])
-    lin(T.lf[:, 10:18], T.iot[:, 0:8], 4.0, col(4), ["iot", "c4"], ["lf10"])
-    lin(T.lf[:, 18:20], T.iot[:, 9:12:2], 4.0, col(4), ["iot", "c4"], ["lf18"])
-    act(T.tt[:, 1:512:4], T.cw[:, 0:128], ["cw"], ["t1b"], AF.Relu, 0.25 / HOLD)
-    lin(T.lf[:, 20:26], T.iot[:, 0:6], 3.2, col(11), ["iot", "c11"], ["lf20"])
-
-    def quant_x(src, h):
-        qz(T.qx[:, 128 * h:128 * h + 128], T.sx[:, 128 * h:128 * h + 128], src[:, 512 * h:512 * h + 512],
-           ["X%d" % h], ["qx%d" % h])
-
-    def scores(h):
-        mmc(h, "x", 128 * h, "up", 0, 128, ["qx%d" % h, "qup", "sup"])
-
-    def signs(h):
-        ts(T.hv[:, 48 * h:48 * h + 44], bank(h, 0, 44), 0.0, A.is_gt, ["B%d" % h], ["bits%d" % h])
-
-    def horner(h):
-        scan(T.hv[:, 48 * h + 112:48 * h + 160], T.hd[:], T.hv[:, 48 * h:48 * h + 48], A.mult, A.add,
-             ["hd", "hd1", "bits%d" % h], ["hv%d" % h])
-
-    def onehot(h):
-        ts(T.ot[:, 2 * h:1024:4], T.iot[:], T.hv[:, 48 * h + 159:48 * h + 160], A.subtract,
-           ["iot", "hv%d" % h], ["ot%d" % h], T.hv[:, 48 * h + 151:48 * h + 152], A.is_equal)
-
-    def unpack_own(ks):
-        for k in ks:
-            mmc(2 + k, "d", 128 * k, "x", 0, 256, ["qd%d" % k, "qx0", "qx1"])
-
-    def plane(a, b, k, n):
-        return (a, b)[k % 2][:, k // 2:2 * n:2]
-
-    def copy_own(ks):
-        for k in ks:
-            act(plane(T.fa, T.fb, k, C), bank(2 + k, 0, 256), ["B%d" % (2 + k)], ["fp%d" % k])
-
-    quant_x(T.xt, 0)
-    scores(0)
-    quant_x(T.xt, 1)
-    dma("S", T.qw[:].bitcast(dt.uint8), T.wc[:], ["X1"], ["qw"])
-    dma("S", T.sw[:], T.ws[:], (), ["sw"])
-    dma("S", T.vt[:], T.v[:], (), ["vt"])
+    iota(T.tt[:, 2:1024:4], [[-1, 2], [0, 128]], 1, 0, ["t3"])
+    ms(T.ct[:], 0.0, cts)
+    ms(ones, 1.0, ["ones"])
+    sel(T.tt[:, 1024:1536:2], ones, [[2, 128], [-128, 2]], A.is_ge, 0.0, -1, ["ones"], ["t2a"], 1)
+    sel(T.tt[:, 1024:1536:2], T.tt[:, 1024:1536:2], [[-2, 128], [128, 2]], A.is_gt, 2.0, 1, [], ["t2a"])
+    ts(T.rint[:, 0:1], T.rint[:, 0:1], 48, A.bitwise_and, [], ["ri0"])
+    scan(T.iot[:], ones, ones, A.mult, A.add, ["ones"], ["iot"], -1.0)
+    ts(T.rint[:, 1:2], T.rint[:, 1:2], 16, A.bitwise_and, [], ["ri1"])
+    ts(T.rint[:, 2:3], T.rint[:, 2:3], 4, A.arith_shift_right, [], ["ri2"], 240, A.bitwise_and)
+    ts(T.rint[:, 4:28], T.rint[:, 4:28], 240, A.bitwise_and, [], ["ri4", "ri12"])
+    ts(T.rint[:, 28:44], T.rint[:, 28:44], 1, A.arith_shift_right, [], ["ri28"], 112, A.bitwise_and)
+    lin(T.ot[:, 1:1024:2], T.ct[:, 0:512], 0.0, None, cts, ["otz"])
+    dma("S", T.la[:], T.ct[:], cts, ["la"])
+    ms(T.tt[:, 3:1024:4], 0.0, ["tz"])
+    cp(T.rf[:], T.rint[:], ["ri0", "ri1", "ri2", "ri4", "ri12", "ri28"], ["rf"])
+    ms(T.half[:], 0.5, ["half"])
+    ts(T.sm8[:], T.iot[:, 0:128:16], G16, A.is_lt, ["iot", "rf"], ["s8"], 1.0, A.add)
+    ts(col(E0), R16, 0.0, A.is_equal, ["rf"], ["e0"], 1.0 / 32, A.mult)
+    act(col(W3), R16, ["rf"], ["w3"], AF.Relu, -1.0 / 512, 3.0 / 32)
+    act(T.dd[:, 0:32], T.rf[:, 12:44], ["rf"], ["dd0"], AF.Relu, -0.375 * HOLD, 6.0 * HOLD)
+    act(T.dd[:, 32:64], T.rf[:, 12:44], ["rf"], ["dd1"], AF.Relu, -HOLD / 16, 2.0 * HOLD)
+    op("V", lambda: V.tensor_reduce(col(POW), T.sm8[:], AX, A.mult, negate=True), ["s8"], ["pow"])
     ts(T.tt[:, 1027:1536:4], T.gri[:], G16, A.is_equal, ["gri", "rf"], ["t2c"], 4.0, A.mult)
-    ts(T.la[:, 3:515:4], T.iot[:, 0:128], col(12), A.is_equal, ["iot", "c12"], ["la"])
-    signs(0)
-    unpackers([0])
+    ts(col(WCOL), col(E0), col(W3), A.add, ["e0", "w3"], ["wcol"], 128.0, A.mult)
+    ts(col(BCOL), col(E0), -3.0, A.mult, ["e0", "w3"], ["bcol"], col(W3), A.add)
+    ts(col(ACOL), col(E0), col(POW), A.mult, ["e0", "pow"], ["acol"], -32.0, A.mult)
+    lin(T.tt[:, 513:1024:4], T.tt[:, 1027:1536:4], col(WCOL), None, ["t2c", "wcol"], ["k2"])
+    lin(T.tt[:, 1:512:4], T.tt[:, 1027:1536:4], col(BCOL), col(ACOL), ["t2c", "bcol", "acol"], ["k1"])
+    ts(T.lr[:], T.rf[:, 4:12], 0.0625, A.mult, ["rf"], ["lr"])
+    tt(T.dd[:, 64:96], T.dd[:, 0:32], T.dd[:, 32:64], A.subtract, ["dd0", "dd1"], ["dd2"])
+    qz(T.qu[:], T.su[:], T.ut[:], ["ut"], ["qu"])
+    act(T.cw[:], T.dd[:, 64:80].indirect(T.lr[:]), ["dd2", "lr"], ["cw"])
+    ramps([0, 1])
     sel(T.tt[:, 1025:1536:4], T.tt[:, 1027:1536:4], [[1, 128]], A.is_gt, 0.0, -1, ["t2c"], ["t2b"])
-    iota(T.tf[:, 512:640], [[0, 128]], 0, 0, ["tvz"])
     sel(T.tt[:, 1025:1536:4], T.tt[:, 1025:1536:4], [[1, 128]], A.not_equal, -OWN, -1, ["t2b"], ["t2b"])
-    iota(T.cc[:], [[0, 16], [256, 5]], -192, 0, ["cc"])
-    sel(T.keep[:], T.tt[:, 513:577:2], [[1, 32]], A.not_equal, 0.0, 0, ["ones"], ["keep"], -15)
-    iota(T.cc[:, 0:80:5], [[0, 16]], 8192, 0, ["cc"])
-    iota(T.kd[:], [[0, 80]], -1, 0, ["kd", "kd1"])
-    iota(T.swin[:, 0:128], [[0, 128]], C, 0, ["swin"])
-    iota(T.kd[:, 0:80:5], [[16, 16]], DUMP - int(OWN), 1, ["kd"])
-    iota(T.kd[:, 4:80:5], [[0, 16]], int(OWN) + 3, 0, ["kd1"])
-    iota(T.m128[:, 0:256], [[0, 2], [1, 128]], 0, 0, ["m0"])
+    iota(T.tf[:, 512:640], [[0, 128]], 0, 0, ["tvz"])
+    iota(T.back[:], [[int(STEP), 8]], int(STEP), 0, ["back"])
     iota(T.mate[:, 256:272], [[0, 16]], C, 0, ["matez"])
     iota(T.fa[:, 512:528], [[0, 16]], 0, 0, ["faz"])
     iota(T.fb[:, 512:528], [[0, 16]], 0, 0, ["fbz"])
+    for k in range(2):
+        iota(T.m128[:, 128 * k:128 * k + 128], [[4, 4], [16, 8], [1, 4]], 0, 0, ["m0"])
+    iota(T.kd[:], [[0, 64]], -1, 0, ["kd"])
+    iota(T.kd[:, 3:64:4], [[0, 16]], int(OWN) + 3, 0, ["kd"])
+
+    def scores(h):
+        mmc(6 * h, "x", 128 * h, "u", 0, 128, ["qx%d" % h, "qu"])
+        mmc(6 * h + 1, "u", 0, "x", 128 * h, 128 * h + 128, ["qx%d" % h, "qu"])
+
+    def signs(h):
+        ts(T.bits[:, 8 * h:8 * h + 8], bank(6 * h, 0, 128, 16), 0.0, A.is_gt, ["B%d" % (6 * h)], ["bits%d" % h])
+
+    def signrow(h):
+        ts(T.ct[:, 1:512:4], bank(6 * h + 1, 0, 128), 0.0, A.is_gt, ["B%d" % (6 * h + 1)], cts[:4])
+
+    def rows(h):
+        qz(T.qb[:, 128 * h:128 * h + 128], T.sb[:, 128 * h:128 * h + 128], T.ct[:, 0:512], cts, ["qb%d" % h])
+
+    def turn(h, k):
+        mmc(6 * h + k, "t", 128 * k, "b", 128 * h, 128 * h + 128, ["qt%d" % k, "qb%d" % h])
+
+    def wrap(h):
+        v = slice(128 * h, 128 * h + 128)
+        scan(T.gw[:, v], T.cw[:], bank(6 * h, 0, 128), A.add, A.min, ["cw", "B%d" % (6 * h)], ["gw%d" % h])
+
+    def mask(h):
+        ts(T.mask[:, 128 * h:128 * h + 128], bank(6 * h + 1, 0, 128), K16, A.is_equal, ["B%d" % (6 * h + 1), "rf"],
+           ["mask%d" % h], -STEP, A.mult)
+
+    def word(h):
+        scan(T.hv[:, 8 * h:8 * h + 8], T.half[:], T.bits[:, 8 * h:8 * h + 8], A.mult, A.add, ["half", "bits%d" % h], ["hv%d" % h])
+
+    def onehot(h):
+        ts(T.ot[:, 2 * h:1024:4], T.iot[:], 1.0 / 128, A.mult, ["iot", "hv%d" % h], ["ot%d" % h],
+           T.hv[:, 8 * h + 7:8 * h + 8], A.is_equal)
+
+    def unpack_own(h, ks):
+        for k in ks:
+            mmc(2 + k, "d", 128 * k, "x", 128 * h, 128 * h + 128, ["qd%d" % k, "qx%d" % h])
+
+    def plane(a, b, k, lo, hi):
+        return (a, b)[k % 2][:, 2 * lo + k // 2:2 * hi:2]
+
+    def copy_own(h, ks):
+        for k in ks:
+            act(plane(T.fa, T.fb, k, 128 * h, 128 * h + 128), bank(2 + k, 0, 128), ["B%d" % (2 + k)], ["f%d%d" % (h, k)])
+
+    def flags(s):
+        ts(T.ct[:, 1 + 4 * s:256:16], T.fr[:], s / 8.0, A.is_equal, ["fr"], ["cf%d" % s])
+
+    def running(s):
+        f = T.ct[:, 1 + 4 * s:256:16]
+        scan(T.ct[:, 19 + 4 * s:272:16], f, f, A.add, A.max, ["cf%d" % s], ["cr%d" % s])
+
+    quant("x", T.xt, 0, 128, ["X0"], ["qx0"])
+    scores(0)
+    quant("x", T.xt, 128, 256, ["X1"], ["qx1"])
+    dma("S", T.qw[:].bitcast(dt.uint8), T.wc[:], ["X1"], ["qw"])
+    dma("S", T.sw[:], T.ws[:], (), ["sw"])
+    dma("S", T.vt[:], T.v[:], (), ["vt"])
     for k in (1, 2, 3):
         dma("S", T.m128[:, 256 * k:256 * k + 256], T.m128[:, 0:256], ["m0"], ["m%d" % k])
+    quant("t", T.tt, 0, 256, ["k1", "k2", "t3", "tz", "ones"], ["qt0", "qt1"])
+    signs(0)
+    signrow(0)
 
-    hv = ["hv0", "hv1", "hvz"]
     for t in range(R):
         first = t == 0
+
+        def own(ks, whole=first):
+            if not whole:
+                unpack_own(1, ks)
+                copy_own(1, ks)
+            for k in ks if whole else ():
+                mmc(2 + k, "d", 128 * k, "x", 0, C, ["qd%d" % k, "qx0", "qx1"])
+                act(plane(T.fa, T.fb, k, 0, C), bank(2 + k, 0, C), ["B%d" % (2 + k)], ["f0%d" % k, "f1%d" % k])
+
         scores(1)
+        word(0)
+        rows(0)
+        turn(0, 0)
+        turn(0, 1)
         if not first:
-            unpack_own([0, 2])
-        horner(0)
+            own([3], True)
         signs(1)
         onehot(0)
-        horner(1)
+        if first:
+            ts(T.la[:, 3:515:4], T.iot[:, 0:128], 16.0, A.mult, ["iot", "rf"], ["la"], P16, A.is_equal)
+            ramps(range(2, SCANS))
+            act(T.cw8[:, 0:128], T.dd[:, 80:96].indirect(T.lr[:]), ["dd2", "lr"], ["cw8"])
+            dma("A", T.cw8[:, 128:256], T.cw8[:, 0:128], ["cw8"], ["cw8b"])
+        word(1)
+        signrow(1)
+        onehot(1)
+        rows(1)
+        turn(1, 0)
+        quant("o", T.ot, 0, 256, ["ot0", "ot1", "otz"], ["qo"])
+        mmc(2, "t", 0, "o", 0, 256, ["qt0", "qo"])
+        turn(1, 1)
+        if first:
+            ts(T.col[:, H16:H8 + 1], T.rf[:, 27:36:8], 0.0, A.is_gt, ["rf"], ["hold"], -HOLD, A.mult)
+        wrap(0)
+        if first:
+            quant("t", T.tt, 256, 384, ["t2a", "t2b", "t2c"], ["qt2"])
+        wrap(1)
+        if first:
+            ts(col(TCOL), col(H16), col(POW), A.add, ["hold", "pow"], ["tcol"], NEAR, A.add)
+            unpackers([0])
+        mask(0)
+        mmc(0, "t", 256, "o", 0, 256, ["qt2", "qo"])
+        act(T.tf[:, 256:512], bank(2, 0, 256), ["B2"], ["tv"], AF.Sign)
+        gw = ["gw0", "gw1"]
+        ts(T.t16[:], T.gw[:, 15:256:16], NEAR, A.add, gw + ["tcol"], ["t16"], col(TCOL), A.subtract)
+        if first:
+            ts(col(CNT0), R16, K16, A.subtract, ["rf"], ["cnt0"], 64.0, A.mult)
+        else:
+            ts(T.rr[:], T.gw[:, 15:256:16], NEAR, A.add, gw, ["rr"], NEAR, A.subtract)
+        mask(1)
         if first:
             unpackers([2])
-            unpack_own([0, 2])
-            ts(ly, T.lf[:, 10:20], col(10), A.mult, ["lf10", "lf18", "c10"], ["ly"])
-        act(T.ct[:, 1:640:4], T.hv[:, 96:208].indirect(ly), hv + ["ly"], ["ct", "cu"])
-        onehot(1)
+        else:
+            tt(T.fr[:], T.gw[:, 15:256:16], T.rr[:], A.subtract, gw + ["rr"], ["fr"])
+        act(T.ot[:, 0:1024:4], bank(0, 0, 256), ["B0"], ["ot0"], AF.Relu, -1.0, 2.0)
+        tt(T.fl[:], tv.indirect(T.t16[:]), T.mask[:], A.mult, ["tv", "tvz", "t16", "mask0", "mask1"], ["fl"])
+        own([0, 2] if first else [0, 2, 1])
+        quant("n", T.ot, 0, 256, ["ot0", "ot1"], ["qn"])
+        mmc(7, "t", 128, "n", 0, 256, ["qt1", "qn"])
+        scan(T.cnt[:], ones, T.fl[:], A.mult, A.add, ["ones", "fl", "cnt0"], ["cnt"], col(CNT0))
+        later = [lambda s=s: flags(s) for s in range(4)] + [lambda s=s: running(s) for s in range(4)]
         if first:
-            qz(T.qt[:, 0:128], T.st[:, 0:128], T.tt[:, 0:512], ["t1b", "t1c"], ["qt1"])
-        qz(T.qo[:], T.so[:], T.ot[:], ["ot0", "ot1", "otz"], ["qo"])
-        if first:
-            ts(T.sm8[:], T.iot[:, 0:128:16], G16, A.is_lt, ["iot", "rf"], ["s8"], 1.0, A.add)
-            unpackers([1])
-        qz(T.qy[:], T.sy[:], T.ct[:, 0:640], ["ct", "cu", "ct0", "ct1", "ct2", "ct3"], ["qy"])
-        mmc(0, "t", 0, "o", 0, 256, ["qt1", "qo"])
-        mmc(1, "t", 0, "y", 16, 144, ["qt1", "qy"], (), 16)
-        mmc(5, "t", 0, "y", 0, 128, ["qt1", "qy"])
-        if first:
-            op("V", lambda: V.tensor_reduce(col(2), T.sm8[:], AX, A.mult), ["s8"], ["c2"])
-            cp(T.ji[:], T.lf[:, 20:26], ["lf20"], ["ji"])
-            ts(T.col[:, 5:7], T.rf[:, 35:44:8], 0.0, A.is_gt, ["rf"], ["c5"], HOLD, A.mult)
-            unpackers([3])
-        copy_own([0])
-        act(T.tf[:, 256:512], bank(0, 0, 256), ["B0"], ["tv"], AF.Sign)
-        if first:
-            act(T.cw8[:], T.dd[:, 80:96].indirect(lr), ["dd2", "lr"], ["cw8"])
-        ts(T.t16[:], bank(1, 112, 128), col(2), A.add, ["B1", "c2"], ["t16"])
-        if first:
-            ts(ls_, T.ji[:, 0:5], G16, A.add, ["ji", "rf"], ["ls"])
-        ts(T.sym[:], bank(5, 0, 128), 128.0, A.mult, ["B5"], ["sym"])
-        if first:
-            qz(T.qt[:, 128:384], T.st[:, 128:384], T.tt[:, 512:1536], ["t2a", "t2b", "t2c", "t3"], ["qt2"])
-            ts(lg, T.ji[:, 0:5], 16.0, A.mult, ["ji"], ["lg"], 15.0, A.add)
-        mmc(6, "t", 256, "o", 0, 256, ["qt2", "qo"])
-        mmc(7, "t", 128, "o", 0, 256, ["qt2", "qo"])
-        unpack_own([1, 3])
-        cut = 10
-        lin(T.tvr[:, 0:16 * cut], tv.indirect(T.t16[:, 0:cut]), -64.0, col(5), ["tv", "tvz", "t16", "c5"], ["tvr"])
-        if first:
-            lin(col(7), R2, 1.0 / 256, col(6), ["rf", "c5"], ["c7"])
-        act(T.ot[:, 0:1024:4], bank(6, 0, 256), ["B6"], ["ot0"], AF.Relu, -1.0, 1.0)
-        act(T.ot[:, 2:1024:4], bank(7, 0, 256), ["B7"], ["ot1"], AF.Relu, -1.0, 1.0)
-        ts(T.tvr[:, 16 * cut:256], tv.indirect(T.t16[:, cut:16]), -64.0, A.mult, ["tv", "tvz", "t16", "c5"], ["tvs"],
-           col(5), A.add)
-        tt(T.thr[:], T.sym[:].indirect(ls_), T.cc[:], A.subtract, ["sym", "ls", "cc"], ["thr"])
-        scan(T.gw[:], T.cw[:], T.tvr[:], A.add, A.min, ["cw", "tvr", "tvs"], ["gw"])
-        ts(T.ct[:, 321:640:4], T.thr[:], NEAR, A.add, ["thr", "ctz"], ["cu"], NEAR, A.is_equal)
-        tt(T.ct[:, 1:320:4], T.gw[:].indirect(lg), T.thr[:], A.is_equal, ["gw", "lg", "thr", "ctz"], ["ct"])
-        for s in range(4):
-            scan(T.ct[:, 27 + 4 * s:660:20], T.ct[:, 5 + 4 * s:640:20], T.keep[:], A.add, A.mult, ["keep", "ct", "cu"], ["ct%d" % s])
-        qz(T.qc[:], T.sc[:], T.ct[:, 0:640], ["ct", "cu", "ct0", "ct1", "ct2", "ct3"], ["qc"])
-        mmc(1, "t", 256, "c", 0, 160, ["qt2", "qc"])
-        qz(T.qn[:], T.sn[:], T.ot[:], ["ot0", "ot1"], ["qn"])
-        mmc(0, "t", 0, "n", 0, 256, ["qt1", "qn"])
-        copy_own([2, 1, 3])
-        scan(T.x1[:], bank(1, 0, 80), T.kd[:], A.min, A.add, ["B1", "kd", "kd1"], ["x1"])
-        cp(T.p16[:], T.x1[:, 4:80:5], ["x1"], ["p16"])
-        act(T.tf[:, 0:256], bank(0, 0, 256), ["B0"], ["ft"])
+            unpackers([1, 3])
+            later = [lambda: ts(col(PAR), R2, 1.0 / 32, A.mult, ["rf", "hold"], ["par"], col(H8), A.subtract),
+                     lambda: ts(T.rr[:], T.gw[:, 15:256:16], NEAR, A.add, gw, ["rr"], NEAR, A.subtract),
+                     lambda: tt(T.fr[:], T.gw[:, 15:256:16], T.rr[:], A.subtract, gw + ["rr"], ["fr"])] + later
+        else:
+            later.pop(0)()
+        for c in range(8):
+            if c < SCANS:
+                scan(T.th[:, C * c:C * c + C], T.ramp[:, C * c:C * c + C], T.cnt[:], A.min, A.max,
+                     ["ramp%d" % c, "cnt"], ["th%d" % c])
+            else:
+                op("A", lambda: S_.activation(T.junk[:], T.cnt[:], AF.Sign, bias=STEP * (c + 0.5), scale=1.0,
+                                              accum_out=T.ya[:, c:c + 1]), ["cnt"], ["junk", "yb%d" % c])
+            if c == SCANS:
+                act(T.tf[:, 0:256], bank(7, 0, 256), ["B7"], ["ft"])
+        yb = ["yb%d" % c for c in range(SCANS, 8)]
+        lin(T.ya[:, SCANS:8], T.ya[:, SCANS:8], 1.0, float(C), [], yb)
         act(T.mate[:, 0:256], ft.indirect(T.t16[:]), ["ft", "tv", "t16"], ["mate"])
-        cp(T.swin[:].indirect(T.p16[:]), T.iot[:], ["iot", "p16"], ["swin"])
-        scan(T.wa8[:], T.cw8[:, 0:128], T.swin[:, 0:128], A.add, A.min, ["cw8", "swin"], ["wa8"])
-        scan(T.wa[:], T.cw[:, 0:128], T.swin[:, 0:128], A.add, A.min, ["cw", "swin"], ["wa"])
-        ts(T.a8[:], T.wa8[:, 7:128:8], col(7), A.add, ["wa8", "c7"], ["a8"], 2.0, A.mult)
-        ts(T.a16[:], T.wa[:, 15:128:16], col(5), A.add, ["wa", "c5"], ["a16"])
-        fab = ((T.fa, ["fp0", "fp2", "faz"]), (T.fb, ["fp1", "fp3", "fbz"]))
-        for k in range(2):
-            act(T.ap[:, 256 * k:256 * k + 256], fab[k][0][:].indirect(T.a8[:]), fab[k][1] + ["a8"], ["ap%d" % k])
+        if first:
+            own([1, 3])
+        later.pop(0)()
+        tt(T.ya[:, 0:SCANS], T.th[:, C - 1:C * SCANS:C], T.back[:, 0:SCANS], A.add,
+           ["th%d" % c for c in range(SCANS)] + ["back"], ["ya"])
+        later.pop(0)()
+        ts(T.a16[:], T.ya[:], STEP, A.min, ["ya"] + yb, ["a16"], 0.5, A.mult)
+        ts(T.a0[:], T.ya[:], STEP, A.min, ["ya"] + yb, ["a0"])
+        ts(T.a1[:], T.ya[:], STEP, A.min, ["ya"] + yb, ["a1"], 1.0, A.add)
+        fab = ((T.fa, ["f00", "f02", "f10", "f12", "faz"]), (T.fb, ["f01", "f03", "f11", "f13", "fbz"]))
+        for k in (0, 2, 1, 3):
+            act(T.ap[:, 256 * (k % 2) + k // 2:256 * (k % 2) + 256:2], fab[k % 2][0][:].indirect(T["a%d" % (k // 2)][:]),
+                fab[k % 2][1] + ["a%d" % (k // 2)], ["ap%d" % k])
         cp(T.brow[:], T.mate[:].indirect(T.a16[:]), ["mate", "matez", "a16"], ["brow"])
+        later.pop(0)()
         scan(T.wb8[:], T.cw8[:, 0:128], T.brow[:], A.add, A.min, ["cw8", "brow"], ["wb8"])
-        ts(T.b8[:], T.wb8[:, 7:128:8], col(7), A.add, ["wb8", "c7"], ["b8"], 2.0, A.mult)
+        later.pop(0)()
+        ts(T.b8[:], T.wb8[:, 7:128:8], col(PAR), A.add, ["wb8", "par"], ["b8"], 2.0, A.mult)
+        later.pop(0)()
         for k in range(2):
             tt(T.et[:, k:512:2], fab[k][0][:].indirect(T.b8[:]), T.ap[:, 256 * k:256 * k + 256], A.subtract,
-               fab[k][1] + ["b8", "ap%d" % k], ["et%d" % k])
+               fab[k][1] + ["b8", "ap%d" % k, "ap%d" % (k + 2)], ["et%d" % k])
+        later.pop(0)()
         qz(T["qe%d" % t][:], T["se%d" % t][:], T.et[:], ["et0", "et1"], ["qe%d" % t])
         dst = T.cores[(rank + 1 + t) % N]
         src = T.cores[(rank - 1 - t) % N]
@@ -352,46 +384,52 @@ def rank_program(g, core, T, topo):
         g.remote_dma(T["sl%d" % t][:], T["se%d" % t][:], T.sem["arr%d" % t], T.sem.sent, pid, rid, engines(core))
         count["sent"] = count.get("sent", 0) + 2 * bin(engines(core)).count("1")
         arrived = [("arr%d" % t, 2 * bin(engines(src)).count("1"))]
-        scan(T.x2[:], bank(1, 80, 160), T.kd[:], A.min, A.add, ["B1", "kd"], ["x2"])
-        if t < R - 1:
-            ms(T.swin[:, 0:128], 256.0, ["swin"])
-        cp(T.k16[:], T.x2[:, 4:80:5], ["x2"], ["k16"])
-        cp(T.tkb[:], T.m128[:].indirect(T.k16[:]), ["m0", "m1", "m2", "m3", "k16"], ["tk"])
+        for call in later:
+            call()
         if first:
             qz(T.qv[:], T.sv[:], T.vt[:], ["vt"], ["qv"])
-        scan(T.wk[:], T.cw8[:], T.tkb[:], A.add, A.min, ["cw8", "tk"], ["wk"])
-        ts(T.k8[:], T.wk[:, 7:256:8], col(7), A.add, ["wk", "c7"], ["k8"], 2.0, A.mult)
-        order("V", ["k8", "fp0", "fp1", "fp2", "fp3", "B2", "B3", "B4", "B5"], (), ())
+        quant("c", T.ct, 0, 128, cts, ["qc"])
+        mmc(0, "t", 256, "c", 0, 128, ["qt2", "qc"])
+        unpack_own(1, [0, 2, 1, 3])
+        scan(T.x2[:], bank(0, 0, 64), T.kd[:], A.min, A.add, ["B0", "kd"], ["x2"])
+        cp(T.k16[:], T.x2[:, 3:64:4], ["x2"], ["k16"])
+        cp(T.tkb[:], T.m128[:].indirect(T.k16[:]), ["m0", "m1", "m2", "m3", "k16"], ["tk"])
+        scan(T.wk[:], T.cw8[:], T.tkb[:], A.add, A.min, ["cw8", "cw8b", "tk"], ["wk"])
+        ts(T.k8[:], T.wk[:, 7:256:8], col(PAR), A.add, ["wk", "par"], ["k8"], 2.0, A.mult)
+        order("V", ["k8", "B2", "B3", "B4", "B5"], (), ())
         order("A", ["k8"], (), ())
         order("P", ["qw", "sw"], ["B0", "B1", "B6", "B7"], ())
         gb = [0, 1, 6, 7]
         for k in (0, 2, 1, 3):
             mmc(gb[k], "d", 128 * k, "l%d" % t, 0, 128, ["qd%d" % k], arrived if k == 0 else ())
         for k in (0, 2):
-            cp(plane(T.ga, T.gb, k, 128), bank(gb[k], 0, 128), ["B%d" % gb[k]], ["gp%d" % k])
+            cp(plane(T.ga, T.gb, k, 0, 128), bank(gb[k], 0, 128), ["B%d" % gb[k]], ["gp%d" % k])
         for k in (1, 3):
-            act(plane(T.ga, T.gb, k, 128), bank(gb[k], 0, 128), ["B%d" % gb[k]], ["gp%d" % k])
+            act(plane(T.ga, T.gb, k, 0, 128), bank(gb[k], 0, 128), ["B%d" % gb[k]], ["gp%d" % k])
         rb = [gb, [2, 3, 4, 5]]
         gab = (T.ga, T.gb)
         for k in range(2):
             act(T.zg[:, 256 * k:256 * k + 256], gab[k][:].indirect(T.k8[:, 16:32]), ["gp%d" % k, "gp%d" % (k + 2), "k8"], ["zg%d" % k])
 
         def layer(h):
-            qz(T.qz[:, 128 * h:128 * h + 128], T.sz[:, 128 * h:128 * h + 128], T.zt[:, 512 * h:512 * h + 512],
-               ["z%d%d" % (h, k) for k in range(4)], ["qz%d" % h])
+            quant("z", T.zt, 128 * h, 128 * h + 128, ["z%d%d" % (h, k) for k in range(4)], ["qz%d" % h])
             for k in (0, 2, 1, 3):
                 mmc(rb[h][k], "w", 128 * k, "z", 128 * h, 128 * h + 128, ["qw", "sw", "qz%d" % h])
                 act(T.rl[:, 512 * h + k:512 * h + 512:4], bank(rb[h][k], 0, 128), ["B%d" % rb[h][k]],
                     ["rl%d%d" % (h, k)], AF.Relu, 0.015625)
 
-        def add(h, k):
-            v = slice(512 * h + k, 512 * h + 512, 2)
+        def addz(ks):
+            for k in ks:
+                tt(T.zt[:, 512 + k:1024:4], bank(2 + k, 0, 128), T.zg[:, 256 * (k % 2) + k // 2:256 * (k % 2) + 256:2], A.add,
+                   ["B%d" % (2 + k), "zg%d" % (k % 2)], ["z1%d" % k])
+
+        def add(h, *ks):
+            v = slice(512 * h + ks[0], 512 * h + 512, 4 // len(ks))
             tt(T.xn[:, v], T.rl[:, v], T.zt[:, v], A.add,
-               ["rl%d%d" % (h, k), "rl%d%d" % (h, k + 2), "z%d%d" % (h, k), "z%d%d" % (h, k + 2)], ["xn%d%d" % (h, k)])
+               ["%s%d%d" % (n, h, k) for k in ks for n in ("rl", "z")], ["xn%d%d" % (h, k) for k in ks])
 
         def newx(h):
-            qz(T.qx[:, 128 * h:128 * h + 128], T.sx[:, 128 * h:128 * h + 128], T.xn[:, 512 * h:512 * h + 512],
-               ["xn%d0" % h, "xn%d1" % h], ["qx%d" % h])
+            quant("x", T.xn, 128 * h, 128 * h + 128, ["xn%d%d" % (h, k) for k in range(4)], ["qx%d" % h])
 
         def store(h, qc, qs):
             lo, hi = 128 * h, 128 * h + 128
@@ -402,21 +440,21 @@ def rank_program(g, core, T, topo):
         for k in range(2):
             tt(T.zt[:, k:512:2], gab[k][:].indirect(T.k8[:, 0:16]), fab[k][0][:, 0:256], A.add,
                ["gp%d" % k, "gp%d" % (k + 2), "k8"] + fab[k][1], ["z0%d" % k, "z0%d" % (k + 2)])
+        addz([0])
         layer(0)
-        for k in (0, 2, 1, 3):
-            tt(T.zt[:, 512 + k:1024:4], bank(2 + k, 128, 256), T.zg[:, 256 * (k % 2) + k // 2:256 * (k % 2) + 256:2], A.add,
-               ["B%d" % (2 + k), "zg%d" % (k % 2)], ["z1%d" % k])
+        addz([2, 1, 3])
         layer(1)
-        add(0, 0)
-        add(0, 1)
+        for k in (0, 2, 1, 3):
+            add(0, k)
         add(1, 0)
         newx(0)
+        add(1, 2)
         if t == R - 1:
             mmc(0, "v", 0, "x", 0, 128, ["qv", "qx0"])
             store(0, "S", "")
             act(T.yo[:, 0:128], bank(0, 0, 128), ["B0"], ["yo0"])
             dma("A", T.y[:, 0:128], T.yo[:, 0:128], ["yo0"])
-            add(1, 1)
+            add(1, 1, 3)
             newx(1)
             mmc(1, "v", 0, "x", 128, 256, ["qv", "qx1"])
             store(1, "A", "SAAA")
@@ -424,9 +462,12 @@ def rank_program(g, core, T, topo):
             dma("S", T.y[:, 128:256], T.yo[:, 128:256], ["yo1"])
         else:
             scores(0)
-            act(T.sg[:, 0:44], bank(0, 0, 44), ["B0"], ["sg"], AF.Sign)
-            act(T.hv[:, 0:44], T.sg[:, 0:44], ["sg"], ["bits0"], AF.Relu)
-            add(1, 1)
+            unpack_own(0, [0, 2, 1])
+            act(T.sg[:], bank(1, 0, 128), ["B1"], ["sg"], AF.Sign)
+            act(T.ct[:, 1:512:4], T.sg[:], ["sg"], cts[:4], AF.Relu)
+            copy_own(0, [0, 2, 1])
+            add(1, 1, 3)
+            signs(0)
             newx(1)
 
     for s, n in sorted(count.items()):

@@ -2,29 +2,93 @@ from concourse.mybir import dt, AluOpType, AxisListType, ActivationFunctionType
 
 N, C, M, R = 8, 256, 32, 3
 X4, U8, BF, F16, F32, I32, U16 = "float8_e4m3fn_x4", "uint8", "bfloat16", "float16", "float32", "int32", "uint16"
+STEP = 1.0 / 512
+JOINT = 5
 OWN = 2048.0
 HOLD = 256.0
-STEP = 2.0 * C
 NEAR = 1.5 * 2.0 ** 23
-SCANS = 7
+PL = 272
+PLANES = (0, 2, 1, 3)
+HAND = 245
+LEAST = {"V": 64, "A": 64, "P": 0, "G": 0, "S": 0}
+EXTRA = {"V": 10, "A": 80, "P": 40, "G": 170, "S": 0}
+LATE = {"V": 0, "A": 30, "P": 70, "G": 10}
+LOAD, SEND = 2100, 1700
+SLACKS = (10, 10, 0, 20, 10, 40, 5, 15)
+AHEAD = 600
+ORDER = []
 
 SCRATCH = {"ps": ("psum", [128, 4096], F32)}
 for _d, _l in (
-    (BF, "xt:1024 ut:512 vt:512 xn:1024 zt:1024 et:512 tt:1536 la:528 iot:256 dd:96 cw:128 cw8:256 half:8 gri:128 "
-         "sg:128 bits:16 hv:16 ot:1024 ct:528 tf:640 mask:256 fl:256 cnt:256 junk:256 mate:272 "
-         "brow:128 wb8:128 fa:528 fb:528 ap:512 ga:256 gb:256 zg:512 m128:1024 tkb:256 wk:256"),
-    (F16, "ramp:%d th:%d" % (C * SCANS, C * SCANS)),
-    (F32, "rf:44 col:16 sm8:8 gw:256 rr:16 fr:16 back:8 ya:8 kd:64 x2:64 rl:1024 yo:256"),
-    (I32, "rint:44"),
-    (U16, "lr:8 t16:16 k16:16 a16:8 a0:8 a1:8 b8:16 k8:32"),
+    (BF, "xt:1024 ut:512 vt:512 xn:1024 zt:1024 et:512 tk:528 pp:528 tp:528 la:528 iot:256 down:256 cw:128 cw8:128 half:8 "
+         "gri:256 sg:128 bits:16 hv:16 ot:512 ct:528 nt:512 rt:1024 tf:384 ones:256 mate:272 brow:128 "
+         "ff:%d ap:512 gg:512 zg:512" % (4 * PL)),
+    (F16, "ramp:1088 th:1088 mk:256 fl:272 two:272 wb8:128"),
+    (F32, "rf:8 col:16 sm8:8 gw:256 rr:16 fr:16 back:8 ya:8 kd:64 x2:64 rl:1024 yo:256 tv:384"),
+    (I32, "rint:8 ki:16"),
+    (U16, "t16:16 a16:8 b8:16 kk:24"),
 ):
     for _e in _l.split():
         SCRATCH[_e.split(":")[0]] = ("sbuf", [128, int(_e.split(":")[1])], _d)
-for _e in "x:256 z:256 u:128 v:128 w:512 t:384 d:512 o:256 b:256 n:256 c:128 e0:128 e1:128 e2:128 l0:128 l1:128 l2:128".split():
+for _e in ("x:256 z:256 u:128 v:128 w:512 k:384 t:256 p:256 d:512 o:128 b:256 n:128 c:128 "
+           "e0:128 e1:128 e2:128 l0:128 l1:128 l2:128").split():
     SCRATCH["q" + _e.split(":")[0]] = ("sbuf", [128, int(_e.split(":")[1])], X4)
     SCRATCH["s" + _e.split(":")[0]] = ("sbuf", [128, int(_e.split(":")[1])], U8)
 
 SEMAPHORES = ["cV", "cA", "cP", "cG", "sent"] + ["arr%d" % _t for _t in range(R)] + ["d%d" % _i for _i in range(24)]
+
+
+def schedule(calls):
+    before, wrote, reads = [], {}, {}
+    for i, (q, _, r, w, busy, late) in enumerate(calls):
+        pre = set()
+        for k in r:
+            pre |= set(wrote.get(k, ())) | (set(j for j in reads.get(k, ()) if calls[j][0] != q) if k[0] == "B" else set())
+        for k in w:
+            pre |= set(wrote.get(k, ())) | set(reads.get(k, ()))
+        before.append(sorted(pre))
+        for k in r:
+            reads.setdefault(k, []).append(i)
+        for k in w:
+            wrote[k], reads[k] = [i], []
+    after = [[] for _ in calls]
+    for i, pre in enumerate(before):
+        for j in pre:
+            after[j].append(i)
+    queue, busy, late = [[c[k] for c in calls] for k in (0, 4, 5)]
+
+    def place(rest, before, lag, way, slack):
+        free, start = {q: 0 for q in LEAST}, {}
+        while rest:
+            soon = dict(start)
+            for i in rest:
+                soon[i] = max([free[queue[i]], lag(None, i)] + [soon[j] + busy[j] + lag(j, i) for j in before[i]])
+            picks = []
+            for q in LEAST:
+                mine = [i for i in rest if queue[i] == q]
+                now = min([soon[i] for i in mine] + [1e9])
+                near = [i for i in mine if soon[i] <= now + AHEAD]
+                end = {i: max([soon[i] + way[i]] + [max(soon[j], soon[i] + busy[i]) + way[j] for j in near if j != i]) for i in near}
+                if near:
+                    picks.append(min((soon[i], -way[i], i) for i in near if end[i] <= min(end.values()) + slack))
+            i = min([p for p in picks if all(j in start for j in before[p[2]])] or
+                    [(soon[j], 0, j) for j in rest if all(k in start for k in before[j])])[2]
+            start[i] = soon[i]
+            free[queue[i]] = soon[i] + busy[i]
+            rest.remove(i)
+        return start
+
+    ids = list(range(len(calls)))
+    way = [0] * len(calls)
+    for i in reversed(ids):
+        way[i] = busy[i] + late[i] + max([HAND + way[j] for j in after[i]] + [0])
+    tries = []
+    for slack in SLACKS:
+        start = place(ids[:], before, lambda j, i: 0 if j is None else late[j] + HAND, way, slack)
+        tries.append((max(start[i] + busy[i] + late[i] for i in ids), sorted(ids, key=lambda i: (start[i], i))))
+        back = place(ids[::-1], after, lambda j, i: late[i] + (0 if j is None else HAND), [start[i] + busy[i] for i in ids], slack)
+        way = [back[i] + busy[i] for i in ids]
+    return min(tries)[1]
 
 
 def rank_program(g, core, T, topo):
@@ -33,13 +97,13 @@ def rank_program(g, core, T, topo):
         return
     A, AF, AX = AluOpType, ActivationFunctionType, AxisListType.X
     eng = {"V": g.vector, "A": g.scalar, "P": g.tensor, "G": g, "S": g.sync}
+    calls = []
     clock = {q: {} for q in eng}
     count = {}
     seen = {}
     wrote, reads = {}, {}
-    ndma = [0]
 
-    def order(q, r, w, ext):
+    def order(q, r, w):
         need = {}
         for k in r:
             for e in ([wrote[k]] if k in wrote else []) + ([x for x in reads.get(k, []) if x[2] != q] if k[0] == "B" else []):
@@ -47,9 +111,7 @@ def rank_program(g, core, T, topo):
         for k in w:
             for e in ([wrote[k]] if k in wrote else []) + reads.get(k, []):
                 need[e[0]] = max(need.get(e[0], 0), e[1])
-        for s, n in ext:
-            need[s] = n
-        todo = sorted(need.items())
+        todo = sorted(need.items(), key=lambda e: (e[0][:3] == "arr", e))
         for s, n in todo:
             if any(seen.get(o, {}).get(s, 0) >= n for o in todo if o[0] != s):
                 continue
@@ -68,68 +130,71 @@ def rank_program(g, core, T, topo):
             wrote[k] = (s, n, q)
             reads[k] = []
 
-    def op(q, fn, r=(), w=(), ext=()):
-        order(q, r, w, ext)
-        s = "c" + q
-        fn().then_inc(T.sem[s], 1)
-        done(q, s, count.get(s, 0) + 1, r, w)
+    def op(q, c, fn, r, w):
+        def issue():
+            s = "c" + q
+            fn().then_inc(T.sem[s], 1)
+            done(q, s, count.get(s, 0) + 1, r, w)
+        calls.append((q, issue, r, w, max(c, LEAST[q]) + EXTRA[q], LATE[q]))
 
     def dma(q, out, in_, r=(), w=()):
-        order(q, r, w, ())
-        s = "d%d" % ndma[0]
-        ndma[0] += 1
-        eng[q].dma_start(out, in_).then_inc(T.sem[s], 16)
-        done(q, s, 16, r, w)
+        def issue():
+            s = "d%d" % sum(k[0] == "d" for k in count)
+            eng[q].dma_start(out, in_).then_inc(T.sem[s], 16)
+            done(q, s, 16, r, w)
+        calls.append((q, issue, r, w, 60, LOAD))
 
     V, S_ = g.vector, g.scalar
+    look = lambda n: 60 + 7 * n // 5
 
-    def ts(out, in0, s1, o0, r, w, s2=None, o1=None):
+    def ts(c, out, in0, s1, o0, r, w, s2=None, o1=None):
         if o1 is None:
-            op("V", lambda: V.tensor_scalar(out, in0, s1, None, o0), r, w)
+            op("V", c, lambda: V.tensor_scalar(out, in0, s1, None, o0), r, w)
         else:
-            op("V", lambda: V.tensor_scalar(out, in0, s1, s2, o0, o1), r, w)
+            op("V", c, lambda: V.tensor_scalar(out, in0, s1, s2, o0, o1), r, w)
 
-    def tt(out, a, b, o, r, w):
-        op("V", lambda: V.tensor_tensor(out, a, b, o), r, w)
+    def tt(c, out, a, b, o, r, w):
+        op("V", c, lambda: V.tensor_tensor(out, a, b, o), r, w)
 
-    def cp(out, in_, r, w):
-        op("V", lambda: V.tensor_copy(out, in_), r, w)
+    def cp(c, out, in_, r, w):
+        op("V", c, lambda: V.tensor_copy(out, in_), r, w)
 
-    def ms(out, c, w):
-        op("V", lambda: V.memset(out, c), (), w)
+    def ms(c, out, x, w):
+        op("V", c, lambda: V.memset(out, x), (), w)
 
-    def scan(out, d0, d1, o0, o1, r, w, init=0.0):
-        op("V", lambda: V.tensor_tensor_scan(out, d0, d1, init, o0, o1), r, w)
+    def scan(c, out, d0, d1, o0, o1, r, w, init=0.0):
+        op("V", c, lambda: V.tensor_tensor_scan(out, d0, d1, init, o0, o1), r, w)
 
     def qz(q, s, t, r, w):
-        op("V", lambda: V.quantize_mx(q, s, t), r, w)
+        op("V", 150, lambda: V.quantize_mx(q, s, t), r, w)
 
-    def act(out, in_, r, w, f=None, scale=1.0, bias=None):
+    def act(c, out, in_, r, w, f=None, scale=1.0, bias=None):
         if f is None:
-            op("A", lambda: S_.activation(out, in_, AF.Copy), r, w)
+            op("A", c, lambda: S_.activation(out, in_, AF.Copy), r, w)
         elif bias is None:
-            op("A", lambda: S_.activation(out, in_, f, scale=scale), r, w)
+            op("A", c, lambda: S_.activation(out, in_, f, scale=scale), r, w)
         else:
-            op("A", lambda: S_.activation(out, in_, f, bias=bias, scale=scale), r, w)
+            op("A", c, lambda: S_.activation(out, in_, f, bias=bias, scale=scale), r, w)
 
-    def lin(out, in_, scale, bias, r, w):
-        act(out, in_, r, w, AF.Identity, scale, bias)
+    def lin(c, out, in_, scale, bias, r, w):
+        act(c, out, in_, r, w, AF.Identity, scale, bias)
 
-    def iota(out, pat, base, cm, w, small=True):
+    def iota(n, out, pat, base, cm, w, small=True):
         if small:
-            op("G", lambda: g.iota(out, pat, base, cm, allow_small_or_imprecise_dtypes=True), (), w)
+            op("G", 2 * n, lambda: g.iota(out, pat, base, cm, allow_small_or_imprecise_dtypes=True), (), w)
         else:
-            op("G", lambda: g.iota(out, pat, base, cm), (), w)
+            op("G", 2 * n, lambda: g.iota(out, pat, base, cm), (), w)
 
-    def sel(out, in_, pat, cmp, fill, cm, r, w, base=0):
-        op("G", lambda: g.affine_select(out, in_, pat, cmp, fill, base, cm), r, w)
+    def sel(n, out, in_, pat, cmp, fill, cm, r, w, base=0):
+        op("G", 2 * n + 50, lambda: g.affine_select(out, in_, pat, cmp, fill, base, cm), r, w)
 
     def bank(b, lo, hi, step=1):
         return T.ps[:, 512 * b + lo:512 * b + hi:step]
 
-    def mmc(b, lname, la, rname, ra, rb, r, ext=()):
-        op("P", lambda: g.tensor.matmul_mx(bank(b, 0, rb - ra), T["q" + lname][:, la:la + 128], T["s" + lname][:, la:la + 128],
-                                           T["q" + rname][:, ra:rb], T["s" + rname][:, ra:rb], True, True), r, ["B%d" % b], ext)
+    def mmc(b, lname, la, rname, ra, rb, r):
+        op("P", 2 * (rb - ra + 16) // 3, lambda: g.tensor.matmul_mx(
+            bank(b, 0, rb - ra), T["q" + lname][:, la:la + 128], T["s" + lname][:, la:la + 128],
+            T["q" + rname][:, ra:rb], T["s" + rname][:, ra:rb], True, True), r, ["B%d" % b])
 
     def engines(c):
         i, m = T.rank_of(c), -1
@@ -137,339 +202,236 @@ def rank_program(g, core, T, topo):
             m &= topo.mask(c, T.cores[(i + 1 + t) % N])
         return m
 
-    def quant(name, src, lo, hi, r, w):
-        qz(T["q" + name][:, lo:hi], T["s" + name][:, lo:hi], src[:, 4 * lo:4 * hi], r, w)
+    def send(t):
+        dst, src = T.cores[(rank + 1 + t) % N], T.cores[(rank - 1 - t) % N]
+        rid, pid = topo.addr(dst)[0], topo.addr(dst)[1]
 
-    def unpackers(bs):
-        for b in bs:
-            qz(T.qd[:, 128 * b:128 * b + 128], T.sd[:, 128 * b:128 * b + 128], T.la[:, 3 - b:515 - b], ["la"], ["qd%d" % b])
+        def issue():
+            g.remote_dma(T["ql%d" % t][:].bitcast(dt.uint8), T["qe%d" % t][:].bitcast(dt.uint8),
+                         T.sem["arr%d" % t], T.sem.sent, pid, rid, engines(core))
+            g.remote_dma(T["sl%d" % t][:], T["se%d" % t][:], T.sem["arr%d" % t], T.sem.sent, pid, rid, engines(core))
+            count["sent"] = count.get("sent", 0) + 2 * bin(engines(core)).count("1")
+            wrote["came%d" % t] = ("arr%d" % t, 2 * bin(engines(src)).count("1"), "G")
+        calls.append(("G", issue, ["qe%d" % t], ["came%d" % t], 400, SEND))
 
-    def ramps(cs):
-        for c in cs:
-            lin(T.ramp[:, C * c:C * c + C], T.iot[:], 2.0, -STEP * (c + 1), ["iot"], ["ramp%d" % c])
+    def window(name, k, src, lo, r):
+        qz(T["q" + name][:, 128 * k:128 * k + 128], T["s" + name][:, 128 * k:128 * k + 128], src[:, lo:lo + 512], r, ["q%s%d" % (name, k)])
 
     col = lambda i: T.col[:, i:i + 1]
-    K16, R2, G16, P16, R16 = [T.rf[:, i:i + 1] for i in range(5)]
-    ones = T.tt[:, 0:1024:4]
-    ft, tv = T.tf[:, 0:384], T.tf[:, 256:640]
-    POW, H16, H8, PAR, E0, W3, ACOL, BCOL, WCOL, CNT0, TCOL = range(11)
+    K16, G16, S16, R8, R16 = [T.rf[:, i:i + 1] for i in range(5)]
+    POW, PAR, E0, W3, ACOL, BCOL, WCOL, CNT0, TCOL, UP8, UP16, TMP, TM2 = range(13)
+    blk, tri = T.tk[:, 3:512:4], T.tk[:, 1:512:4]
+    tks = ["k1", "k2", "tri", "blk", "tkz"]
     cts = ["cf%d" % s for s in range(4)] + ["cr%d" % s for s in range(4)]
+    tps = ["tp2", "tp3"]
+    sns = ["sn0", "sn2", "snz"]
+    gw = ["gw0", "gw1"]
 
     dma("S", T.xt[:, 0:512], T.x[:, 0:512], (), ["X0"])
     dma("A", T.ut[:], T.u[:], (), ["ut"])
     dma("S", T.xt[:, 512:1024], T.x[:, 512:1024], (), ["X1"])
-
-    iota(T.rint[:, 0:12], [[0, 12]], 0, 16, ["ri0", "ri1", "ri2", "ri4"], False)
-    iota(T.rint[:, 12:28], [[16, 16]], 2048, -16, ["ri12"], False)
-    iota(T.rint[:, 28:44], [[0, 2], [32, 8]], 2064, -16, ["ri28"], False)
-    iota(T.gri[:], [[16, 8], [0, 16]], 0, 0, ["gri"])
-    iota(T.tt[:, 2:1024:4], [[-1, 2], [0, 128]], 1, 0, ["t3"])
-    ms(T.ct[:], 0.0, cts)
-    ms(ones, 1.0, ["ones"])
-    sel(T.tt[:, 1024:1536:2], ones, [[2, 128], [-128, 2]], A.is_ge, 0.0, -1, ["ones"], ["t2a"], 1)
-    sel(T.tt[:, 1024:1536:2], T.tt[:, 1024:1536:2], [[-2, 128], [128, 2]], A.is_gt, 2.0, 1, [], ["t2a"])
-    ts(T.rint[:, 0:1], T.rint[:, 0:1], 48, A.bitwise_and, [], ["ri0"])
-    scan(T.iot[:], ones, ones, A.mult, A.add, ["ones"], ["iot"], -1.0)
-    ts(T.rint[:, 1:2], T.rint[:, 1:2], 16, A.bitwise_and, [], ["ri1"])
-    ts(T.rint[:, 2:3], T.rint[:, 2:3], 4, A.arith_shift_right, [], ["ri2"], 240, A.bitwise_and)
-    ts(T.rint[:, 4:28], T.rint[:, 4:28], 240, A.bitwise_and, [], ["ri4", "ri12"])
-    ts(T.rint[:, 28:44], T.rint[:, 28:44], 1, A.arith_shift_right, [], ["ri28"], 112, A.bitwise_and)
-    lin(T.ot[:, 1:1024:2], T.ct[:, 0:512], 0.0, None, cts, ["otz"])
-    dma("S", T.la[:], T.ct[:], cts, ["la"])
-    ms(T.tt[:, 3:1024:4], 0.0, ["tz"])
-    cp(T.rf[:], T.rint[:], ["ri0", "ri1", "ri2", "ri4", "ri12", "ri28"], ["rf"])
-    ms(T.half[:], 0.5, ["half"])
-    ts(T.sm8[:], T.iot[:, 0:128:16], G16, A.is_lt, ["iot", "rf"], ["s8"], 1.0, A.add)
-    ts(col(E0), R16, 0.0, A.is_equal, ["rf"], ["e0"], 1.0 / 32, A.mult)
-    act(col(W3), R16, ["rf"], ["w3"], AF.Relu, -1.0 / 512, 3.0 / 32)
-    act(T.dd[:, 0:32], T.rf[:, 12:44], ["rf"], ["dd0"], AF.Relu, -0.375 * HOLD, 6.0 * HOLD)
-    act(T.dd[:, 32:64], T.rf[:, 12:44], ["rf"], ["dd1"], AF.Relu, -HOLD / 16, 2.0 * HOLD)
-    op("V", lambda: V.tensor_reduce(col(POW), T.sm8[:], AX, A.mult, negate=True), ["s8"], ["pow"])
-    ts(T.tt[:, 1027:1536:4], T.gri[:], G16, A.is_equal, ["gri", "rf"], ["t2c"], 4.0, A.mult)
-    ts(col(WCOL), col(E0), col(W3), A.add, ["e0", "w3"], ["wcol"], 128.0, A.mult)
-    ts(col(BCOL), col(E0), -3.0, A.mult, ["e0", "w3"], ["bcol"], col(W3), A.add)
-    ts(col(ACOL), col(E0), col(POW), A.mult, ["e0", "pow"], ["acol"], -32.0, A.mult)
-    lin(T.tt[:, 513:1024:4], T.tt[:, 1027:1536:4], col(WCOL), None, ["t2c", "wcol"], ["k2"])
-    lin(T.tt[:, 1:512:4], T.tt[:, 1027:1536:4], col(BCOL), col(ACOL), ["t2c", "bcol", "acol"], ["k1"])
-    ts(T.lr[:], T.rf[:, 4:12], 0.0625, A.mult, ["rf"], ["lr"])
-    tt(T.dd[:, 64:96], T.dd[:, 0:32], T.dd[:, 32:64], A.subtract, ["dd0", "dd1"], ["dd2"])
-    qz(T.qu[:], T.su[:], T.ut[:], ["ut"], ["qu"])
-    act(T.cw[:], T.dd[:, 64:80].indirect(T.lr[:]), ["dd2", "lr"], ["cw"])
-    ramps([0, 1])
-    sel(T.tt[:, 1025:1536:4], T.tt[:, 1027:1536:4], [[1, 128]], A.is_gt, 0.0, -1, ["t2c"], ["t2b"])
-    sel(T.tt[:, 1025:1536:4], T.tt[:, 1025:1536:4], [[1, 128]], A.not_equal, -OWN, -1, ["t2b"], ["t2b"])
-    iota(T.tf[:, 512:640], [[0, 128]], 0, 0, ["tvz"])
-    iota(T.back[:], [[int(STEP), 8]], int(STEP), 0, ["back"])
-    iota(T.mate[:, 256:272], [[0, 16]], C, 0, ["matez"])
-    iota(T.fa[:, 512:528], [[0, 16]], 0, 0, ["faz"])
-    iota(T.fb[:, 512:528], [[0, 16]], 0, 0, ["fbz"])
-    for k in range(2):
-        iota(T.m128[:, 128 * k:128 * k + 128], [[4, 4], [16, 8], [1, 4]], 0, 0, ["m0"])
-    iota(T.kd[:], [[0, 64]], -1, 0, ["kd"])
-    iota(T.kd[:, 3:64:4], [[0, 16]], int(OWN) + 3, 0, ["kd"])
-
-    def scores(h):
-        mmc(6 * h, "x", 128 * h, "u", 0, 128, ["qx%d" % h, "qu"])
-        mmc(6 * h + 1, "u", 0, "x", 128 * h, 128 * h + 128, ["qx%d" % h, "qu"])
-
-    def signs(h):
-        ts(T.bits[:, 8 * h:8 * h + 8], bank(6 * h, 0, 128, 16), 0.0, A.is_gt, ["B%d" % (6 * h)], ["bits%d" % h])
-
-    def signrow(h):
-        ts(T.ct[:, 1:512:4], bank(6 * h + 1, 0, 128), 0.0, A.is_gt, ["B%d" % (6 * h + 1)], cts[:4])
-
-    def rows(h):
-        qz(T.qb[:, 128 * h:128 * h + 128], T.sb[:, 128 * h:128 * h + 128], T.ct[:, 0:512], cts, ["qb%d" % h])
-
-    def turn(h, k):
-        mmc(6 * h + k, "t", 128 * k, "b", 128 * h, 128 * h + 128, ["qt%d" % k, "qb%d" % h])
-
-    def wrap(h):
-        v = slice(128 * h, 128 * h + 128)
-        scan(T.gw[:, v], T.cw[:], bank(6 * h, 0, 128), A.add, A.min, ["cw", "B%d" % (6 * h)], ["gw%d" % h])
-
-    def mask(h):
-        ts(T.mask[:, 128 * h:128 * h + 128], bank(6 * h + 1, 0, 128), K16, A.is_equal, ["B%d" % (6 * h + 1), "rf"],
-           ["mask%d" % h], -STEP, A.mult)
-
-    def word(h):
-        scan(T.hv[:, 8 * h:8 * h + 8], T.half[:], T.bits[:, 8 * h:8 * h + 8], A.mult, A.add, ["half", "bits%d" % h], ["hv%d" % h])
-
-    def onehot(h):
-        ts(T.ot[:, 2 * h:1024:4], T.iot[:], 1.0 / 128, A.mult, ["iot", "hv%d" % h], ["ot%d" % h],
-           T.hv[:, 8 * h + 7:8 * h + 8], A.is_equal)
-
-    def unpack_own(h, ks):
-        for k in ks:
-            mmc(2 + k, "d", 128 * k, "x", 128 * h, 128 * h + 128, ["qd%d" % k, "qx%d" % h])
-
-    def plane(a, b, k, lo, hi):
-        return (a, b)[k % 2][:, 2 * lo + k // 2:2 * hi:2]
-
-    def copy_own(h, ks):
-        for k in ks:
-            act(plane(T.fa, T.fb, k, 128 * h, 128 * h + 128), bank(2 + k, 0, 128), ["B%d" % (2 + k)], ["f%d%d" % (h, k)])
-
-    def flags(s):
-        ts(T.ct[:, 1 + 4 * s:256:16], T.fr[:], s / 8.0, A.is_equal, ["fr"], ["cf%d" % s])
-
-    def running(s):
-        f = T.ct[:, 1 + 4 * s:256:16]
-        scan(T.ct[:, 19 + 4 * s:272:16], f, f, A.add, A.max, ["cf%d" % s], ["cr%d" % s])
-
-    quant("x", T.xt, 0, 128, ["X0"], ["qx0"])
-    scores(0)
-    quant("x", T.xt, 128, 256, ["X1"], ["qx1"])
     dma("S", T.qw[:].bitcast(dt.uint8), T.wc[:], ["X1"], ["qw"])
-    dma("S", T.sw[:], T.ws[:], (), ["sw"])
-    dma("S", T.vt[:], T.v[:], (), ["vt"])
-    for k in (1, 2, 3):
-        dma("S", T.m128[:, 256 * k:256 * k + 256], T.m128[:, 0:256], ["m0"], ["m%d" % k])
-    quant("t", T.tt, 0, 256, ["k1", "k2", "t3", "tz", "ones"], ["qt0", "qt1"])
-    signs(0)
-    signrow(0)
+    dma("S", T.sw[:], T.ws[:], ["X1"], ["sw"])
+    dma("S", T.vt[:], T.v[:], ["X1"], ["vt"])
 
+    iota(8, T.rint[:], [[0, 8]], 0, 16, ["ri%d" % i for i in range(5)], False)
+    iota(256, T.gri[:], [[16, 8], [0, 32]], 0, 0, ["gri"])
+    iota(516, T.pp[:, 0:516], [[2, 129], [1024, 2], [-128, 2]], -1022, -1, ["pp"])
+    ms(128, T.ones[:], 1.0, ["ones"])
+    ms(1, T.fl[:, 0:16], STEP, ["flz"])
+    ms(1, T.two[:, 256:272], -1024.0, ["twoz"])
+    ms(264, T.rt[:, 0:528], 0.0, ["rt0"])
+    lin(528, T.tp[:], T.rt[:, 0:528], 0.0, None, ["rt0", "rt1"], tps)
+    lin(512, T.rt[:, 512:1024], T.rt[:, 0:512], 0.0, None, ["rt0"], ["rt1"])
+    scan(128, T.iot[:], T.ones[:], T.ones[:], A.mult, A.add, ["ones"], ["iot"], -1.0)
+    ts(1, T.rint[:, 0:1], T.rint[:, 0:1], 48, A.bitwise_and, [], ["ri0"])
+    ts(1, T.rint[:, 1:2], T.rint[:, 1:2], 4, A.arith_shift_right, [], ["ri1"], 240, A.bitwise_and)
+    ts(1, T.rint[:, 2:3], T.rint[:, 2:3], 2, A.arith_shift_right, [], ["ri2"], 48, A.bitwise_and)
+    ts(1, T.rint[:, 3:4], T.rint[:, 3:4], 224, A.bitwise_and, [], ["ri3"])
+    ts(1, T.rint[:, 4:5], T.rint[:, 4:5], 240, A.bitwise_and, [], ["ri4"])
+    ms(1, T.half[:], 0.5, ["half"])
+    cp(1, T.rf[:], T.rint[:], ["ri%d" % i for i in range(5)], ["rf"])
+    ms(1, T.tk[:, 512:528], 0.0, ["tkz"])
+    ms(1, T.tp[:, 2:516:4], 1.0, ["tp2"])
+    ms(1, T.tp[:, 3:516:4], 1.0, ["tp3"])
+    sel(516, T.la[:, 0:516], T.tp[:, 0:516], [[1, 516]], A.is_equal, 0.0, -4, tps, ["la"], -3)
+    iota(256, T.down[:], [[0, 16], [-16384, 16]], 0, 0, ["down"])
+    iota(256, T.nt[:, 1:512:2], [[0, 256]], 0, 0, ["snz"])
+    iota(128, T.tv[:, 256:384], [[0, 128]], 0, 0, ["tvz"])
+    iota(128, T.tf[:, 256:384], [[0, 128]], 0, 0, ["ftz"])
+    iota(8, T.back[:], [[2, 8]], -7, 0, ["back"])
+    iota(16, T.mate[:, 256:272], [[0, 16]], C, 0, ["matez"])
+    for k in range(4):
+        iota(16, T.ff[:, PL * k + C:PL * k + PL], [[0, PL - C]], 0, 0, ["fz%d" % k])
+    iota(528, T.ct[:], [[0, 528]], 0, 0, cts)
+    iota(64, T.kd[:], [[0, 64]], -1, 0, ["kd"])
+    iota(16, T.kd[:, 3:64:4], [[0, 16]], int(OWN) + 3, 0, ["kd"])
+    ts(1, T.sm8[:], T.iot[:, 0:128:16], G16, A.is_lt, ["iot", "rf"], ["s8"], 1.0, A.add)
+    ts(1, col(E0), R16, 0.0, A.is_equal, ["rf"], ["e0"], 1.0 / 32, A.mult)
+    act(1, col(W3), R16, ["rf"], ["w3"], AF.Relu, -1.0 / 512, 3.0 / 32)
+    op("V", 1, lambda: V.tensor_reduce(col(POW), T.sm8[:], AX, A.mult, negate=True), ["s8"], ["pow"])
+    ts(128, T.tk[:, 1:512:2], T.gri[:], G16, A.is_equal, ["gri", "rf"], ["blk", "tri"], 4.0, A.mult)
+    ts(1, col(ACOL), col(E0), col(POW), A.mult, ["e0", "pow"], ["acol"], -32.0, A.mult)
+    ts(1, col(WCOL), col(E0), col(W3), A.add, ["e0", "w3"], ["wcol"], 128.0, A.mult)
+    ts(1, col(BCOL), col(E0), -3.0, A.mult, ["e0", "w3"], ["bcol"], col(W3), A.add)
+    lin(1, T.col[:, UP8:UP16 + 1], T.rf[:, 3:5], 1024.0, 8192.0, ["rf"], ["up"])
+    lin(128, T.tk[:, 2:512:4], blk, col(WCOL), None, ["blk", "wcol"], ["k2"])
+    lin(128, T.tk[:, 0:512:4], blk, col(BCOL), col(ACOL), ["blk", "bcol", "acol"], ["k1"])
+    lin(1, col(TMP), R16, 16.0, NEAR - 15 * HOLD, ["rf"], ["tmp"])
+    lin(1, col(TM2), R8, -8.0 - PL / 16.0, None, ["rf"], ["tm2"])
+    lin(1, col(CNT0), K16, 1.0, 8.0 - 2 * STEP, ["rf"], ["cnt0"])
+    lin(1, col(TCOL), col(TMP), 1.0, col(POW), ["pow", "tmp"], ["tcol"])
+    lin(1, col(PAR), R16, PL / 16.0, col(TM2), ["rf", "tm2"], ["par"])
+    ts(64, T.cw[:], T.down[:, 0:128], col(UP16), A.add, ["down", "up"], ["cw"], -HOLD, A.max)
+    ts(64, T.cw8[:], T.down[:, 0:256:2], col(UP8), A.add, ["down", "up"], ["cw8"], -HOLD, A.max)
+    act(516, T.pp[:, 0:516], T.pp[:, 0:516], [], ["pp"], AF.Relu)
+    for c in range(8):
+        lin(128, T.ramp[:, 136 * c:136 * c + 129], T.iot[:, 0:129], 1.0 / 128, 7.0 - 2 * c, ["iot"], ["ramp%d" % c])
+    window("u", 0, T.ut, 0, ["ut"])
+    window("v", 0, T.vt, 0, ["vt"])
+    for k in range(2):
+        window("x", k, T.xt, 512 * k, ["X%d" % k])
+        window("k", k, T.tk, 2 * k, tks)
+        window("t", k, T.tp, 2 - 2 * k, tps)
+        window("p", k, T.pp, 2 - 2 * k, ["pp"])
+    for k in PLANES:
+        window("d", k, T.la, 3 - k, ["la"])
+    sel(128, tri, blk, [[1, 128]], A.is_gt, 0.0, -1, ["blk"], ["tri"])
+    sel(128, tri, tri, [[1, 128]], A.not_equal, -OWN, -1, [], ["tri"])
+    window("k", 2, T.tk, 0, tks)
+
+    def unpack(h, k, b):
+        hs = (0, 1) if h == 2 else (h,)
+        mmc(b, "d", 128 * k, "x", 128 * hs[0], 128 * hs[-1] + 128, ["qd%d" % k] + ["qx%d" % i for i in hs])
+
+    def own(h, k, b):
+        hs = (0, 1) if h == 2 else (h,)
+        lo, hi = 128 * hs[0], 128 * hs[-1] + 128
+        unpack(h, k, b)
+        act(hi - lo, T.ff[:, PL * PLANES.index(k) + lo:PL * PLANES.index(k) + hi], bank(b, 0, hi - lo), ["B%d" % b],
+            ["f%d%d" % (i, k) for i in hs])
+
+    def signs(h, first):
+        b0, b1, v = 6 * h, 6 * h + 1, slice(128 * h, 128 * h + 128)
+        mmc(b0, "x", 128 * h, "u", 0, 128, ["qx%d" % h, "qu0"])
+        mmc(b1, "u", 0, "x", 128 * h, 128 * h + 128, ["qx%d" % h, "qu0"])
+        ts(1, T.bits[:, 8 * h:8 * h + 8], bank(b0, 0, 128, 16), 0.0, A.is_gt, ["B%d" % b0], ["bits%d" % h])
+        scan(1, T.hv[:, 8 * h:8 * h + 8], T.half[:], T.bits[:, 8 * h:8 * h + 8], A.mult, A.add, ["half", "bits%d" % h], ["hv%d" % h])
+        ts(128, T.ot[:, h:512:2], T.iot[:], 1.0 / 128, A.mult, ["iot", "hv%d" % h], ["ot%d" % h],
+           T.hv[:, 8 * h + 7:8 * h + 8], A.is_equal)
+        ts(128, T.rt[:, 512 * h:512 * h + 512:4], bank(b1, 0, 128), 0.0, A.is_gt, ["B%d" % b1], ["rt%d" % h])
+        window("b", h, T.rt, 512 * h, ["rt%d" % h])
+        mmc(b0, "k", 0, "b", 128 * h, 128 * h + 128, ["qk0", "qb%d" % h])
+        mmc(b1, "k", 128, "b", 128 * h, 128 * h + 128, ["qk1", "qb%d" % h])
+        scan(128, T.gw[:, v], T.cw[:], bank(b0, 0, 128), A.add, A.min, ["cw", "B%d" % b0], ["gw%d" % h])
+        ts(128, T.mk[:, v], bank(b1, 0, 128), S16, A.not_equal, ["B%d" % b1, "rf"], ["mk%d" % h], STEP - 1.0, A.add)
+
+    signs(0, True)
     for t in range(R):
         first = t == 0
-
-        def own(ks, whole=first):
-            if not whole:
-                unpack_own(1, ks)
-                copy_own(1, ks)
-            for k in ks if whole else ():
-                mmc(2 + k, "d", 128 * k, "x", 0, C, ["qd%d" % k, "qx0", "qx1"])
-                act(plane(T.fa, T.fb, k, 0, C), bank(2 + k, 0, C), ["B%d" % (2 + k)], ["f0%d" % k, "f1%d" % k])
-
-        scores(1)
-        word(0)
-        rows(0)
-        turn(0, 0)
-        turn(0, 1)
-        if not first:
-            own([3], True)
-        signs(1)
-        onehot(0)
-        if first:
-            ts(T.la[:, 3:515:4], T.iot[:, 0:128], 16.0, A.mult, ["iot", "rf"], ["la"], P16, A.is_equal)
-            ramps(range(2, SCANS))
-            act(T.cw8[:, 0:128], T.dd[:, 80:96].indirect(T.lr[:]), ["dd2", "lr"], ["cw8"])
-            dma("A", T.cw8[:, 128:256], T.cw8[:, 0:128], ["cw8"], ["cw8b"])
-        word(1)
-        signrow(1)
-        onehot(1)
-        rows(1)
-        turn(1, 0)
-        quant("o", T.ot, 0, 256, ["ot0", "ot1", "otz"], ["qo"])
-        mmc(2, "t", 0, "o", 0, 256, ["qt0", "qo"])
-        turn(1, 1)
-        if first:
-            ts(T.col[:, H16:H8 + 1], T.rf[:, 27:36:8], 0.0, A.is_gt, ["rf"], ["hold"], -HOLD, A.mult)
-        wrap(0)
-        if first:
-            quant("t", T.tt, 256, 384, ["t2a", "t2b", "t2c"], ["qt2"])
-        wrap(1)
-        if first:
-            ts(col(TCOL), col(H16), col(POW), A.add, ["hold", "pow"], ["tcol"], NEAR, A.add)
-            unpackers([0])
-        mask(0)
-        mmc(0, "t", 256, "o", 0, 256, ["qt2", "qo"])
-        act(T.tf[:, 256:512], bank(2, 0, 256), ["B2"], ["tv"], AF.Sign)
-        gw = ["gw0", "gw1"]
-        ts(T.t16[:], T.gw[:, 15:256:16], NEAR, A.add, gw + ["tcol"], ["t16"], col(TCOL), A.subtract)
-        if first:
-            ts(col(CNT0), R16, K16, A.subtract, ["rf"], ["cnt0"], 64.0, A.mult)
-        else:
-            ts(T.rr[:], T.gw[:, 15:256:16], NEAR, A.add, gw, ["rr"], NEAR, A.subtract)
-        mask(1)
-        if first:
-            unpackers([2])
-        else:
-            tt(T.fr[:], T.gw[:, 15:256:16], T.rr[:], A.subtract, gw + ["rr"], ["fr"])
-        act(T.ot[:, 0:1024:4], bank(0, 0, 256), ["B0"], ["ot0"], AF.Relu, -1.0, 2.0)
-        tt(T.fl[:], tv.indirect(T.t16[:]), T.mask[:], A.mult, ["tv", "tvz", "t16", "mask0", "mask1"], ["fl"])
-        own([0, 2] if first else [0, 2, 1])
-        quant("n", T.ot, 0, 256, ["ot0", "ot1"], ["qn"])
-        mmc(7, "t", 128, "n", 0, 256, ["qt1", "qn"])
-        scan(T.cnt[:], ones, T.fl[:], A.mult, A.add, ["ones", "fl", "cnt0"], ["cnt"], col(CNT0))
-        later = [lambda s=s: flags(s) for s in range(4)] + [lambda s=s: running(s) for s in range(4)]
-        if first:
-            unpackers([1, 3])
-            later = [lambda: ts(col(PAR), R2, 1.0 / 32, A.mult, ["rf", "hold"], ["par"], col(H8), A.subtract),
-                     lambda: ts(T.rr[:], T.gw[:, 15:256:16], NEAR, A.add, gw, ["rr"], NEAR, A.subtract),
-                     lambda: tt(T.fr[:], T.gw[:, 15:256:16], T.rr[:], A.subtract, gw + ["rr"], ["fr"])] + later
-        else:
-            later.pop(0)()
+        signs(1, first)
+        window("o", 0, T.ot, 0, ["ot0", "ot1"])
+        for k in range(2):
+            mmc(2 + k, "t", 128 * k, "o", 0, 128, ["qt%d" % k, "qo0"])
+        for k in range(2):
+            mmc(4 + k, "p", 128 * k, "o", 0, 128, ["qp%d" % k, "qo0"])
+        for k in range(2):
+            ts(128, T.tv[:, k:256:2], bank(2 + k, 0, 128), 0.0, A.is_equal, ["B%d" % (2 + k)], ["tv%d" % k], STEP - 1.0, A.add)
+        ts(1, T.t16[:], T.gw[:, 15:256:16], NEAR, A.add, gw + ["tcol"], ["t16"], col(TCOL), A.subtract)
+        for k in range(2):
+            act(128, T.nt[:, 2 * k:512:4], bank(4 + k, 0, 128), ["B%d" % (4 + k)], ["sn%d" % (2 * k)], AF.Relu, -1.0, 2.0)
+        for k, b in zip(PLANES, (0, 1, 6, 7)):
+            own(2 if first else 1, k, b)
+        window("n", 0, T.nt, 0, sns)
+        for k in range(2):
+            mmc(2 + k, "t", 128 * k, "n", 0, 128, ["qt%d" % k, "qn0"])
+            act(128, T.tf[:, k:256:2], bank(2 + k, 0, 128), ["B%d" % (2 + k)], ["ft%d" % k])
+        act(look(256) - 60, T.mate[:, 0:256], T.tf[:].indirect(T.t16[:]), ["ft0", "ft1", "ftz", "t16"], ["mate"])
+        tt(look(256), T.fl[:, 16:272], T.tv[:].indirect(T.t16[:]), T.mk[:], A.max, ["tv0", "tv1", "tvz", "t16", "mk0", "mk1"], ["fl"])
+        scan(128, T.two[:, 0:256], T.fl[:, 15:271], T.fl[:, 16:272], A.add, A.add, ["flz", "fl", "cnt0"], ["two"], col(CNT0))
         for c in range(8):
-            if c < SCANS:
-                scan(T.th[:, C * c:C * c + C], T.ramp[:, C * c:C * c + C], T.cnt[:], A.min, A.max,
-                     ["ramp%d" % c, "cnt"], ["th%d" % c])
-            else:
-                op("A", lambda: S_.activation(T.junk[:], T.cnt[:], AF.Sign, bias=STEP * (c + 0.5), scale=1.0,
-                                              accum_out=T.ya[:, c:c + 1]), ["cnt"], ["junk", "yb%d" % c])
-            if c == SCANS:
-                act(T.tf[:, 0:256], bank(7, 0, 256), ["B7"], ["ft"])
-        yb = ["yb%d" % c for c in range(SCANS, 8)]
-        lin(T.ya[:, SCANS:8], T.ya[:, SCANS:8], 1.0, float(C), [], yb)
-        act(T.mate[:, 0:256], ft.indirect(T.t16[:]), ["ft", "tv", "t16"], ["mate"])
-        if first:
-            own([1, 3])
-        later.pop(0)()
-        tt(T.ya[:, 0:SCANS], T.th[:, C - 1:C * SCANS:C], T.back[:, 0:SCANS], A.add,
-           ["th%d" % c for c in range(SCANS)] + ["back"], ["ya"])
-        later.pop(0)()
-        ts(T.a16[:], T.ya[:], STEP, A.min, ["ya"] + yb, ["a16"], 0.5, A.mult)
-        ts(T.a0[:], T.ya[:], STEP, A.min, ["ya"] + yb, ["a0"])
-        ts(T.a1[:], T.ya[:], STEP, A.min, ["ya"] + yb, ["a1"], 1.0, A.add)
-        fab = ((T.fa, ["f00", "f02", "f10", "f12", "faz"]), (T.fb, ["f01", "f03", "f11", "f13", "fbz"]))
-        for k in (0, 2, 1, 3):
-            act(T.ap[:, 256 * (k % 2) + k // 2:256 * (k % 2) + 256:2], fab[k % 2][0][:].indirect(T["a%d" % (k // 2)][:]),
-                fab[k % 2][1] + ["a%d" % (k // 2)], ["ap%d" % k])
-        cp(T.brow[:], T.mate[:].indirect(T.a16[:]), ["mate", "matez", "a16"], ["brow"])
-        later.pop(0)()
-        scan(T.wb8[:], T.cw8[:, 0:128], T.brow[:], A.add, A.min, ["cw8", "brow"], ["wb8"])
-        later.pop(0)()
-        ts(T.b8[:], T.wb8[:, 7:128:8], col(PAR), A.add, ["wb8", "par"], ["b8"], 2.0, A.mult)
-        later.pop(0)()
+            scan(65, T.th[:, 136 * c:136 * c + 129], T.ramp[:, 136 * c:136 * c + 129], T.two[:, 1:258:2], A.min, A.max,
+                 ["ramp%d" % c, "two", "twoz"], ["th%d" % c], 16.0)
+        tt(1, T.ya[:, 0:JOINT], T.th[:, 128:136 * JOINT:136], T.back[:, 0:JOINT], A.add,
+           ["th%d" % c for c in range(JOINT)] + ["back"], ["ya"])
+        ts(1, T.a16[:, 0:JOINT], T.ya[:, 0:JOINT], float(C), A.mult, ["ya"], ["a16"])
+        for c in range(JOINT, 8):
+            ts(1, T.a16[:, c:c + 1], T.th[:, 136 * c + 128:136 * c + 129], 2.0 * c - 7, A.add, ["th%d" % c], ["a16%d" % c],
+               float(C), A.mult)
+        a16 = ["a16"] + ["a16%d" % c for c in range(JOINT, 8)]
+        fk = lambda k: ["f0%d" % k, "f1%d" % k, "fz%d" % PLANES.index(k)]
+        for i, k in enumerate(PLANES):
+            act(look(128) - 60, T.ap[:, 256 * (k % 2) + k // 2:256 * (k % 2) + 256:2], T.ff[:, PL * i:PL * i + PL].indirect(T.a16[:]),
+                fk(k) + a16, ["ap%d" % k])
+        cp(look(128), T.brow[:], T.mate[:].indirect(T.a16[:]), ["mate", "matez"] + a16, ["brow"])
+        scan(64, T.wb8[:], T.cw8[:], T.brow[:], A.add, A.min, ["cw8", "brow"], ["wb8"])
+        ts(1, T.b8[:], T.wb8[:, 7:128:8], col(PAR), A.add, ["wb8", "par"], ["b8"], 7 * HOLD, A.add)
         for k in range(2):
-            tt(T.et[:, k:512:2], fab[k][0][:].indirect(T.b8[:]), T.ap[:, 256 * k:256 * k + 256], A.subtract,
-               fab[k][1] + ["b8", "ap%d" % k, "ap%d" % (k + 2)], ["et%d" % k])
-        later.pop(0)()
-        qz(T["qe%d" % t][:], T["se%d" % t][:], T.et[:], ["et0", "et1"], ["qe%d" % t])
-        dst = T.cores[(rank + 1 + t) % N]
-        src = T.cores[(rank - 1 - t) % N]
-        rid, pid = topo.addr(dst)[0], topo.addr(dst)[1]
-        order("G", ["qe%d" % t], (), ())
-        g.remote_dma(T["ql%d" % t][:].bitcast(dt.uint8), T["qe%d" % t][:].bitcast(dt.uint8),
-                     T.sem["arr%d" % t], T.sem.sent, pid, rid, engines(core))
-        g.remote_dma(T["sl%d" % t][:], T["se%d" % t][:], T.sem["arr%d" % t], T.sem.sent, pid, rid, engines(core))
-        count["sent"] = count.get("sent", 0) + 2 * bin(engines(core)).count("1")
-        arrived = [("arr%d" % t, 2 * bin(engines(src)).count("1"))]
-        for call in later:
-            call()
-        if first:
-            qz(T.qv[:], T.sv[:], T.vt[:], ["vt"], ["qv"])
-        quant("c", T.ct, 0, 128, cts, ["qc"])
-        mmc(0, "t", 256, "c", 0, 128, ["qt2", "qc"])
-        unpack_own(1, [0, 2, 1, 3])
-        scan(T.x2[:], bank(0, 0, 64), T.kd[:], A.min, A.add, ["B0", "kd"], ["x2"])
-        cp(T.k16[:], T.x2[:, 3:64:4], ["x2"], ["k16"])
-        cp(T.tkb[:], T.m128[:].indirect(T.k16[:]), ["m0", "m1", "m2", "m3", "k16"], ["tk"])
-        scan(T.wk[:], T.cw8[:], T.tkb[:], A.add, A.min, ["cw8", "cw8b", "tk"], ["wk"])
-        ts(T.k8[:], T.wk[:, 7:256:8], col(PAR), A.add, ["wk", "par"], ["k8"], 2.0, A.mult)
-        order("V", ["k8", "B2", "B3", "B4", "B5"], (), ())
-        order("A", ["k8"], (), ())
-        order("P", ["qw", "sw"], ["B0", "B1", "B6", "B7"], ())
-        gb = [0, 1, 6, 7]
-        for k in (0, 2, 1, 3):
-            mmc(gb[k], "d", 128 * k, "l%d" % t, 0, 128, ["qd%d" % k], arrived if k == 0 else ())
-        for k in (0, 2):
-            cp(plane(T.ga, T.gb, k, 0, 128), bank(gb[k], 0, 128), ["B%d" % gb[k]], ["gp%d" % k])
-        for k in (1, 3):
-            act(plane(T.ga, T.gb, k, 0, 128), bank(gb[k], 0, 128), ["B%d" % gb[k]], ["gp%d" % k])
-        rb = [gb, [2, 3, 4, 5]]
-        gab = (T.ga, T.gb)
+            tt(look(256), T.et[:, k:512:2], T.ff[:, 2 * PL * k:2 * PL * k + 2 * PL].indirect(T.b8[:]), T.ap[:, 256 * k:256 * k + 256],
+               A.subtract, fk(k) + fk(k + 2) + ["b8", "ap%d" % k, "ap%d" % (k + 2)], ["et%d" % k])
+        window("e%d" % t, 0, T.et, 0, ["et0", "et1"])
+        wrote_e = calls[-1][3]
+        wrote_e.append("qe%d" % t)
+        send(t)
+        ts(1, T.rr[:], T.gw[:, 15:256:16], NEAR, A.add, gw, ["rr"], NEAR, A.subtract)
+        tt(1, T.fr[:], T.gw[:, 15:256:16], T.rr[:], A.subtract, gw + ["rr"], ["fr"])
+        for s in range(4):
+            f = T.ct[:, 1 + 4 * s:256:16]
+            ts(1, f, T.fr[:], s / 8.0, A.is_equal, ["fr"], ["cf%d" % s])
+            scan(1, T.ct[:, 19 + 4 * s:272:16], f, f, A.add, A.max, ["cf%d" % s], ["cr%d" % s])
+        window("c", 0, T.ct, 0, cts)
+        mmc(4, "k", 256, "c", 0, 128, ["qk2", "qc0"])
+        scan(64, T.x2[:], bank(4, 0, 64), T.kd[:], A.min, A.add, ["B4", "kd"], ["x2"])
+        cp(1, T.ki[:], T.x2[:, 3:64:4], ["x2"], ["ki"])
+        ts(1, T.ki[:], T.ki[:], 127, A.bitwise_and, [], ["ki"])
+        ts(1, T.ki[:], T.ki[:], 129.0, A.mult, [], ["ki"])
+        ts(1, T.ki[:], T.ki[:], 5, A.arith_shift_right, [], ["ki"], 127, A.bitwise_and)
+        cp(1, T.kk[:, 0:16], T.ki[:], ["ki"], ["kk"])
+        ts(1, T.kk[:, 16:24], T.ki[:, 8:16], 128.0, A.add, ["ki"], ["kk2"])
+        rb = [[0, 1, 6, 7], [2, 3, 4, 5]]
+        for k in PLANES:
+            unpack(1, k, 2 + k)
+        for q, k in zip("VVVA", PLANES):
+            b, lo = rb[0][k], 128 * PLANES.index(k)
+            mmc(b, "d", 128 * k, "l%d" % t, 0, 128, ["qd%d" % k, "came%d" % t])
+            (cp if q == "V" else act)(128, T.gg[:, lo:lo + 128], bank(b, 0, 128), ["B%d" % b], ["gp%d" % k])
+        for i, k in enumerate(PLANES):
+            tt(look(128), T.zt[:, k:512:4], T.gg[:, 128 * i:128 * i + 128].indirect(T.kk[:, 0:8]), T.ff[:, PL * i:PL * i + 128],
+               A.add, ["gp%d" % k, "kk", "f0%d" % k], ["z0%d" % k])
         for k in range(2):
-            act(T.zg[:, 256 * k:256 * k + 256], gab[k][:].indirect(T.k8[:, 16:32]), ["gp%d" % k, "gp%d" % (k + 2), "k8"], ["zg%d" % k])
-
-        def layer(h):
-            quant("z", T.zt, 128 * h, 128 * h + 128, ["z%d%d" % (h, k) for k in range(4)], ["qz%d" % h])
-            for k in (0, 2, 1, 3):
+            v = slice(256 * k, 256 * k + 256)
+            act(look(256) - 60, T.zg[:, v], T.gg[:, v].indirect(T.kk[:, 8:24]), ["gp%d" % k, "gp%d" % (k + 2), "kk", "kk2"], ["zg%d" % k])
+        for i, k in enumerate(PLANES):
+            tt(128, T.zt[:, 512 + k:1024:4], bank(2 + k, 0, 128), T.zg[:, 128 * i:128 * i + 128], A.add,
+               ["B%d" % (2 + k), "zg%d" % (k % 2)], ["z1%d" % k])
+        for h in range(2):
+            window("z", h, T.zt, 512 * h, ["z%d%d" % (h, k) for k in range(4)])
+            for k in PLANES:
+                v = slice(512 * h + k, 512 * h + 512, 4)
                 mmc(rb[h][k], "w", 128 * k, "z", 128 * h, 128 * h + 128, ["qw", "sw", "qz%d" % h])
-                act(T.rl[:, 512 * h + k:512 * h + 512:4], bank(rb[h][k], 0, 128), ["B%d" % rb[h][k]],
-                    ["rl%d%d" % (h, k)], AF.Relu, 0.015625)
+                act(128, T.rl[:, v], bank(rb[h][k], 0, 128), ["B%d" % rb[h][k]], ["rl%d%d" % (h, k)], AF.Relu, 0.015625)
+                tt(256, T.xn[:, v], T.rl[:, v], T.zt[:, v], A.add, ["rl%d%d" % (h, k), "z%d%d" % (h, k)], ["xn%d%d" % (h, k)])
+        for h in range(2):
+            window("x", h, T.xn, 512 * h, ["xn%d%d" % (h, k) for k in range(4)])
+        if t < R - 1:
+            signs(0, False)
+            for k in PLANES:
+                own(0, k, 2 + k)
 
-        def addz(ks):
-            for k in ks:
-                tt(T.zt[:, 512 + k:1024:4], bank(2 + k, 0, 128), T.zg[:, 256 * (k % 2) + k // 2:256 * (k % 2) + 256:2], A.add,
-                   ["B%d" % (2 + k), "zg%d" % (k % 2)], ["z1%d" % k])
+    for h in range(2):
+        lo, hi = 128 * h, 128 * h + 128
+        mmc(h, "v", 0, "x", lo, hi, ["qv0", "qx%d" % h])
+        (cp if h else act)(128, T.yo[:, lo:hi], bank(h, 0, 128), ["B%d" % h], ["yo%d" % h])
+        dma("SA"[h], T.oc[:, 4 * lo:4 * hi], T.qx[:, lo:hi].bitcast(dt.uint8), ["qx%d" % h])
+        dma("AS"[h], T.y[:, lo:hi], T.yo[:, lo:hi], ["yo%d" % h])
+    for k in range(4):
+        dma("SAAA"[k], T.osc[4 * k:4 * k + 4, :], T.sx[32 * k:32 * k + 4, :], ["qx0", "qx1"])
 
-        def add(h, *ks):
-            v = slice(512 * h + ks[0], 512 * h + 512, 4 // len(ks))
-            tt(T.xn[:, v], T.rl[:, v], T.zt[:, v], A.add,
-               ["%s%d%d" % (n, h, k) for k in ks for n in ("rl", "z")], ["xn%d%d" % (h, k) for k in ks])
-
-        def newx(h):
-            quant("x", T.xn, 128 * h, 128 * h + 128, ["xn%d%d" % (h, k) for k in range(4)], ["qx%d" % h])
-
-        def store(h, qc, qs):
-            lo, hi = 128 * h, 128 * h + 128
-            dma(qc, T.oc[:, 4 * lo:4 * hi], T.qx[:, lo:hi].bitcast(dt.uint8), ["qx%d" % h])
-            for k in range(len(qs)):
-                dma(qs[k], T.osc[4 * k:4 * k + 4, :], T.sx[32 * k:32 * k + 4, :], ["qx0", "qx1"])
-
-        for k in range(2):
-            tt(T.zt[:, k:512:2], gab[k][:].indirect(T.k8[:, 0:16]), fab[k][0][:, 0:256], A.add,
-               ["gp%d" % k, "gp%d" % (k + 2), "k8"] + fab[k][1], ["z0%d" % k, "z0%d" % (k + 2)])
-        addz([0])
-        layer(0)
-        addz([2, 1, 3])
-        layer(1)
-        for k in (0, 2, 1, 3):
-            add(0, k)
-        add(1, 0)
-        newx(0)
-        add(1, 2)
-        if t == R - 1:
-            mmc(0, "v", 0, "x", 0, 128, ["qv", "qx0"])
-            store(0, "S", "")
-            act(T.yo[:, 0:128], bank(0, 0, 128), ["B0"], ["yo0"])
-            dma("A", T.y[:, 0:128], T.yo[:, 0:128], ["yo0"])
-            add(1, 1, 3)
-            newx(1)
-            mmc(1, "v", 0, "x", 128, 256, ["qv", "qx1"])
-            store(1, "A", "SAAA")
-            cp(T.yo[:, 128:256], bank(1, 0, 128), ["B1"], ["yo1"])
-            dma("S", T.y[:, 128:256], T.yo[:, 128:256], ["yo1"])
-        else:
-            scores(0)
-            unpack_own(0, [0, 2, 1])
-            act(T.sg[:], bank(1, 0, 128), ["B1"], ["sg"], AF.Sign)
-            act(T.ct[:, 1:512:4], T.sg[:], ["sg"], cts[:4], AF.Relu)
-            copy_own(0, [0, 2, 1])
-            add(1, 1, 3)
-            signs(0)
-            newx(1)
-
+    if not ORDER:
+        ORDER.extend(schedule(calls))
+    for i in ORDER:
+        order(calls[i][0], calls[i][2], calls[i][3])
+        calls[i][1]()
     for s, n in sorted(count.items()):
         if not any(clock[q].get(s, 0) >= n for q in clock):
             g.wait_ge(T.sem[s], n)

from concourse.mybir import dt, AluOpType, AxisListType, ActivationFunctionType

N, C, M, R = 8, 256, 32, 3
X4, U8, BF, F16, F32, I32, U16 = "float8_e4m3fn_x4", "uint8", "bfloat16", "float16", "float32", "int32", "uint16"
STEP = 1.0 / 512
JOINT = 5
OWN = 2048.0
HOLD = 256.0
NEAR = 1.5 * 2.0 ** 23
PL = 272
PLANES = (0, 2, 1, 3)
HAND = 245
LEAST = {"V": 64, "A": 64, "P": 0, "G": 0, "S": 0}
EXTRA = {"V": 10, "A": 80, "P": 40, "G": 170, "S": 0}
LATE = {"V": 0, "A": 30, "P": 70, "G": 10}
LOAD, SEND = 2100, 1700
SLACKS = (10, 10, 0, 20, 10, 40, 5, 15)
AHEAD = 600
ORDER = []

SCRATCH = {"ps": ("psum", [128, 4096], F32)}
for _d, _l in (
    (BF, "xt:1024 ut:512 vt:512 xn:1024 zt:1024 et:512 tk:528 pp:528 tp:528 la:528 iot:256 down:256 cw:128 cw8:128 half:8 "
         "gri:256 sg:128 bits:16 hv:16 ot:512 ct:528 nt:512 rt:1024 tf:384 ones:256 mate:272 brow:128 "
         "ff:%d ap:512 gg:512 zg:512" % (4 * PL)),
    (F16, "ramp:1088 th:1088 mk:256 fl:272 two:272 wb8:128"),
    (F32, "rf:8 col:16 sm8:8 gw:256 rr:16 fr:16 back:8 ya:8 kd:64 x2:64 rl:1024 yo:256 tv:384"),
    (I32, "rint:8 ki:16"),
    (U16, "t16:16 a16:8 b8:16 kk:24"),
):
    for _e in _l.split():
        SCRATCH[_e.split(":")[0]] = ("sbuf", [128, int(_e.split(":")[1])], _d)
for _e in ("x:256 z:256 u:128 v:128 w:512 k:384 t:256 p:256 d:512 o:128 b:256 n:128 c:128 "
           "e0:128 e1:128 e2:128 l0:128 l1:128 l2:128").split():
    SCRATCH["q" + _e.split(":")[0]] = ("sbuf", [128, int(_e.split(":")[1])], X4)
    SCRATCH["s" + _e.split(":")[0]] = ("sbuf", [128, int(_e.split(":")[1])], U8)

SEMAPHORES = ["cV", "cA", "cP", "cG", "sent"] + ["arr%d" % _t for _t in range(R)] + ["d%d" % _i for _i in range(24)]


def schedule(calls):
    before, wrote, reads = [], {}, {}
    for i, (q, _, r, w, busy, late) in enumerate(calls):
        pre = set()
        for k in r:
            pre |= set(wrote.get(k, ())) | (set(j for j in reads.get(k, ()) if calls[j][0] != q) if k[0] == "B" else set())
        for k in w:
            pre |= set(wrote.get(k, ())) | set(reads.get(k, ()))
        before.append(sorted(pre))
        for k in r:
            reads.setdefault(k, []).append(i)
        for k in w:
            wrote[k], reads[k] = [i], []
    after = [[] for _ in calls]
    for i, pre in enumerate(before):
        for j in pre:
            after[j].append(i)
    queue, busy, late = [[c[k] for c in calls] for k in (0, 4, 5)]

    def place(rest, before, lag, way, slack):
        free, start = {q: 0 for q in LEAST}, {}
        while rest:
            soon = dict(start)
            for i in rest:
                soon[i] = max([free[queue[i]], lag(None, i)] + [soon[j] + busy[j] + lag(j, i) for j in before[i]])
            picks = []
            for q in LEAST:
                mine = [i for i in rest if queue[i] == q]
                now = min([soon[i] for i in mine] + [1e9])
                near = [i for i in mine if soon[i] <= now + AHEAD]
                end = {i: max([soon[i] + way[i]] + [max(soon[j], soon[i] + busy[i]) + way[j] for j in near if j != i]) for i in near}
                if near:
                    picks.append(min((soon[i], -way[i], i) for i in near if end[i] <= min(end.values()) + slack))
            i = min([p for p in picks if all(j in start for j in before[p[2]])] or
                    [(soon[j], 0, j) for j in rest if all(k in start for k in before[j])])[2]
            start[i] = soon[i]
            free[queue[i]] = soon[i] + busy[i]
            rest.remove(i)
        return start

    ids = list(range(len(calls)))
    way = [0] * len(calls)
    for i in reversed(ids):
        way[i] = busy[i] + late[i] + max([HAND + way[j] for j in after[i]] + [0])
    tries = []
    for slack in SLACKS:
        start = place(ids[:], before, lambda j, i: 0 if j is None else late[j] + HAND, way, slack)
        tries.append((max(start[i] + busy[i] + late[i] for i in ids), sorted(ids, key=lambda i: (start[i], i))))
        back = place(ids[::-1], after, lambda j, i: late[i] + (0 if j is None else HAND), [start[i] + busy[i] for i in ids], slack)
        way = [back[i] + busy[i] for i in ids]
    return min(tries)[1]


def rank_program(g, core, T, topo):
    rank = T.rank_of(core)
    if rank is None:
        return
    A, AF, AX = AluOpType, ActivationFunctionType, AxisListType.X
    eng = {"V": g.vector, "A": g.scalar, "P": g.tensor, "G": g, "S": g.sync}
    calls = []
    clock = {q: {} for q in eng}
    count = {}
    seen = {}
    wrote, reads = {}, {}

    def order(q, r, w):
        need = {}
        for k in r:
            for e in ([wrote[k]] if k in wrote else []) + ([x for x in reads.get(k, []) if x[2] != q] if k[0] == "B" else []):
                need[e[0]] = max(need.get(e[0], 0), e[1])
        for k in w:
            for e in ([wrote[k]] if k in wrote else []) + reads.get(k, []):
                need[e[0]] = max(need.get(e[0], 0), e[1])
        todo = sorted(need.items(), key=lambda e: (e[0][:3] == "arr", e))
        for s, n in todo:
            if any(seen.get(o, {}).get(s, 0) >= n for o in todo if o[0] != s):
                continue
            if clock[q].get(s, 0) < n:
                eng[q].wait_ge(T.sem[s], n)
                clock[q][s] = n
                for s2, n2 in seen.get((s, n), {}).items():
                    clock[q][s2] = max(clock[q].get(s2, 0), n2)

    def done(q, s, n, r, w):
        count[s] = n
        seen[(s, n)] = dict(clock[q])
        for k in r:
            reads.setdefault(k, []).append((s, n, q))
        for k in w:
            wrote[k] = (s, n, q)
            reads[k] = []

    def op(q, c, fn, r, w):
        def issue():
            s = "c" + q
            fn().then_inc(T.sem[s], 1)
            done(q, s, count.get(s, 0) + 1, r, w)
        calls.append((q, issue, r, w, max(c, LEAST[q]) + EXTRA[q], LATE[q]))

    def dma(q, out, in_, r=(), w=()):
        def issue():
            s = "d%d" % sum(k[0] == "d" for k in count)
            eng[q].dma_start(out, in_).then_inc(T.sem[s], 16)
            done(q, s, 16, r, w)
        calls.append((q, issue, r, w, 60, LOAD))

    V, S_ = g.vector, g.scalar
    look = lambda n: 60 + 7 * n // 5

    def ts(c, out, in0, s1, o0, r, w, s2=None, o1=None):
        if o1 is None:
            op("V", c, lambda: V.tensor_scalar(out, in0, s1, None, o0), r, w)
        else:
            op("V", c, lambda: V.tensor_scalar(out, in0, s1, s2, o0, o1), r, w)

    def tt(c, out, a, b, o, r, w):
        op("V", c, lambda: V.tensor_tensor(out, a, b, o), r, w)

    def cp(c, out, in_, r, w):
        op("V", c, lambda: V.tensor_copy(out, in_), r, w)

    def ms(c, out, x, w):
        op("V", c, lambda: V.memset(out, x), (), w)

    def scan(c, out, d0, d1, o0, o1, r, w, init=0.0):
        op("V", c, lambda: V.tensor_tensor_scan(out, d0, d1, init, o0, o1), r, w)

    def qz(q, s, t, r, w):
        op("V", 150, lambda: V.quantize_mx(q, s, t), r, w)

    def act(c, out, in_, r, w, f=None, scale=1.0, bias=None):
        if f is None:
            op("A", c, lambda: S_.activation(out, in_, AF.Copy), r, w)
        elif bias is None:
            op("A", c, lambda: S_.activation(out, in_, f, scale=scale), r, w)
        else:
            op("A", c, lambda: S_.activation(out, in_, f, bias=bias, scale=scale), r, w)

    def lin(c, out, in_, scale, bias, r, w):
        act(c, out, in_, r, w, AF.Identity, scale, bias)

    def iota(n, out, pat, base, cm, w, small=True):
        if small:
            op("G", 2 * n, lambda: g.iota(out, pat, base, cm, allow_small_or_imprecise_dtypes=True), (), w)
        else:
            op("G", 2 * n, lambda: g.iota(out, pat, base, cm), (), w)

    def sel(n, out, in_, pat, cmp, fill, cm, r, w, base=0):
        op("G", 2 * n + 50, lambda: g.affine_select(out, in_, pat, cmp, fill, base, cm), r, w)

    def bank(b, lo, hi, step=1):
        return T.ps[:, 512 * b + lo:512 * b + hi:step]

    def mmc(b, lname, la, rname, ra, rb, r):
        op("P", 2 * (rb - ra + 16) // 3, lambda: g.tensor.matmul_mx(
            bank(b, 0, rb - ra), T["q" + lname][:, la:la + 128], T["s" + lname][:, la:la + 128],
            T["q" + rname][:, ra:rb], T["s" + rname][:, ra:rb], True, True), r, ["B%d" % b])

    def engines(c):
        i, m = T.rank_of(c), -1
        for t in range(R):
            m &= topo.mask(c, T.cores[(i + 1 + t) % N])
        return m

    def send(t):
        dst, src = T.cores[(rank + 1 + t) % N], T.cores[(rank - 1 - t) % N]
        rid, pid = topo.addr(dst)[0], topo.addr(dst)[1]

        def issue():
            g.remote_dma(T["ql%d" % t][:].bitcast(dt.uint8), T["qe%d" % t][:].bitcast(dt.uint8),
                         T.sem["arr%d" % t], T.sem.sent, pid, rid, engines(core))
            g.remote_dma(T["sl%d" % t][:], T["se%d" % t][:], T.sem["arr%d" % t], T.sem.sent, pid, rid, engines(core))
            count["sent"] = count.get("sent", 0) + 2 * bin(engines(core)).count("1")
            wrote["came%d" % t] = ("arr%d" % t, 2 * bin(engines(src)).count("1"), "G")
        calls.append(("G", issue, ["qe%d" % t], ["came%d" % t], 400, SEND))

    def window(name, k, src, lo, r):
        qz(T["q" + name][:, 128 * k:128 * k + 128], T["s" + name][:, 128 * k:128 * k + 128], src[:, lo:lo + 512], r, ["q%s%d" % (name, k)])

    col = lambda i: T.col[:, i:i + 1]
    K16, G16, S16, R8, R16 = [T.rf[:, i:i + 1] for i in range(5)]
    POW, PAR, E0, W3, ACOL, BCOL, WCOL, CNT0, TCOL, UP8, UP16, TMP, TM2 = range(13)
    blk, tri = T.tk[:, 3:512:4], T.tk[:, 1:512:4]
    tks = ["k1", "k2", "tri", "blk", "tkz"]
    cts = ["cf%d" % s for s in range(4)] + ["cr%d" % s for s in range(4)]
    tps = ["tp2", "tp3"]
    sns = ["sn0", "sn2", "snz"]
    gw = ["gw0", "gw1"]

    dma("S", T.xt[:, 0:512], T.x[:, 0:512], (), ["X0"])
    dma("A", T.ut[:], T.u[:], (), ["ut"])
    dma("S", T.xt[:, 512:1024], T.x[:, 512:1024], (), ["X1"])
    dma("S", T.qw[:].bitcast(dt.uint8), T.wc[:], ["X1"], ["qw"])
    dma("S", T.sw[:], T.ws[:], ["X1"], ["sw"])
    dma("S", T.vt[:], T.v[:], ["X1"], ["vt"])

    iota(8, T.rint[:], [[0, 8]], 0, 16, ["ri%d" % i for i in range(5)], False)
    iota(256, T.gri[:], [[16, 8], [0, 32]], 0, 0, ["gri"])
    iota(516, T.pp[:, 0:516], [[2, 129], [1024, 2], [-128, 2]], -1022, -1, ["pp"])
    ms(128, T.ones[:], 1.0, ["ones"])
    ms(1, T.fl[:, 0:16], STEP, ["flz"])
    ms(1, T.two[:, 256:272], -1024.0, ["twoz"])
    ms(264, T.rt[:, 0:528], 0.0, ["rt0"])
    lin(528, T.tp[:], T.rt[:, 0:528], 0.0, None, ["rt0", "rt1"], tps)
    lin(512, T.rt[:, 512:1024], T.rt[:, 0:512], 0.0, None, ["rt0"], ["rt1"])
    scan(128, T.iot[:], T.ones[:], T.ones[:], A.mult, A.add, ["ones"], ["iot"], -1.0)
    ts(1, T.rint[:, 0:1], T.rint[:, 0:1], 48, A.bitwise_and, [], ["ri0"])
    ts(1, T.rint[:, 1:2], T.rint[:, 1:2], 4, A.arith_shift_right, [], ["ri1"], 240, A.bitwise_and)
    ts(1, T.rint[:, 2:3], T.rint[:, 2:3], 2, A.arith_shift_right, [], ["ri2"], 48, A.bitwise_and)
    ts(1, T.rint[:, 3:4], T.rint[:, 3:4], 224, A.bitwise_and, [], ["ri3"])
    ts(1, T.rint[:, 4:5], T.rint[:, 4:5], 240, A.bitwise_and, [], ["ri4"])
    ms(1, T.half[:], 0.5, ["half"])
    cp(1, T.rf[:], T.rint[:], ["ri%d" % i for i in range(5)], ["rf"])
    ms(1, T.tk[:, 512:528], 0.0, ["tkz"])
    ms(1, T.tp[:, 2:516:4], 1.0, ["tp2"])
    ms(1, T.tp[:, 3:516:4], 1.0, ["tp3"])
    sel(516, T.la[:, 0:516], T.tp[:, 0:516], [[1, 516]], A.is_equal, 0.0, -4, tps, ["la"], -3)
    iota(256, T.down[:], [[0, 16], [-16384, 16]], 0, 0, ["down"])
    iota(256, T.nt[:, 1:512:2], [[0, 256]], 0, 0, ["snz"])
    iota(128, T.tv[:, 256:384], [[0, 128]], 0, 0, ["tvz"])
    iota(128, T.tf[:, 256:384], [[0, 128]], 0, 0, ["ftz"])
    iota(8, T.back[:], [[2, 8]], -7, 0, ["back"])
    iota(16, T.mate[:, 256:272], [[0, 16]], C, 0, ["matez"])
    for k in range(4):
        iota(16, T.ff[:, PL * k + C:PL * k + PL], [[0, PL - C]], 0, 0, ["fz%d" % k])
    iota(528, T.ct[:], [[0, 528]], 0, 0, cts)
    iota(64, T.kd[:], [[0, 64]], -1, 0, ["kd"])
    iota(16, T.kd[:, 3:64:4], [[0, 16]], int(OWN) + 3, 0, ["kd"])
    ts(1, T.sm8[:], T.iot[:, 0:128:16], G16, A.is_lt, ["iot", "rf"], ["s8"], 1.0, A.add)
    ts(1, col(E0), R16, 0.0, A.is_equal, ["rf"], ["e0"], 1.0 / 32, A.mult)
    act(1, col(W3), R16, ["rf"], ["w3"], AF.Relu, -1.0 / 512, 3.0 / 32)
    op("V", 1, lambda: V.tensor_reduce(col(POW), T.sm8[:], AX, A.mult, negate=True), ["s8"], ["pow"])
    ts(128, T.tk[:, 1:512:2], T.gri[:], G16, A.is_equal, ["gri", "rf"], ["blk", "tri"], 4.0, A.mult)
    ts(1, col(ACOL), col(E0), col(POW), A.mult, ["e0", "pow"], ["acol"], -32.0, A.mult)
    ts(1, col(WCOL), col(E0), col(W3), A.add, ["e0", "w3"], ["wcol"], 128.0, A.mult)
    ts(1, col(BCOL), col(E0), -3.0, A.mult, ["e0", "w3"], ["bcol"], col(W3), A.add)
    lin(1, T.col[:, UP8:UP16 + 1], T.rf[:, 3:5], 1024.0, 8192.0, ["rf"], ["up"])
    lin(128, T.tk[:, 2:512:4], blk, col(WCOL), None, ["blk", "wcol"], ["k2"])
    lin(128, T.tk[:, 0:512:4], blk, col(BCOL), col(ACOL), ["blk", "bcol", "acol"], ["k1"])
    lin(1, col(TMP), R16, 16.0, NEAR - 15 * HOLD, ["rf"], ["tmp"])
    lin(1, col(TM2), R8, -8.0 - PL / 16.0, None, ["rf"], ["tm2"])
    lin(1, col(CNT0), K16, 1.0, 8.0 - 2 * STEP, ["rf"], ["cnt0"])
    lin(1, col(TCOL), col(TMP), 1.0, col(POW), ["pow", "tmp"], ["tcol"])
    lin(1, col(PAR), R16, PL / 16.0, col(TM2), ["rf", "tm2"], ["par"])
    ts(64, T.cw[:], T.down[:, 0:128], col(UP16), A.add, ["down", "up"], ["cw"], -HOLD, A.max)
    ts(64, T.cw8[:], T.down[:, 0:256:2], col(UP8), A.add, ["down", "up"], ["cw8"], -HOLD, A.max)
    act(516, T.pp[:, 0:516], T.pp[:, 0:516], [], ["pp"], AF.Relu)
    for c in range(8):
        lin(128, T.ramp[:, 136 * c:136 * c + 129], T.iot[:, 0:129], 1.0 / 128, 7.0 - 2 * c, ["iot"], ["ramp%d" % c])
    window("u", 0, T.ut, 0, ["ut"])
    window("v", 0, T.vt, 0, ["vt"])
    for k in range(2):
        window("x", k, T.xt, 512 * k, ["X%d" % k])
        window("k", k, T.tk, 2 * k, tks)
        window("t", k, T.tp, 2 - 2 * k, tps)
        window("p", k, T.pp, 2 - 2 * k, ["pp"])
    for k in PLANES:
        window("d", k, T.la, 3 - k, ["la"])
    sel(128, tri, blk, [[1, 128]], A.is_gt, 0.0, -1, ["blk"], ["tri"])
    sel(128, tri, tri, [[1, 128]], A.not_equal, -OWN, -1, [], ["tri"])
    window("k", 2, T.tk, 0, tks)

    def unpack(h, k, b):
        hs = (0, 1) if h == 2 else (h,)
        mmc(b, "d", 128 * k, "x", 128 * hs[0], 128 * hs[-1] + 128, ["qd%d" % k] + ["qx%d" % i for i in hs])

    def own(h, k, b):
        hs = (0, 1) if h == 2 else (h,)
        lo, hi = 128 * hs[0], 128 * hs[-1] + 128
        unpack(h, k, b)
        act(hi - lo, T.ff[:, PL * PLANES.index(k) + lo:PL * PLANES.index(k) + hi], bank(b, 0, hi - lo), ["B%d" % b],
            ["f%d%d" % (i, k) for i in hs])

    def signs(h, first):
        b0, b1, v = 6 * h, 6 * h + 1, slice(128 * h, 128 * h + 128)
        mmc(b0, "x", 128 * h, "u", 0, 128, ["qx%d" % h, "qu0"])
        mmc(b1, "u", 0, "x", 128 * h, 128 * h + 128, ["qx%d" % h, "qu0"])
        ts(1, T.bits[:, 8 * h:8 * h + 8], bank(b0, 0, 128, 16), 0.0, A.is_gt, ["B%d" % b0], ["bits%d" % h])
        scan(1, T.hv[:, 8 * h:8 * h + 8], T.half[:], T.bits[:, 8 * h:8 * h + 8], A.mult, A.add, ["half", "bits%d" % h], ["hv%d" % h])
        ts(128, T.ot[:, h:512:2], T.iot[:], 1.0 / 128, A.mult, ["iot", "hv%d" % h], ["ot%d" % h],
           T.hv[:, 8 * h + 7:8 * h + 8], A.is_equal)
        ts(128, T.rt[:, 512 * h:512 * h + 512:4], bank(b1, 0, 128), 0.0, A.is_gt, ["B%d" % b1], ["rt%d" % h])
        window("b", h, T.rt, 512 * h, ["rt%d" % h])
        mmc(b0, "k", 0, "b", 128 * h, 128 * h + 128, ["qk0", "qb%d" % h])
        mmc(b1, "k", 128, "b", 128 * h, 128 * h + 128, ["qk1", "qb%d" % h])
        scan(128, T.gw[:, v], T.cw[:], bank(b0, 0, 128), A.add, A.min, ["cw", "B%d" % b0], ["gw%d" % h])
        ts(128, T.mk[:, v], bank(b1, 0, 128), S16, A.not_equal, ["B%d" % b1, "rf"], ["mk%d" % h], STEP - 1.0, A.add)

    signs(0, True)
    for t in range(R):
        first = t == 0
        signs(1, first)
        window("o", 0, T.ot, 0, ["ot0", "ot1"])
        for k in range(2):
            mmc(2 + k, "t", 128 * k, "o", 0, 128, ["qt%d" % k, "qo0"])
        for k in range(2):
            mmc(4 + k, "p", 128 * k, "o", 0, 128, ["qp%d" % k, "qo0"])
        for k in range(2):
            ts(128, T.tv[:, k:256:2], bank(2 + k, 0, 128), 0.0, A.is_equal, ["B%d" % (2 + k)], ["tv%d" % k], STEP - 1.0, A.add)
        ts(1, T.t16[:], T.gw[:, 15:256:16], NEAR, A.add, gw + ["tcol"], ["t16"], col(TCOL), A.subtract)
        for k in range(2):
            act(128, T.nt[:, 2 * k:512:4], bank(4 + k, 0, 128), ["B%d" % (4 + k)], ["sn%d" % (2 * k)], AF.Relu, -1.0, 2.0)
        for k, b in zip(PLANES, (0, 1, 6, 7)):
            own(2 if first else 1, k, b)
        window("n", 0, T.nt, 0, sns)
        for k in range(2):
            mmc(2 + k, "t", 128 * k, "n", 0, 128, ["qt%d" % k, "qn0"])
            act(128, T.tf[:, k:256:2], bank(2 + k, 0, 128), ["B%d" % (2 + k)], ["ft%d" % k])
        act(look(256) - 60, T.mate[:, 0:256], T.tf[:].indirect(T.t16[:]), ["ft0", "ft1", "ftz", "t16"], ["mate"])
        tt(look(256), T.fl[:, 16:272], T.tv[:].indirect(T.t16[:]), T.mk[:], A.max, ["tv0", "tv1", "tvz", "t16", "mk0", "mk1"], ["fl"])
        scan(128, T.two[:, 0:256], T.fl[:, 15:271], T.fl[:, 16:272], A.add, A.add, ["flz", "fl", "cnt0"], ["two"], col(CNT0))
        for c in range(8):
            scan(65, T.th[:, 136 * c:136 * c + 129], T.ramp[:, 136 * c:136 * c + 129], T.two[:, 1:258:2], A.min, A.max,
                 ["ramp%d" % c, "two", "twoz"], ["th%d" % c], 16.0)
        tt(1, T.ya[:, 0:JOINT], T.th[:, 128:136 * JOINT:136], T.back[:, 0:JOINT], A.add,
           ["th%d" % c for c in range(JOINT)] + ["back"], ["ya"])
        ts(1, T.a16[:, 0:JOINT], T.ya[:, 0:JOINT], float(C), A.mult, ["ya"], ["a16"])
        for c in range(JOINT, 8):
            ts(1, T.a16[:, c:c + 1], T.th[:, 136 * c + 128:136 * c + 129], 2.0 * c - 7, A.add, ["th%d" % c], ["a16%d" % c],
               float(C), A.mult)
        a16 = ["a16"] + ["a16%d" % c for c in range(JOINT, 8)]
        fk = lambda k: ["f0%d" % k, "f1%d" % k, "fz%d" % PLANES.index(k)]
        for i, k in enumerate(PLANES):
            act(look(128) - 60, T.ap[:, 256 * (k % 2) + k // 2:256 * (k % 2) + 256:2], T.ff[:, PL * i:PL * i + PL].indirect(T.a16[:]),
                fk(k) + a16, ["ap%d" % k])
        cp(look(128), T.brow[:], T.mate[:].indirect(T.a16[:]), ["mate", "matez"] + a16, ["brow"])
        scan(64, T.wb8[:], T.cw8[:], T.brow[:], A.add, A.min, ["cw8", "brow"], ["wb8"])
        ts(1, T.b8[:], T.wb8[:, 7:128:8], col(PAR), A.add, ["wb8", "par"], ["b8"], 7 * HOLD, A.add)
        for k in range(2):
            tt(look(256), T.et[:, k:512:2], T.ff[:, 2 * PL * k:2 * PL * k + 2 * PL].indirect(T.b8[:]), T.ap[:, 256 * k:256 * k + 256],
               A.subtract, fk(k) + fk(k + 2) + ["b8", "ap%d" % k, "ap%d" % (k + 2)], ["et%d" % k])
        window("e%d" % t, 0, T.et, 0, ["et0", "et1"])
        wrote_e = calls[-1][3]
        wrote_e.append("qe%d" % t)
        send(t)
        ts(1, T.rr[:], T.gw[:, 15:256:16], NEAR, A.add, gw, ["rr"], NEAR, A.subtract)
        tt(1, T.fr[:], T.gw[:, 15:256:16], T.rr[:], A.subtract, gw + ["rr"], ["fr"])
        for s in range(4):
            f = T.ct[:, 1 + 4 * s:256:16]
            ts(1, f, T.fr[:], s / 8.0, A.is_equal, ["fr"], ["cf%d" % s])
            scan(1, T.ct[:, 19 + 4 * s:272:16], f, f, A.add, A.max, ["cf%d" % s], ["cr%d" % s])
        window("c", 0, T.ct, 0, cts)
        mmc(4, "k", 256, "c", 0, 128, ["qk2", "qc0"])
        scan(64, T.x2[:], bank(4, 0, 64), T.kd[:], A.min, A.add, ["B4", "kd"], ["x2"])
        cp(1, T.ki[:], T.x2[:, 3:64:4], ["x2"], ["ki"])
        ts(1, T.ki[:], T.ki[:], 127, A.bitwise_and, [], ["ki"])
        ts(1, T.ki[:], T.ki[:], 129.0, A.mult, [], ["ki"])
        ts(1, T.ki[:], T.ki[:], 5, A.arith_shift_right, [], ["ki"], 127, A.bitwise_and)
        cp(1, T.kk[:, 0:16], T.ki[:], ["ki"], ["kk"])
        ts(1, T.kk[:, 16:24], T.ki[:, 8:16], 128.0, A.add, ["ki"], ["kk2"])
        rb = [[0, 1, 6, 7], [2, 3, 4, 5]]
        for k in PLANES:
            unpack(1, k, 2 + k)
        for q, k in zip("VVVA", PLANES):
            b, lo = rb[0][k], 128 * PLANES.index(k)
            mmc(b, "d", 128 * k, "l%d" % t, 0, 128, ["qd%d" % k, "came%d" % t])
            (cp if q == "V" else act)(128, T.gg[:, lo:lo + 128], bank(b, 0, 128), ["B%d" % b], ["gp%d" % k])
        for i, k in enumerate(PLANES):
            tt(look(128), T.zt[:, k:512:4], T.gg[:, 128 * i:128 * i + 128].indirect(T.kk[:, 0:8]), T.ff[:, PL * i:PL * i + 128],
               A.add, ["gp%d" % k, "kk", "f0%d" % k], ["z0%d" % k])
        for k in range(2):
            v = slice(256 * k, 256 * k + 256)
            act(look(256) - 60, T.zg[:, v], T.gg[:, v].indirect(T.kk[:, 8:24]), ["gp%d" % k, "gp%d" % (k + 2), "kk", "kk2"], ["zg%d" % k])
        for i, k in enumerate(PLANES):
            tt(128, T.zt[:, 512 + k:1024:4], bank(2 + k, 0, 128), T.zg[:, 128 * i:128 * i + 128], A.add,
               ["B%d" % (2 + k), "zg%d" % (k % 2)], ["z1%d" % k])
        for h in range(2):
            window("z", h, T.zt, 512 * h, ["z%d%d" % (h, k) for k in range(4)])
            for k in PLANES:
                v = slice(512 * h + k, 512 * h + 512, 4)
                mmc(rb[h][k], "w", 128 * k, "z", 128 * h, 128 * h + 128, ["qw", "sw", "qz%d" % h])
                act(128, T.rl[:, v], bank(rb[h][k], 0, 128), ["B%d" % rb[h][k]], ["rl%d%d" % (h, k)], AF.Relu, 0.015625)
                tt(256, T.xn[:, v], T.rl[:, v], T.zt[:, v], A.add, ["rl%d%d" % (h, k), "z%d%d" % (h, k)], ["xn%d%d" % (h, k)])
        for h in range(2):
            window("x", h, T.xn, 512 * h, ["xn%d%d" % (h, k) for k in range(4)])
        if t < R - 1:
            signs(0, False)
            for k in PLANES:
                own(0, k, 2 + k)

    for h in range(2):
        lo, hi = 128 * h, 128 * h + 128
        mmc(h, "v", 0, "x", lo, hi, ["qv0", "qx%d" % h])
        (cp if h else act)(128, T.yo[:, lo:hi], bank(h, 0, 128), ["B%d" % h], ["yo%d" % h])
        dma("SA"[h], T.oc[:, 4 * lo:4 * hi], T.qx[:, lo:hi].bitcast(dt.uint8), ["qx%d" % h])
        dma("AS"[h], T.y[:, lo:hi], T.yo[:, lo:hi], ["yo%d" % h])
    for k in range(4):
        dma("SAAA"[k], T.osc[4 * k:4 * k + 4, :], T.sx[32 * k:32 * k + 4, :], ["qx0", "qx1"])

    if not ORDER:
        ORDER.extend(schedule(calls))
    for i in ORDER:
        order(calls[i][0], calls[i][2], calls[i][3])
        calls[i][1]()
    for s, n in sorted(count.items()):
        if not any(clock[q].get(s, 0) >= n for q in clock):
            g.wait_ge(T.sem[s], n)
